import numpy as np, ml_dtypes
CORES = [36,164,52,180,100,228,116,244]
N = 8
BF = ml_dtypes.bfloat16
V, B, W, K, L, T, S, RO = 1024, 128, 1280, 128, 4, 30, 832, 3
def ghosts(a):
    return np.concatenate([a, np.roll(a, 1, 0)[:, :, V - B:], np.roll(a, -1, 0)[:, :, :B]], axis=2)
def home(a):
    b = np.array(a[:, :, :V])
    b[:, :, V - B:] += np.roll(a, -1, 0)[:, :, V:V + B]
    b[:, :, :B] += np.roll(a, 1, 0)[:, :, V + B:]
    return b
def counts(mem):
    a = np.zeros((N, 8, W + 1), np.int64)
    np.add.at(a, (np.arange(N)[:, None, None, None], np.arange(8)[None, :, None, None], mem), 1)
    return home(a[:, :, :W])
def change(q, d, n):
    return np.clip(q + d - np.minimum(np.roll(n, -1, 1), 3), 1, 16)
def grow(vw, tl, t):
    gi = np.arange(8)[:, None]; cell = (np.arange(V) + S * t) % V
    small = vw[:, cell] < 8
    o = np.argsort(~small, axis=1, kind="stable")[:, :K]
    has = np.take_along_axis(small, o, 1); last = cell[o]
    mem = np.full((8, K, L), W); mem[:, :, 0] = np.where(has, last, W)
    size = has.astype(np.int64); tot = np.where(has, vw[gi, last], 0); go = has & (tot < T)
    for j in range(1, L):
        x = tl[gi, :, last]; nm = x >> 4
        sc = (x & 15) * vw[gi[:, :, None], nm]
        sc = np.where(np.any(nm[:, :, :, None] == mem[:, :, None, :j], axis=3), -1, sc)
        k = np.argmax(sc, axis=2)[:, :, None]
        new = np.take_along_axis(nm, k, 2)[:, :, 0]
        go = go & (np.take_along_axis(sc, k, 2)[:, :, 0] >= 0)
        mem[:, :, j] = np.where(go, new, W)
        size = size + go; tot = tot + np.where(go, vw[gi, new], 0)
        last = np.where(go, new, last); go = go & (tot < T)
    return mem, size, tot
def floats(rng):
    broad = rng.random((1, 8, 16, 1)) < 0.4; base = np.exp2(2 * rng.random((1, 8, 16, 1)) - 1)
    z = rng.standard_normal((N, 8, 16, V), dtype=np.float32)
    return np.clip(np.where(broad, np.exp2(4 * rng.random((N, 8, 16, V)) - 2), base * (1 + 0.06 * z)), 0.25, 4.0)
def weights(rng):
    n = np.arange(1, 2 * K + 1); x = rng.random((N, 128, 2 * K))
    return np.where(n < 8, 0.95 + 0.1 * x, 0.6 + 0.8 * x) * np.reciprocal(n.astype(np.float64))
def parts(rng):
    nm = rng.integers(0, W, (N, 8, 16, W)); p = rng.random(nm.shape)
    pool = rng.integers(0, W, (N, 8, 64))
    few = pool[np.arange(N)[:, None, None, None], np.arange(8)[None, :, None, None], rng.integers(0, 64, nm.shape)]
    nm = np.where(p < 0.1, few, np.where(p < 0.2, rng.integers(V, W, nm.shape), np.where(p < 0.23, np.arange(W), nm)))
    return nm, rng.integers(0, 16, nm.shape)
def volumes(rng, share):
    sm = rng.random((N, 8, V)) < share
    return np.where(sm, rng.integers(1, 8, sm.shape), rng.integers(8, 17, sm.shape)), rng.integers(-3, 5, (N, 8, RO, V)), sm
def keep(rng, sm):
    return np.where(sm[:, :, None, :], rng.integers(-1, 1, (N, 8, RO, V)), rng.integers(3, 6, (N, 8, RO, V)))
def hub(rng, nm, al, vol, dv, g, own, far):
    b = nm[:, g]
    al[:, g] = np.where((b == own) | (b == far), al[:, g], np.minimum(al[:, g], 14))
    k = np.argsort(rng.random((N, 16, W)), axis=1)
    for j, c in ((0, own), (1, far)):
        np.put_along_axis(nm[:, g], k[:, j:j + 1], c, axis=1); np.put_along_axis(al[:, g], k[:, j:j + 1], 15, axis=1)
    vol[:, g, own] = 16; dv[:, g, :, own] = 15
def pack(u, nm, al, vol, dv, wt):
    return {"u": np.ascontiguousarray(u.reshape(N, 128, V)).astype(np.float32), "nt": np.ascontiguousarray((16 * nm + al).reshape(N, 128, W)).astype(np.int32),
            "vol": np.ascontiguousarray(vol).astype(np.int32), "dv": np.ascontiguousarray(dv.reshape(N, 8, RO * V)).astype(np.int32), "wt": np.ascontiguousarray(wt).astype(np.float32)}
def setup_inputs(rng):
    nm, al = parts(rng); vol, dv, sm = volumes(rng, rng.choice(np.array([0.04, 0.15, 0.35, 0.6]), (N, 8, 1)))
    return pack(floats(rng), nm, al, vol, dv, weights(rng))
def setup_inputs_spread(rng):
    shape = (N, 8, 16, W)
    nm = np.minimum((W * rng.random(shape) ** 2).astype(np.int64), W - 1); nm[:, 1::2] = W - 1 - nm[:, 1::2]
    al = np.minimum((16 * rng.random(shape) ** 2).astype(np.int64), 15)
    vol = 1 + np.minimum((16 * rng.random((N, 8, V)) ** 2).astype(np.int64), 15); dv = rng.integers(-15, 16, (N, 8, RO, V))
    u = np.exp2(2 * rng.random((N, 8, 16, V)) - 1) * np.exp2(rng.integers(-1, 2, (N, 8, 1, V)))
    return pack(u, nm, al, vol, dv, weights(rng))
def setup_inputs_ends(rng):
    nm, al = parts(rng); p = rng.random(nm.shape); e = rng.integers(0, 2, nm.shape)
    nm = np.where(p < 0.74, e * (W - 1), nm); al = np.where(p < 0.9, 15 * e, al)
    zero = rng.random((N, 8, 1, W)) < 0.05; nm = np.where(zero, 0, nm); al = np.where(zero, 0, al)
    vol = np.where(rng.random((N, 8, V)) < 0.5, 1, 16); dv = np.where(rng.random((N, 8, RO, V)) < 0.5, -15, 15)
    hubs = (7, int(rng.integers(0, 6)))
    for g in hubs: hub(rng, nm, al, vol, dv, g, B - 1, W - 1)
    full = L - 3; chain = [60] + [V - 1, V - 3][:full] + [V - 2, W - 2]; size = [7] + [16] * full + [T - 8 - 16 * full]
    for g in range(8):
        vol[:, g, B - 2] = 16; dv[:, g, 0, B - 2] = 15
        for r in range(N):
            if g in hubs and r < N - 1: continue
            for a, b in zip(chain, chain[1:]):
                nm[r, g, :, a] = b; al[r, g, :, a] = 15
            for a, x in zip(chain, size):
                vol[r, g, a] = x; dv[r, g, 0, a] = 0
            if g not in hubs:
                nm[r, g, :, 61] = 61; vol[r, g, 61] = 1; dv[r, g, 0, 61] = -15
    wt = np.where(rng.random((N, 128, 2 * K)) < 0.5, 0.500001, 1.499999) * np.reciprocal(np.arange(1, 2 * K + 1).astype(np.float64))
    u = floats(rng); u = np.where(rng.random(u.shape) < 0.65, np.where(rng.random(u.shape) < 0.5, 0.25, 4.0), u)
    return pack(u, nm, al, vol, dv, wt)
def setup_inputs_corners(rng):
    nm, al = parts(rng); col = np.arange(W); k = np.arange(16)[:, None]; sh = int(rng.integers(0, 6))
    many = np.array([0, 1, K - 1, K, K + 1, V])[(3 * np.arange(N)[:, None] + np.arange(8)[None, :] + sh) % 6]
    draw = rng.random((N, 8, V)); way = (S * np.arange(RO) - 1) % V
    draw[:, :, way] = np.where((many == K)[:, :, None], -1.0, draw[:, :, way])
    sm = np.argsort(np.argsort(draw, axis=2), axis=2) < many[:, :, None]
    vol = np.where(sm, rng.integers(1, 8, sm.shape), rng.integers(8, 17, sm.shape)); e = rng.integers(0, 4, (N, 8, 1))
    vol = np.where(e == 1, np.where(sm, 1, 16), np.where(e == 2, np.where(sm, 7, 8), vol)); dv = keep(rng, sm)
    z = rng.integers(0, 16, (N, 8, 1, W)); one = rng.integers(0, W, (N, 8, 1, W))
    ends = np.array([0, V - 1, V, V + B - 1, V + B, W - 1])[rng.integers(0, 6, nm.shape)]
    nm = np.where(z == 0, col, np.where(z == 1, np.where(k == (col & 15), one, col), np.where(z == 2, one, np.where(z < 5, ends, nm))))
    a = rng.integers(0, 8, (N, 8, 1, W)); al = np.where(a == 0, 0, np.where(a == 1, 15, al))
    return pack(floats(rng), nm, al, vol, dv, weights(rng))
def setup_inputs_crowd(rng):
    nm, al = parts(rng); vol, dv, sm = volumes(rng, 0.5); dv = keep(rng, sm); sh = int(rng.integers(0, 4))
    hs = [int(x) for x in V - 100 + rng.permutation(80)[:8]]
    four = np.array([V - 10, V - 10 + B, 5, V + B + 5])
    for g in range(8):
        m = (g + sh) % 4
        if m < 2: hub(rng, nm, al, vol, dv, g, hs[g], hs[g] + B)
        if m == 1:
            for r in range(0, N, 2):
                nm[r, g, :, 40] = 40; vol[r, g, 40] = 5; dv[r, g, :, 40] = 0
        if m == 2: nm[:, g] = four[rng.integers(0, 4, (N, 16, W))]
    for g in range(8):
        if (g + sh) % 4 < 2:
            p = (g - 1) % 8; vol[:, p, hs[g]] = 12; dv[:, p, 0, hs[g]] = 0; dv[:, p, 1, hs[g]] = rng.integers(-2, 0, N); dv[:, p, 2:, hs[g]] = 3
    return pack(floats(rng), nm, al, vol, dv, weights(rng))
def setup_inputs_calm(rng):
    nm, al = parts(rng); vol, dv, sm = volumes(rng, 0.3); kind = (np.arange(8) + int(rng.integers(0, 4))) % 4
    late, turn = [int(g) for g in np.flatnonzero(kind == 0)]
    vol[:, late] = rng.integers(8, 17, (N, V))
    for g in range(8):
        if kind[g] >= 2:
            pool = rng.permutation(W)[:120 if kind[g] == 2 else 300]; nm[:, g] = pool[rng.integers(0, len(pool), (N, 16, W))]
    tl = 16 * nm + al; dv[:, :, 0] = 0; q = vol
    for t in range(1, RO):
        none = ((np.arange(8) == turn) & (t % 2 == 1))[None, :, None]
        vw = ghosts(q); n = counts(np.stack([grow(vw[r], tl[r], t - 1)[0] for r in range(N)]))
        h = np.minimum(np.roll(n, -1, 1), 3); goal = np.where(none, 8, rng.integers(7, 9, q.shape))
        dv[:, :, t] = np.where((rng.random(q.shape) < 0.6) | (none & (q < 8)), goal - q + h, np.where(none, 3, 0))
        q = change(q, dv[:, :, t], n)
    return pack(floats(rng), nm, al, vol, dv, weights(rng))
def check_ranges(d):
    bad = []
    for k, lo, hi in (("nt", 0, 16 * W - 1), ("vol", 1, 16), ("dv", -15, 15)):
        if np.min(d[k]) < lo or np.max(d[k]) > hi: bad.append("range of " + k)
    if not (np.min(d["u"]) >= 0.25 and np.max(d["u"]) <= 4): bad.append("range of u")
    p = np.asarray(d["wt"], np.float64) * np.arange(1, 2 * K + 1)
    if not (np.min(p) >= 0.5 and np.max(p) <= 1.5): bad.append("range of wt")
    return bad
def reference(u, nt, vol, dv, wt):
    x = u.astype(np.float64).reshape(N, 8, 16, V).transpose(0, 1, 3, 2)
    tl = nt.astype(np.int64).reshape(N, 8, 16, W); w = wt.astype(np.float64).reshape(N, 8, 16, 2 * K).transpose(0, 1, 3, 2)
    q = vol.astype(np.int64); d = dv.astype(np.int64).reshape(N, 8, RO, V)
    n = np.zeros((N, 8, V), np.int64); gi = np.arange(8)[:, None]; g3 = gi[:, :, None]
    for t in range(RO):
        q = change(q, d[:, :, t], n); vw = ghosts(q); xw = ghosts(x)
        total = np.zeros((N, 8, W + 1, 16)); named = []
        for r in range(N):
            mem, size, tot = grow(vw[r], tl[r], t); named.append(mem); there = mem < W
            m = np.minimum(np.where(there, mem, mem[:, :, :1]), W - 1)
            um = xw[r][g3, m]
            mean = np.add.reduce(np.where(there, vw[r][g3, m], 0)[..., None] * um, axis=2) * w[r][gi, np.maximum(tot, 1) - 1]
            slope = 0.5 * (np.take_along_axis(um, np.maximum(size - 1, 0)[:, :, None, None], 2)[:, :, 0] - um[:, :, 0])
            un = xw[r][g3[:, :, :, None], tl[r][g3, :, m] >> 4]
            lo = np.min(un, axis=(2, 3)); hi = np.max(un, axis=(2, 3))
            c = 0.125 * (2 * np.arange(L) - (size - 1)[:, :, None])
            est = np.clip(mean[:, :, None] + slope[:, :, None] * c[..., None], lo[:, :, None], hi[:, :, None])
            np.add.at(total[r], (g3, mem), est)
        n = counts(np.stack(named)); s = home(total[:, :, :W])
        wn = np.stack([w[r][gi, np.maximum(n[r], 1) - 1] for r in range(N)])
        x = np.where((n > 0)[..., None], s * wn, x)
    return {"y": np.ascontiguousarray(x.transpose(0, 1, 3, 2)).reshape(N, 128, V).astype(np.float32)}

def check_inputs(d):
    bad = list(check_ranges(d))
    if not bad:
        for name, y in reference(**d).items():
            for q in range(N):
                v = np.abs(np.asarray(y[q], np.float64)); s = np.sqrt(np.mean(v * v))
                if v.max() > 11 * s or s < 2.0 ** -1: bad.append('%s of rank %d is uneven or too small' % (name, q))
    return bad

@@ -1,0 +1,753 @@
+import numpy as np
+from concourse.bass import DstId, RemoteDMATransfer
+from concourse.mybir import AluOpType as A, AxisListType as AX, ActivationFunctionType as F
+
+S_ = np.s_
+f32, bf, i32, u16 = "float32", "bfloat16", "int32", "uint16"
+LV = 4
+GR = 4
+FW = 3208 + 1288 * (LV - 1)
+SB = {
+    "Lin": ([4, 64], i32), "Ls": ([3, 64], f32), "Ld": ([12, 2, 16], f32), "Lt": ([3, 4, 2, 16], f32),
+    "V1": ([3, 80], bf), "D2": ([80, 2], bf), "VW": ([3, 80], bf), "VD": ([80], bf), "VR": ([2, 1296], bf),
+    "NT": ([1280], i32), "NM": ([1288], f32), "AL": ([1288], i32),
+    "F0": ([FW], f32), "F1": ([FW], f32), "F2": ([FW], f32), "LF": ([3, 512], f32),
+    "WT": ([792], f32), "IOT": ([1296], f32), "XT": ([1288], bf), "RC": ([8], f32), "DU": ([32], f32), "CG": ([8], u16),
+    "GO": ([3, 8, 4], f32), "NG": ([3, 32], f32), "OM": ([32], f32), "FX": ([32], f32), "FI": ([32], f32), "TG": ([32], f32),
+    "UT": ([3, 32], u16), "LH": ([128], f32), "XR": ([128], bf),
+    "RG": ([128], f32), "RI": ([128], f32), "DM": ([128], f32), "BO": ([128], bf), "TB": ([128], bf), "SH": ([128], bf),
+    "IDB": ([128], bf), "IDF": ([128], f32), "NEG": ([128], bf), "AK": ([144], bf), "RB": ([16, 128], bf),
+    "CO": ([32], f32), "CB": ([2], bf), "CI": ([32], i32), "CR": ([8, 16], f32), "C8": ([6, 8], f32), "TH": ([24], f32),
+    "T1": ([128], f32), "T2": ([128], f32), "T3": ([8, 16], f32), "TI": ([96], i32), "XH": ([96], f32), "XL": ([16], f32),
+    "HA": ([96], f32), "HC": ([896], bf), "US": ([128], f32), "LT": ([128], f32), "NF": ([2, 256], f32), "C80": ([3, 80], f32),
+    "SM": ([64], bf), "SP": ([64], bf), "ZR": ([64], f32), "LC": ([8, 64], bf), "RK": ([72], f32), "CM": ([128], bf), "IM": ([8, 16], f32),
+    "W": ([3, 12, 8], f32), "I": ([3, 12, 8], i32), "U": ([3, 20, 8], u16), "UF": ([3, 32], u16), "UM": ([3, 32], u16),
+    "NU": ([128], u16), "GV": ([2048], bf), "A15": ([128], f32), "MR": ([3, 128], f32), "EQ": ([3, 128], bf), "NC": ([128], f32),
+    "PR": ([128], f32), "VM": ([2, 512], bf), "NO": ([2, 2, 256], u16),
+    "XA": ([128], bf), "XB": ([2, 128], bf), "HB": ([896], bf), "EB": ([6, 8, 2, 2, 2, 16], bf),
+    "CN": ([3, 80], bf), "LN": ([3, 32], bf), "NP": ([80], bf), "HM": ([80], bf),
+    "N1": ([3, 80], f32), "UW": ([2, 80], u16), "UO": ([2, 80], u16), "WN": ([1280], f32),
+    "G": ([2, 512 * GR], f32), "ON": ([2048], f32), "OX": ([2048], f32), "LO": ([128], f32), "HI": ([128], f32),
+    "UV": ([512], f32), "U0": ([128], f32), "DD": ([128], f32), "D8": ([128], f32), "S1": ([128], f32),
+    "MM": ([128], f32), "TE": ([128], f32), "ES": ([512], f32), "ZH": ([2, 72, 16], bf), "ZL": ([2, 72, 16], bf),
+    "CC": ([3, 128], f32), "GA": ([128], f32),
+}
+SCRATCH = {k: ("sbuf", [128] + v[0], v[1]) for k, v in SB.items()}
+for _b in range(8):
+    SCRATCH["P%d" % _b] = ("psum", [128, 32, 16] if _b in (1, 2, 3, 4) else [128, 512], f32)
+NDMA = 14
+SEMAPHORES = ["eD", "eA", "eP", "eG", "sent"] + ["d%d" % k for k in range(NDMA)] + ["x%d" % k for k in range(10)]
+CY = 0.83 * 1.2e-3
+GA_, SC_ = 1.55, 3.8
+BIG = float(2 ** 24)
+
+
+def _shape(name):
+    return SCRATCH[name][1]
+
+
+def _cells(ap):
+    name, idx = ap
+    if name not in SCRATCH:
+        return None
+    sh = _shape(name)
+    n = int(np.prod(sh[1:]))
+    m = np.zeros(n, bool)
+    ix = idx if isinstance(idx, tuple) else (idx,)
+    m[np.arange(n).reshape(sh[1:])[ix[1:]].ravel()] = True
+    return name, m
+
+
+def _n(ap):
+    if ap[0] == "ind":
+        return 16 * _n(ap[2])
+    return int(_cells(ap)[1].sum())
+
+
+def _isap(x):
+    return isinstance(x, tuple)
+
+
+def _two(*aps):
+    return all(SCRATCH[a[0]][2] in (bf, u16) for a in aps)
+
+
+def build():
+    ops = []
+
+    def add(var, rd, wr, lat=0.0):
+        r, w = [], []
+        for a in rd:
+            if _isap(a):
+                r += [a[1], a[2]] if a[0] == "ind" else [a]
+        for a in wr:
+            if a[0] == "ind":
+                w.append(a[1]); r.append(a[2])
+            else:
+                w.append(a)
+        ops.append(dict(var=var, r=[c for c in map(_cells, r) if c], w=[c for c in map(_cells, w) if c], lat=lat))
+        return ops[-1]
+
+    def dcost(out, ins, per):
+        if out[0] == "ind":
+            return 0.06 + _n(out) * SC_ * CY
+        if ins[0][0] == "ind":
+            return 0.06 + _n(ins[0]) * GA_ * CY
+        return 0.03 + max(64, _n(ins[0]) * per) * CY
+
+    def tt(o, a, b, op):
+        ps = a[0][0] == "P" and a[0] != "PR" or b[0][0] == "P" and b[0] != "PR"
+        add({"D": ([("tensor_tensor", o, a, b, op)], dcost(o, [a], 1 if ps else 2))}, [a, b], [o])
+
+    def ts(o, a, s1, op0, s2=None, op1=None):
+        c = ("tensor_scalar", o, a, s1, s2, op0) + (() if op1 is None else (op1,))
+        add({"D": ([c], dcost(o, [a], 0.5 if a[0] != "ind" and o[0] != "ind" and _two(o, a) else 1))}, [a, s1, s2], [o])
+
+    def cp(o, a):
+        add({"D": ([("tensor_copy", o, a)], dcost(o, [a], 0.5 if a[0] != "ind" and o[0] != "ind" and _two(o, a) else 1))}, [a], [o])
+
+    def acost(a):
+        return 0.08 + _n(a) * GA_ * CY if a[0] == "ind" else 0.06 + max(64, _n(a)) * CY
+
+    def aff(o, a, sc=1.0, bi=None, eng="AD"):
+        if bi is None:
+            d = ("tensor_copy", o, a) if sc == 1.0 else ("tensor_scalar", o, a, sc, None, A.mult)
+            s = ("act", o, a, F.Copy, None, sc)
+        else:
+            d = ("tensor_scalar", o, a, bi, None, A.add) if sc == 1.0 else ("tensor_scalar", o, a, sc, bi, A.mult, A.add)
+            s = ("act", o, a, F.Identity, bi, sc)
+        var = {"D": ([d], dcost(o, [a], 0.5 if a[0] != "ind" and _two(o, a) else 1)), "A": ([s], acost(a))}
+        add({e: var[e] for e in eng}, [a, sc, bi], [o])
+
+    def hot(o, a):
+        add({"D": ([("tensor_scalar", o, a, -0.5, None, A.is_ge)], dcost(o, [a], 1)), "A": ([("act", o, a, F.Relu, ("CO", S_[:, 31:32]), 1.0)], acost(a))},
+            [a, ("CO", S_[:, 31:32])], [o])
+
+    def red(o, a, op):
+        add({"D": ([("reduce", o, a, op)], dcost(o, [a], 1))}, [a], [o])
+
+    def scan(o, a, b, init, op0, op1):
+        add({"D": ([("tensor_tensor_scan", o, a, b, init, op0, op1)], dcost(o, [a], 1))}, [a, b], [o])
+
+    def vtr(o, a):
+        add({"D": ([("transpose", o, a)], dcost(o, [a], 1))}, [a], [o])
+
+    def ms(o, c, soon=False):
+        if not soon and float(c).is_integer():
+            return iota(o, [[0, _n(o)]], int(c))
+        add({"D": ([("memset", o, c)], dcost(o, [o], 0.5 if _two(o) else 1))}, [], [o])
+
+    def mm(lst, group=True):
+        calls, c, rd, wr = [], 0.0, [], []
+        for k, (o, l, r) in enumerate(lst):
+            gs = len(lst) if group is True else max(1, int(group))
+            calls.append(("matmul", o, l, r, k % gs == 0, k % gs == gs - 1))
+            c += max(64, _n(r)) * 0.7 * CY * (4 if SCRATCH[r[0]][2] == f32 else 1)
+            rd += [l, r]; wr.append(o)
+        add({"P": (calls, c + 0.05)}, rd, wr)
+
+    def iota(o, pat, base=0, cm=0):
+        add({"G": ([("iota", o, pat, base, cm)], 0.15 + 2 * _n(o) * CY)}, [], [o])
+
+    nd = [0]
+
+    def dma(q, o, a, nbytes):
+        op = add({q: ([("dma", o, a, "d%d" % nd[0])], 0.1)}, [a], [o], lat=nbytes)
+        op["dma"] = "d%d" % nd[0]
+        nd[0] += 1
+
+    nx = [0]
+
+    def xchg(parts, nbytes):
+        op = add({"G": ([("remote", parts, "x%d" % nx[0])], 0.3)}, [p[1] for p in parts], [p[2] for p in parts], lat=2.2 + nbytes / 60e3)
+        op["x"] = "x%d" % nx[0]
+        nx[0] += 1
+
+    def col(k):
+        return ("CO", S_[:, k:k + 1])
+
+    def b(name, idx=S_[:]):
+        return (name, idx)
+
+    def ind(w, o):
+        return ("ind", w, o)
+
+    UO_, BS_ = 1416, 2696
+    dma("S", b("Lin", S_[:, 0, :]), b("vol"), 32e3)
+    dma("A", b("Lin", S_[:, 1, :]), b("dv", S_[:, 0:1024]), 32e3)
+    dma("S", b("F0", S_[:, UO_:UO_ + 128]), b("u", S_[:, 0:128]), 64e3)
+    dma("A", b("F0", S_[:, UO_ + 896:UO_ + 1024]), b("u", S_[:, 896:1024]), 64e3)
+    dma("S", b("NT"), b("nt"), 655e3)
+    dma("S", b("Lin", S_[:, 2, :]), b("dv", S_[:, 1024:2048]), 32e3)
+    dma("S", b("Lin", S_[:, 3, :]), b("dv", S_[:, 2048:3072]), 32e3)
+    dma("S", b("WT", S_[:, 8:264]), b("wt"), 131e3)
+    dma("S", b("F0", S_[:, UO_ + 128:UO_ + 896]), b("u", S_[:, 128:896]), 393e3)
+    xchg([(1, b("F0", S_[:, UO_ + 896:UO_ + 1024]), b("F0", S_[:, UO_ + 1024:UO_ + 1152])),
+          (-1, b("F0", S_[:, UO_:UO_ + 128]), b("F0", S_[:, UO_ + 1152:UO_ + 1280]))], 131e3)
+    iota(b("CI", S_[:, 0:1]), [[0, 1]], 0, 1)
+    iota(b("IOT", S_[:, 0:144]), [[1, 144]])
+    iota(b("RG"), [[1, 8], [0, 16]])
+    iota(b("RI", S_[:, 0:128]), [[0, 8], [1, 16]])
+    iota(b("C8", S_[:, 0, :]), [[16, 8]])
+    iota(b("C80", S_[:, 0, :]), [[16, 80]])
+    iota(b("IOT", S_[:, 144:720]), [[1, 576]], 144)
+    iota(b("IOT", S_[:, 720:1296]), [[1, 576]], 720)
+    ci = lambda k: b("CI", S_[:, k:k + 1])
+    ts(ci(1), ci(0), 4, A.arith_shift_right, 1, A.bitwise_and)
+    cp(col(3), ci(1))
+    ts(col(4), ci(1), -1.0, A.mult, 1.0, A.add)
+    ts(ci(2), ci(0), 15, A.bitwise_and)
+    ts(ci(3), ci(0), 4, A.arith_shift_right)
+    cp(col(0), ci(0)); cp(col(1), ci(2)); cp(col(2), ci(3))
+    ms(col(31), 1.0)
+    ms(col(30), 1288.0)
+    ms(b("ZR"), 0.0, True)
+    ms(b("RK", S_[:, 64:72]), 0.0)
+
+    def unblock(a0, a1, outs):
+        for h in (0, 1):
+            ts(b("Ld", S_[:, 4 * a0:4 * a1, h, :]), b("Ls", S_[:, a0:a1, :]), col(4 - h), A.mult)
+        vtr(b("Lt", S_[:, a0:a1]), b("Ld", S_[:, 4 * a0:4 * a1]))
+        for a in range(a0, a1):
+            for c4 in range(4):
+                tt(outs(a, c4), b("Lt", S_[:, a, c4, 0, :]), b("Lt", S_[:, a, c4, 1, :]), A.add)
+    tt(b("Ls", S_[:, 0, :]), b("Lin", S_[:, 0, :]), b("Lin", S_[:, 1, :]), A.add)
+    unblock(0, 1, lambda a, c4: b("V1", S_[:, 0, c4:64:4]))
+    xchg([(1, b("V1", S_[:, 0, 56:64]), b("V1", S_[:, 0, 64:72])), (-1, b("V1", S_[:, 0, 0:8]), b("V1", S_[:, 0, 72:80]))], 16e3)
+    ts(b("BO"), b("RG"), col(2), A.is_equal)
+    ts(b("DM", S_[:, 0:128]), b("RI", S_[:, 0:128]), col(1), A.is_equal)
+    ts(b("T1"), b("RI", S_[:, 0:128]), col(1), A.is_lt, -1.0, A.mult)
+    tt(b("TB"), b("T1"), b("BO"), A.mult)
+    c8 = lambda k: b("C8", S_[:, k, :])
+    ts(c8(0), c8(0), col(1), A.add)
+    ts(c8(1), c8(0), 0.5, A.add)
+    for j in range(4):
+        aff(b("DU", S_[:, 8 * j:8 * j + 8]), c8(0), 1.0, col(30))
+    cp(b("RC"), b("BO", S_[:, 0::16]))
+    cp(b("CG"), b("IOT", S_[:, 0:8]))
+    ms(b("GO", S_[:, :, :, 0]), 1.0)
+    for i in range(16):
+        aff(b("RB", S_[:, i, :]), b("BO"), b("DM", S_[:, i:i + 1]))
+    ts(col(5), col(0), 15.0, A.add)
+    ts(b("AK"), b("IOT", S_[:, 0:144]), col(5), A.is_equal, b("DM", S_[:, 0:1]), A.mult)
+    ts(b("IDB"), b("IOT", S_[:, 0:128]), col(0), A.is_equal)
+    ts(b("IDF"), b("IOT", S_[:, 0:128]), col(0), A.is_equal)
+    aff(b("NEG"), b("IDB"), -BIG)
+    ts(col(7), col(1), -2048.0, A.mult, 31 * 2048.0, A.add)
+    ms(b("VR", S_[:, :, 0:8]), 0.0)
+    ms(b("NM", S_[:, 0:8]), 8.0)
+    ms(b("AL", S_[:, 0:8]), 0)
+    for h in (0, 1):
+        al, nt = b("AL", S_[:, 8 + 640 * h:648 + 640 * h]), b("NT", S_[:, 640 * h:640 * h + 640])
+        ts(al, nt, 4, A.arith_shift_right)
+        ts(b("NM", al[1]), al, 8.0, A.add)
+        ts(al, nt, 15, A.bitwise_and)
+    ts(ci(4), ci(0), 112, A.add)
+    ts(ci(5), ci(4), 127, A.bitwise_and)
+    cp(col(6), ci(5))
+    ts(b("SH"), b("IOT", S_[:, 0:128]), col(6), A.is_equal)
+    cp(b("Ls", S_[:, 1:3, :]), b("Lin", S_[:, 2:4, :]))
+    unblock(1, 3, lambda a, c4: b("D2", S_[:, c4:64:4, a - 1]))
+    xchg([(1, b("D2", S_[:, 56:64, :]), b("D2", S_[:, 64:72, :])), (-1, b("D2", S_[:, 0:8, :]), b("D2", S_[:, 72:80, :]))], 16e3)
+    xchg([(1, b("WT", S_[:, 8:264]), b("WT", S_[:, 272:528])), (-1, b("WT", S_[:, 8:264]), b("WT", S_[:, 536:792]))], 262e3)
+    for k in (0, 264, 528):
+        ms(b("WT", S_[:, k:k + 8]), 1.0)
+    ms(b("CR"), 0.0)
+    for k, sl, v in ((0, S_[0:1], 1.0), (1, S_[2:6:3], 1.0), (2, S_[3:7:3], 1.0), (3, S_[1:2], 1.0), (4, S_[4:8:3], 1.0),
+                     (5, S_[5:8], 1.0), (6, S_[0:2], 2.0), (6, S_[5:8], -1.0), (7, S_[2:4], -1.0)):
+        ms(b("CR", (S_[:], k, sl)), v)
+    tt(b("T3"), b("CR"), b("DM", S_[:, 0:128]), A.mult)
+    red(b("CO", S_[:, 8:16]), b("T3"), A.add)
+    ts(col(16), col(13), -1.0, A.mult, 1.0, A.add)
+    ts(col(17), b("DM", S_[:, 4:5]), -1.0, A.mult)
+    tt(col(18), col(17), col(15), A.add)
+    for h in (0, 1):
+        tt(col(19 + h), col(14), col(4 - h), A.mult)
+        tt(col(21 + h), col(18), col(4 - h), A.mult)
+    x81 = b("IOT", S_[:, 0:96])
+    tt(b("TI"), x81, x81, A.mult)
+    cp(b("T1", S_[:, 0:96]), b("TI"))
+    ts(b("TI"), b("TI"), 31, A.bitwise_and)
+    tt(b("T1", S_[:, 0:96]), b("T1", S_[:, 0:96]), b("TI"), A.subtract)
+    ts(b("T1", S_[:, 0:96]), b("T1", S_[:, 0:96]), col(9), A.mult)
+    ts(b("T2", S_[:, 0:96]), b("TI"), col(10), A.mult)
+    ts(b("XH"), x81, col(8), A.mult)
+    tt(b("XH"), b("XH"), b("T1", S_[:, 0:96]), A.add)
+    tt(b("XH"), b("XH"), b("T2", S_[:, 0:96]), A.add)
+    ts(b("XL"), b("IOT", S_[:, 0:16]), col(12), A.mult, col(11), A.add)
+    tt(b("XL"), b("XL"), b("IOT", S_[:, 0:16]), A.mult)
+    for lo in range(16):
+        aff(b("XT", S_[:, 8 + lo::16]), b("XH", S_[:, 0:80]), 1.0, b("XL", S_[:, lo:lo + 1]))
+    aff(b("XT", S_[:, 0:8]), b("ZR", S_[:, 0:8]), 1.0, b("XH", S_[:, 80:81]))
+    PERM = ((0, 56, 8), (8, 72, 8), (16, 64, 8), (24, 0, 56))
+    for p0, h0, w in PERM:
+        aff(b("HA", S_[:, p0:p0 + w]), b("XH", S_[:, h0:h0 + w]), col(14), col(15))
+    aff(b("HA", S_[:, 80:96]), b("XL"), col(14), col(17))
+    ms(b("HC", S_[:, 640:896]), -1.0)
+    for g in range(8):
+        gm = b("RC", S_[:, g:g + 1])
+        aff(b("HC", S_[:, 80 * g:80 * g + 80]), b("HA", S_[:, 0:80]), gm)
+        o = 640 + 32 * g + 16 * (g % 2)
+        aff(b("HC", S_[:, o:o + 16]), b("HA", S_[:, 80:96]), gm)
+    ms(b("T1"), 0.5)
+    ms(b("GA"), 0.0)
+    scan(b("T2"), b("T1"), b("GA"), float(2 ** 65), A.mult, A.add)
+    tt(b("T1"), b("T2"), b("IDF"), A.mult)
+    red(col(23), b("T1"), A.max)
+    cp(b("CB", S_[:, 0:1]), col(23))
+    tt(b("T3"), b("T2"), b("DM", S_[:, 0:128]), A.mult)
+    red(c8(2), b("T3"), A.max)
+    for j in range(3):
+        aff(b("TH", S_[:, 8 * j:8 * j + 8]), c8(2), 2.5)
+    for v in range(LV):
+        ms(b("US", S_[:, v::LV]), 2.0 ** (8 * v), v == 3)
+        ms(b("LT", S_[:, v::LV]), float(1800 + 1288 * (v - 1) if v else 0))
+    ts(b("C80", S_[:, 0, :]), b("C80", S_[:, 0, :]), col(1), A.add)
+    for sl, o in ((S_[8:56], 8), (S_[0:8], BS_), (S_[56:80], BS_ - 768)):
+        ms(b("C80", (S_[:], 1, sl)), float(UO_ - o))
+        ts(b("C80", (S_[:], 0, sl)), b("C80", (S_[:], 0, sl)), float(o), A.add)
+    ms(b("C80", S_[:, 2, 0:64]), 7.0)
+    ms(b("C80", S_[:, 2, 64:72]), 271.0)
+    ms(b("C80", S_[:, 2, 72:80]), 535.0)
+    ms(b("CN", S_[:, :, 8:24]), 0.0)
+    for t in range(3):
+        for h in range(4):
+            iota(b("F%d" % t, S_[:, 354 * h:354 * h + 354]), [[0, 354]])
+        iota(b("F%d" % t, S_[:, BS_:BS_ + 512]), [[0, 512]])
+    for Z in ("ZH", "ZL"):
+        for z in range(6):
+            iota(b(Z, S_[:, z // 3, 24 * (z % 3):24 * (z % 3) + 24, :]), [[0, 384]])
+
+    def ints(t):
+        w = lambda k: b("W", S_[:, t, k, :])
+        iw = lambda k: b("I", S_[:, t, k, :])
+        uw = lambda k: b("U", S_[:, t, k, :])
+        par = t % 2
+        vr = b("VR", S_[:, par, :])
+        s16 = (832 * t) % 1024 // 16
+        v1 = lambda sl: b("V1", (S_[:], t, sl))
+        for o, c0, n in ((0, s16, 64 - s16), (64 - s16, 0, s16)):
+            if n:
+                ts(b("SM", S_[:, o:o + n]), v1(S_[c0:c0 + n]), 8.0, A.is_lt)
+        ts(b("VW", S_[:, t, :]), v1(S_[:]), 1.0, A.max, 16.0, A.min)
+        scan(b("SP"), b("SM"), b("ZR"), 0.0, A.add, A.add)
+        mm([(b("P0", S_[:, 0:64]), b("BO"), b("SP"))])
+        mm([(b("P1", S_[:, 0:4, :]), b("BO"), b("SP")), (b("P1", S_[:, 0:4, :]), b("TB"), b("SM"))])
+        for bank in range(3):
+            nc = 32 if bank < 2 else 16
+            pb = "P%d" % (2 + bank)
+            mm([(b(pb, S_[:, 0:nc, i]), b("RB", S_[:, i, :]), b("VW", S_[:, t, 32 * bank:32 * bank + nc])) for i in range(16)], False)
+            aff(b("VR", S_[:, par, 8 + 512 * bank:8 + 512 * bank + 16 * nc]), b(pb, S_[:, 0:nc, :]))
+        rk = b("RK", S_[:, 0:64])
+        for c in range(8):
+            o, a, bi, ac = b("LC", S_[:, c, :]), b("P0", S_[:, 0:64]), b("C8", S_[:, 1, c:c + 1]), b("W", S_[:, t, 0, c:c + 1])
+            add({"A": ([("sign", o, a, bi, ac)], 0.15)}, [a, bi], [o, ac])
+        cp(rk, b("P1", S_[:, 0:4, :]))
+        ts(uw(0), w(0), 0.5, A.mult, 32.0, A.add)
+        tt(b("CM"), ind(b("RK"), uw(0)), b("IOT", S_[:, 0:128]), A.is_le)
+        ts(w(1), w(0), 8.0, A.mult, float(512 + 16 * s16), A.add)
+        has = b("FI", S_[:, 0:8])
+        ts(has, w(0), 64.0, A.is_lt)
+        mm([(b("P0", S_[:, 128:256]), b("BO"), b("CM"))])
+        tt(b("IM"), b("P0", S_[:, 128:256]), b("DM", S_[:, 0:128]), A.mult)
+        red(w(3), b("IM"), A.add)
+        tt(iw(0), w(3), w(1), A.add)
+        ts(iw(1), iw(0), 1023, A.bitwise_and)
+        ts(uw(1), iw(1), 8.0, A.add)
+        ts(rk, rk, 128.0, A.is_le)
+        for h0, h1, p0 in ((0, 56, 24), (56, 64, 0)):
+            for a0, a1 in ((h0, min(h1, max(s16, h0))), (max(h0, min(s16, h1)), h1)):
+                if a1 > a0:
+                    r0 = (a0 - s16) % 64
+                    tt(b("CN", S_[:, t, p0 + a0 - h0:p0 + a1 - h0]), b("RK", S_[:, r0:r0 + a1 - a0]), b("SM", S_[:, r0:r0 + a1 - a0]), A.mult)
+        if t < 2:
+            tt(b("VD"), b("VW", S_[:, t, :]), b("D2", S_[:, :, t]), A.add)
+        um = lambda j0, j1: b("UM", S_[:, t, 8 * j0:8 * j1])
+        uf = lambda j0, j1: b("UF", S_[:, t, 8 * j0:8 * j1])
+        ng = lambda j: b("NG", S_[:, t, j::4])
+        ts(ng(0), iw(1), 8.0, A.add)
+        tt(w(4), ng(0), has, A.mult)
+        cp(um(0, 1), w(4))
+        go = has
+        for j in (1, 2, 3):
+            last = uw(j)
+            cp(b("NU"), ind(b("NM"), last))
+            for q in range(4):
+                aff(b("GV", S_[:, 512 * q:512 * q + 512]), ind(vr, b("NU", S_[:, 32 * q:32 * q + 32])))
+            aff(b("MR", S_[:, j - 1, :]), ind(b("IOT"), last))
+            aff(b("NC"), ind(b("NM"), last), 1.0, col(7))
+            for k in range(j):
+                tt(b("EQ", S_[:, k, :]), ind(b("NM"), last), b("MR", S_[:, k, :]), A.is_equal)
+            ts(b("A15"), ind(b("AL"), last), 32768.0, A.mult)
+            for h in (0, 1):
+                mm([(b("P0", S_[:, 64 * h:64 * h + 64]), b("AK", S_[:, 15 - k:143 - k]), b("GV", S_[:, 1024 * h + k:1024 * h + 1024:16])) for k in range(16)])
+            tt(b("PR"), b("P0", S_[:, 0:128]), b("A15"), A.mult)
+            keys = b("P1", S_[:, 8:16, :])
+            mm([(keys, b("EQ", S_[:, k, :]), b("NEG")) for k in range(j)] + [(keys, b("NC"), b("IDF")), (keys, b("PR"), b("IDF"))])
+            red(w(5), keys, A.max)
+            ts(iw(2), w(5), 0.0, A.max)
+            ts(iw(4), iw(2), 2047, A.bitwise_and)
+            tt(b("LH"), ind(iw(4), b("CG")), b("DM", S_[:, 0:128]), A.mult)
+            nw = b("P1", S_[:, 16, 0:8])
+            mm([(nw, b("LH"), b("RC"))])
+            if j < 3:
+                cp(uw(j + 1), nw)
+            tt(ng(j), nw, go, A.mult)
+            cp(um(j, j + 1), ng(j))
+            go = b("GO", S_[:, t, :, j])
+            ts(go, ng(j), 1.0, A.is_ge)
+
+            def volumes(j0, j1):
+                aff(b("VM", S_[:, par, 128 * j0:128 * j1]), ind(vr, um(j0, j1)))
+                mm([(b("P5", S_[:, 344 + 8 * j0:344 + 8 * j1]), b("AK", S_[:, 15 - k:143 - k]), b("VM", S_[:, par, 128 * j0 + k:128 * j1:16])) for k in range(16)])
+            if j == 2:
+                volumes(0, 3)
+                cp(w(8), b("P5", S_[:, 344:352]))
+                tt(w(8), b("P5", S_[:, 352:360]), w(8), A.add)
+                tt(w(8), b("P5", S_[:, 360:368]), w(8), A.add)
+                ts(w(6), w(8), 30.0, A.is_lt)
+                tt(w(6), w(6), go, A.mult)
+                go = w(6)
+            aff(b("XR"), ind(b("XT"), um(j, j + 1)))
+            aff(b("XA"), b("XR"), col(16), col(13))
+            mm([(b("P3"), b("XA"), b("HC", S_[:, 0:512])), (b("P4", S_[:, 0:24, :]), b("XA"), b("HC", S_[:, 512:896]))], False)
+            hot(b("HB", S_[:, 512:896]), b("P4", S_[:, 0:24, :]))
+            hot(b("HB", S_[:, 0:512]), b("P3"))
+            mm([(b("P5", S_[32 * (g // 2):32 * (g // 2) + 32, 80 * j:80 * j + 80]), b("HB", S_[:, 640 + 32 * g:672 + 32 * g]), b("HB", S_[:, 80 * g:80 * g + 80]))
+                for g in range(8)], 2)
+            ops[-1]["tile"] = 9
+            cn = b("CN", S_[:, t, :])
+            tt(cn, b("P5", S_[:, 80 * j:80 * j + 80]), cn, A.add)
+            if j == 3:
+                xchg([(1, b("CN", S_[:, t, 0:16]), b("LN", S_[:, t, 16:32])), (-1, b("CN", S_[:, t, 16:32]), b("LN", S_[:, t, 0:16]))], 30e3)
+            for h in (0, 1):
+                aff(b("XB", S_[:, h, :]), b("XR"), col(19 + h), col(21 + h))
+            e = 3 * par + j - 1
+            for x in (0, 1):
+                for y in (0, 1):
+                    rows = S_[64 * x + 32 * y:64 * x + 32 * y + 32]
+                    mm([(b("P%d" % (2 + y), S_[:, 2 * x + z::4, :]), b("XA", (rows, S_[:])), b("XB", (rows, z, S_[:]))) for z in (0, 1)], False)
+                    ops[-1]["tile"] = 1 + 2 * x + y
+            for y in (0, 1):
+                hot(b("EB", S_[:, e, :, :, y, :, :]), b("P%d" % (2 + y)))
+            mm([(b("P5", S_[:, 312 + 8 * j + c:313 + 8 * j + c]), b("EB", S_[:, e, c]), b("CB", S_[:, 0:1])) for c in range(8)], False)
+        tt(b("FI", S_[:, 8:32]), b("P5", S_[:, 320:344]), b("TH"), A.is_lt)
+        cp(b("TG"), um(0, 4))
+        tt(b("TG"), b("TG"), b("DU"), A.subtract)
+        tt(b("TG"), b("TG"), b("FI"), A.mult)
+        tt(b("TG"), b("TG"), b("DU"), A.add)
+        cp(b("UT", S_[:, t, :]), b("TG"))
+        ts(b("OM"), b("GO", S_[:, t]), -1.0, A.mult, 1.0, A.add)
+        scan(b("FX"), b("OM"), b("NG", S_[:, t, :]), 0.0, A.mult, A.add)
+        for j in range(4):
+            cp(uf(j, j + 1), b("FX", S_[:, j::4]))
+            tt(b("NF", S_[:, j // 2, j % 2::2]), ind(b("NM"), uf(j, j + 1)), b("LT"), A.add)
+        for s in (0, 1):
+            cp(b("NO", S_[:, par, s, :]), b("NF", S_[:, s, :]))
+        volumes(3, 4)
+        tt(w(9), b("P5", S_[:, 368:376]), w(8), A.add)
+        ts(uw(12), w(9), 7.0, A.add)
+        red(w(7), b("GO", S_[:, t, :, 1:4]), A.add)
+        cp(uw(13), w(7))
+        tt(b("NP", S_[:, 0:32]), b("CN", S_[:, t, 0:32]), b("LN", S_[:, t, :]), A.add)
+        if t < 2:
+            ts(b("HM", S_[:, 32:80]), b("CN", S_[:, t, 32:80]), 3.0, A.min)
+            ts(b("HM", S_[:, 0:32]), b("NP", S_[:, 0:32]), 3.0, A.min)
+            mm([(b("P0", S_[:, 256 + h0:256 + h0 + n]), b("SH"), b("HM", S_[:, p0:p0 + n])) for p0, h0, n in PERM], False)
+            tt(b("V1", S_[:, t + 1, :]), b("VD"), b("P0", S_[:, 256:336]), A.subtract)
+        cp(b("NP", S_[:, 32:80]), b("CN", S_[:, t, 32:80]))
+        mm([(b("P5", S_[:, 416 + h0:416 + h0 + n]), b("IDB"), b("NP", S_[:, p0:p0 + n])) for p0, h0, n in PERM], False)
+        n1 = lambda k: b("N1", S_[:, k, :])
+        tt(n1(0), b("P5", S_[:, 416:496]), b("C80", S_[:, 2, :]), A.add)
+        ts(n1(1), b("P5", S_[:, 416:496]), 0.0, A.is_equal)
+        cp(b("UW", S_[:, par, :]), n1(0))
+        tt(n1(1), n1(1), b("C80", S_[:, 1, :]), A.mult)
+        tt(n1(1), n1(1), b("C80", S_[:, 0, :]), A.add)
+        cp(b("UO", S_[:, par, :]), n1(1))
+
+    def floats(t):
+        par = t % 2
+        for c0, c1 in ((8, 32), (32, 56), (0, 8), (56, 80 if t < 2 else 64)):
+            aff(b("WN", S_[:, 16 * c0:16 * c1]), ind(b("WT"), b("UW", S_[:, par, c0:c1])))
+        Ft = "F%d" % t
+        uw = lambda k: b("U", S_[:, t, k, :])
+        u = b(Ft, S_[:, UO_ - 8:UO_ + 1280])
+        ut = lambda j: b("UT", S_[:, t, 8 * j:8 * j + 8])
+        S = b(Ft, S_[:, 0:UO_])
+        for c0, c1 in ((136, 904), (0, 136), (904, 1288)) if t else ((0, 1288),):
+            for v in range(1, LV):
+                o = 3208 + 1288 * (v - 1)
+                aff(b(Ft, S_[:, o + c0:o + c1]), b(Ft, S_[:, UO_ - 8 + c0:UO_ - 8 + c1]), 2.0 ** (-8 * v))
+        n = 32 * LV
+        for q in range(8):
+            for s in (0, 1):
+                aff(b("G", S_[:, s, 512 * (q % GR):512 * (q % GR) + 512]), ind(b(Ft, S_[:, UO_ - 8:]), b("NO", S_[:, par, s, 32 * q:32 * q + 32])))
+            for o in range(512 * q, 512 * q + 512, n):
+                back = lambda x: S_[x + n - 1:x - 1:-1] if x else S_[n - 1::-1]
+                r, o = o % 2048, o % (512 * GR)
+                scan(b("ON", S_[:, r:r + n]), b("G", S_[:, 0, o:o + n]), b("G", S_[:, 1, o:o + n]), 1e29, A.min, A.min)
+                scan(b("OX", (S_[:], back(r))), b("G", (S_[:], 0, back(o))), b("G", (S_[:], 1, back(o))), 0.0, A.max, A.max)
+            if q % 4 == 3:
+                half = S_[:, 16 * q - 48:16 * q + 16]
+                tt(b("LO", half), b("ON", S_[:, 31::32]), b("US", half), A.mult)
+                tt(b("HI", half), b("OX", S_[:, 0::32]), b("US", half), A.mult)
+        tt(b("UV"), ind(u, b("UF", S_[:, t, :])), b("VM", S_[:, par, :]), A.mult)
+        aff(b("U0"), ind(u, b("UF", S_[:, t, 0:8])))
+        tt(b("DD"), ind(u, b("UF", S_[:, t, 24:32])), b("U0"), A.subtract)
+        mm([(b("P7", S_[:, 256:384]), b("IDF"), b("UV", S_[:, 128 * j:128 * j + 128])) for j in range(4)])
+        aff(b("S1"), b("P7", S_[:, 256:384]))
+        tt(b("MM"), ind(b("WT", S_[:, 0:264]), uw(12)), b("S1"), A.mult)
+        aff(b("D8"), b("DD"), 0.125)
+        aff(b("U0"), b("DD"), 0.0625)
+        tt(b("TE"), ind(b("IOT"), uw(13)), b("U0"), A.mult)
+        p6 = lambda j: b("P6", S_[:, 128 * j:128 * j + 128])
+        tt(p6(0), b("MM"), b("TE"), A.subtract)
+        for j in (1, 2, 3):
+            tt(p6(j), p6(j - 1), b("D8"), A.add)
+        for j in (1, 2, 3, 0):
+            tt(p6(j), p6(j), b("LO"), A.max)
+            tt(b("ES", S_[:, 128 * j:128 * j + 128]), p6(j), b("HI"), A.min)
+        cp(ind(S, ut(0)), b("ES", S_[:, 0:128]))
+        for j in (1, 2, 3):
+            pb = "P7" if j % 2 else "P6"
+            z = j % 2
+            add({"P": ([("ptr", b(pb, S_[:, 0:128]), b("ES", S_[:, 128 * j:128 * j + 128]), b("IDF"))], 0.05 + 512 * 0.7 * CY)},
+                [b("ES", S_[:, 128 * j:128 * j + 128]), b("IDF")], [b(pb, S_[:, 0:128])])
+            aff(b("ZH", S_[:, z, 0::9, :]), b(pb, S_[:, 0:128]))
+            tt(b("ZL", S_[:, z, 0::9, :]), b(pb, S_[:, 0:128]), b("ZH", S_[:, z, 0::9, :]), A.subtract)
+            e = 3 * par + j - 1
+            mm([(b(pb, S_[:, 128:256]), b(Z, S_[:, z, 8 * g:8 * g + 8, :]), b("EB", S_[:, e, :, g // 4, g // 2 % 2, g % 2, :])) for Z in ("ZH", "ZL") for g in range(8)])
+            aff(b("CC", S_[:, j - 1, :]), b(pb, S_[:, 128:256]))
+            tt(b("GA"), ind(S, b("UM", S_[:, t, 8 * j:8 * j + 8])), b("CC", S_[:, j - 1, :]), A.add)
+            cp(ind(S, ut(j)), b("GA"))
+        lf = lambda k: b("LF", S_[:, t, 128 * k:128 * k + 128])
+        parts = [(1, b(Ft, S_[:, 1160:1288]), lf(0)), (-1, b(Ft, S_[:, 1032:1160]), lf(1))]
+        if t < 2:
+            parts += [(1, b(Ft, S_[:, 904:1032]), lf(2)), (-1, b(Ft, S_[:, 8:136]), lf(3))]
+        xchg(parts, 131e3 * (2 if t < 2 else 1))
+        top = 80 if t < 2 else 64
+
+        def new(c0, c1, end):
+            o = b("F%d" % (t + 1), S_[:, UO_ + 16 * c0:UO_ + 16 * c1]) if t < 2 else b("F0", S_[:, UO_ + 16 * c0:UO_ + 16 * c1])
+            tt(o, ind(b(Ft, S_[:, 0:end]), b("UO", S_[:, par, c0:c1])), b("WN", S_[:, 16 * c0:16 * c1]), A.mult)
+            if t == 2:
+                dma("S" if c0 else "A", b("y", S_[:, 16 * c0:16 * c1]), o, 8192 * (c1 - c0))
+        new(8, 32, BS_)
+        new(32, 56, BS_)
+        tt(b(Ft, S_[:, BS_:BS_ + 128]), b(Ft, S_[:, 8:136]), lf(0), A.add)
+        tt(b(Ft, S_[:, BS_ + 128:BS_ + 16 * top - 768]), b(Ft, S_[:, 904:8 + 16 * top]), b("LF", S_[:, t, 128:16 * top - 768]), A.add)
+        new(56, top, BS_ + 16 * top - 768)
+        new(0, 8, BS_ + 128)
+
+    ints(0); ints(1); floats(0); ints(2); floats(1); floats(2)
+    return ops
+
+
+def schedule(ops):
+    n = len(ops)
+    hist = {}
+    for k, o in enumerate(ops if "dep" not in ops[0] else []):
+        dep = set()
+        for name, m in o["r"]:
+            for j, wm, wr in hist.get(name, []):
+                if wr and (wm & m).any():
+                    dep.add(j)
+        for name, m in o["w"]:
+            for j, wm, wr in hist.get(name, []):
+                if (wm & m).any():
+                    dep.add(j)
+        o["dep"] = dep
+        for name, m in o["w"]:
+            hist[name] = [h for h in hist.get(name, []) if (h[1] & ~m).any()]
+        for name, m in o["r"]:
+            hist.setdefault(name, []).append((k, m, False))
+        for name, m in o["w"]:
+            hist.setdefault(name, []).append((k, m, True))
+        o["banks"] = {name for name, m in o["r"] + o["w"] if SCRATCH[name][0] == "psum"}
+    succ = [[] for _ in ops]
+    for k, o in enumerate(ops):
+        for j in o["dep"]:
+            succ[j].append(k)
+    SY = 0.08
+    pr = [0.0] * n
+    for k in range(n - 1, -1, -1):
+        o = ops[k]
+        c = min(v[1] for v in o["var"].values()) + (2.0 + o["lat"] / 200e3 if "dma" in o else o["lat"])
+        pr[k] = c + max([pr[s] + SY for s in succ[k]], default=0.0)
+    bias = [0.0] * n
+    for kind, lo, hi, amt in PAR["moves"]:
+        for k in range(lo, min(hi, n)):
+            if kind:
+                bias[k] += amt
+            else:
+                pr[k] += amt
+    for k, o in enumerate(ops):
+        if "dma" in o and not o["dep"]:
+            pr[k] = 1e4 - k
+    free = {q: 0.0 for q in "DAPGS"}
+    bank = {}
+    dmafree = [0.0]
+    done = [None] * n
+    order = {q: [] for q in "DAPGS"}
+    left = [len(o["dep"]) for o in ops]
+    ready = [k for k in range(n) if left[k] == 0]
+    seq = []
+    firstx = [1.5]
+    while ready:
+        cand = []
+        for k in ready:
+            o = ops[k]
+            rt = max([done[j] + SY for j in o["dep"]], default=0.0)
+            v = {}
+            for q, (calls, c) in o["var"].items():
+                v[q] = (max(rt, free[q], max([bank[x][0] + (SY if bank[x][1] != q else 0) for x in o["banks"] if x in bank], default=0.0)), k, q, c)
+            if len(v) == 2 and v["A"][0] <= v["D"][0] + PAR["m0"] + bias[k]:
+                del v["D"]
+            cand += v.values()
+        t0 = min(c[0] for c in cand)
+        q0 = min(cand)[2]
+        pick = min(cand)
+        same = [c for c in cand if c[2] == q0]
+        same.sort(key=lambda c: -pr[c[1]] + (PAR["m1"] if q0 == "D" and len(ops[c[1]]["var"]) == 2 else 0.0))
+        for c in same:
+            if c[0] <= t0 + PAR["e0"]:
+                pick = c
+                break
+        for c in same:
+            if pr[c[1]] > pr[pick[1]] + PAR["p1"] and c[0] < pick[0] + PAR["f1"] * pick[3] and c[0] - pick[0] < PAR["e1"]:
+                pick = c
+                break
+        st, k, q, c = pick
+        o = ops[k]
+        o["q"], o["st"] = q, st
+        free[q] = st + c
+        end = st + c
+        if "dma" in o:
+            dmafree[0] = max(dmafree[0], st + 1.6) + o["lat"] / 250e3
+            end = dmafree[0] + 0.4
+        elif "x" in o:
+            end += o["lat"] + firstx[0]
+            free[q] += firstx[0]
+            firstx[0] = 0.0
+        done[k] = end
+        prev = set()
+        for x in o["banks"]:
+            if x in bank and (bank[x][1] != q or ops[bank[x][2]].get("tile") != o.get("tile")):
+                prev.add(bank[x][2])
+            bank[x] = (end, q, k)
+        o["dep2"] = o["dep"] | prev
+        order[q].append(k)
+        seq.append(k)
+        ready.remove(k)
+        for s in succ[k]:
+            left[s] -= 1
+            if left[s] == 0:
+                ready.append(s)
+    cnt = {q: 0 for q in "DAPG"}
+    know = {q: {} for q in "DAPGS"}
+    for k in seq:
+        o = ops[k]
+        q = o["q"]
+        waits = {}
+        for j in sorted(o["dep2"], key=lambda j: -ops[j]["st"]):
+            sem, val = ops[j]["sig"]
+            if know[q].get(sem, 0) < val:
+                waits[sem] = max(waits.get(sem, 0), val)
+                for s2, v2 in ops[j]["know"].items():
+                    know[q][s2] = max(know[q].get(s2, 0), v2)
+                know[q][sem] = val
+        o["waits"] = waits
+        o["know"] = dict(know[q])
+        if "dma" in o:
+            o["sig"] = (o["dma"], 16)
+        elif "x" in o:
+            o["sig"] = (o["x"], 8)
+        else:
+            cnt[q] += 1
+            o["sig"] = ("e" + q, cnt[q])
+    return seq, cnt, max(done)
+
+
+PLAN = {}
+PAR = dict(m0=0.7, m1=10.0, e0=0.02, p1=1.0, f1=0.3, e1=0.6,
+           moves=[(1, 798, 878, -0.5), (1, 421, 621, 3.0), (1, 1110, 1120, 1.0), (0, 1239, 1242, -1.5), (1, 382, 385, -0.5), (0, 171, 201, -1.5)])
+
+
+def plan():
+    if not PLAN:
+        ops = build()
+        seq, cnt, end = schedule(ops)
+        PLAN.update(ops=ops, seq=seq, cnt=cnt, end=end)
+    return PLAN
+
+
+def rank_program(g, core, T, topo):
+    rank = T.rank_of(core)
+    if rank is None:
+        return
+    P = plan()
+    n = len(T.cores)
+    Q = {"D": g.vector, "A": g.scalar, "P": g.tensor, "G": g, "S": g.sync}
+
+    def ap(a):
+        if not _isap(a):
+            return a
+        if a[0] == "ind":
+            return ap(a[1]).indirect(ap(a[2]))
+        return T[a[0]][a[1]]
+
+    sent = 0
+    for k in P["seq"]:
+        o = P["ops"][k]
+        q = Q[o["q"]]
+        for sem, val in o["waits"].items():
+            q.wait_ge(T.sem[sem], val)
+        last = None
+        for c in o["var"][o["q"]][0]:
+            kind, a = c[0], [ap(x) for x in c[1:]]
+            if kind == "tensor_tensor":
+                last = q.tensor_tensor(*a)
+            elif kind == "tensor_scalar":
+                last = q.tensor_scalar(*a)
+            elif kind == "tensor_copy":
+                last = q.tensor_copy(*a)
+            elif kind == "tensor_tensor_scan":
+                last = q.tensor_tensor_scan(*a)
+            elif kind == "transpose" or kind == "ptr":
+                last = q.transpose(*a)
+            elif kind == "memset":
+                last = q.memset(*a)
+            elif kind == "reduce":
+                last = q.tensor_reduce(a[0], a[1], AX.X, a[2])
+            elif kind == "matmul":
+                last = q.matmul(*a)
+            elif kind == "act":
+                last = q.activation(a[0], a[1], a[2], scale=a[4]) if a[3] is None else q.activation(a[0], a[1], a[2], bias=a[3], scale=a[4])
+            elif kind == "sign":
+                last = q.activation(a[0], a[1], F.Sign, bias=a[2], scale=-1.0, accum_out=a[3])
+            elif kind == "iota":
+                if SCRATCH[c[1][0]][2] == i32:
+                    last = q.iota(*a)
+                else:
+                    last = q.iota(*a, allow_small_or_imprecise_dtypes=True)
+            elif kind == "dma":
+                q.dma_start(a[0], a[1]).then_inc(T.sem[c[3]], 16)
+            elif kind == "remote":
+                parts = c[1]
+                eng = [e for e in topo.engines(core, T.cores[(rank + 1) % n]) if e in topo.engines(core, T.cores[(rank - 1) % n])]
+                per = len(eng) // len(parts)
+                tr = []
+                for m, (side, src, dst) in enumerate(parts):
+                    rid, pid = topo.addr(T.cores[(rank + side) % n], core)
+                    tr.append(RemoteDMATransfer(dst_ids=[DstId(rid=rid, pnc=pid)], dma_engine_mask=sum(1 << e for e in eng[per * m:per * m + per]),
+                                                remote_sem=T.sem[c[2]], src=ap(src), dst=ap(dst)))
+                g.remote_dma_fused(tr, local_sem=T.sem.sent)
+                sent += per * len(parts)
+        if last is not None:
+            last.then_inc(T.sem[o["sig"][0]], 1)
+    for e, v in P["cnt"].items():
+        g.wait_ge(T.sem["e" + e], v)
+    for o in P["ops"]:
+        if "dma" in o or "x" in o:
+            g.wait_ge(T.sem[o["sig"][0]], o["sig"][1])
+    g.wait_ge(T.sem.sent, sent)

@@ -4,42 +4,49 @@ from concourse.mybir import AluOpType as A, AxisListType as AX, ActivationFuncti
 
 S_ = np.s_
 f32, bf, i32, u16 = "float32", "bfloat16", "int32", "uint16"
-LV = 4
-GR = 4
-FW = 3208 + 1288 * (LV - 1)
+OPT = dict(rbg=1, L=(4, 2, 2), pair=(1, 0, 0), nA=(128, 128, 128), merge=((0, 0, 0), (0, 0, 0), (0, 0, 0)), pe_est=1, silu=0, sel=0, cd=32, rg=64, ro=64, ov=0.0, ova=0.04, pe=0.55)
+L_ = OPT["L"]
+UO_, BS_, CP_ = 1424, 2704, 3216
+FW = lambda L: CP_ + 1288 * (L - 1)
+RG_, RO_ = OPT["rg"], OPT["ro"]
+NG_ = max(64 * (128 - n + min(n, RG_)) for n in OPT["nA"])
+NO_ = max(16 * (128 - n) + 32 * min(n, RO_) for n in OPT["nA"])
+ALLA = min(OPT["nA"]) == 128
 SB = {
     "Lin": ([4, 64], i32), "Ls": ([3, 64], f32), "Ld": ([12, 2, 16], f32), "Lt": ([3, 4, 2, 16], f32),
-    "V1": ([3, 80], bf), "D2": ([80, 2], bf), "VW": ([3, 80], bf), "VD": ([80], bf), "VR": ([2, 1296], bf),
-    "NT": ([1280], i32), "NM": ([1288], f32), "AL": ([1288], i32),
-    "F0": ([FW], f32), "F1": ([FW], f32), "F2": ([FW], f32), "LF": ([3, 512], f32),
-    "WT": ([792], f32), "IOT": ([1296], f32), "XT": ([1288], bf), "RC": ([8], f32), "DU": ([32], f32), "CG": ([8], u16),
-    "GO": ([3, 8, 4], f32), "NG": ([3, 32], f32), "OM": ([32], f32), "FX": ([32], f32), "FI": ([32], f32), "TG": ([32], f32),
-    "UT": ([3, 32], u16), "LH": ([128], f32), "XR": ([128], bf),
-    "RG": ([128], f32), "RI": ([128], f32), "DM": ([128], f32), "BO": ([128], bf), "TB": ([128], bf), "SH": ([128], bf),
-    "IDB": ([128], bf), "IDF": ([128], f32), "NEG": ([128], bf), "AK": ([144], bf), "RB": ([16, 128], bf),
-    "CO": ([32], f32), "CB": ([2], bf), "CI": ([32], i32), "CR": ([8, 16], f32), "C8": ([6, 8], f32), "TH": ([24], f32),
+    "V1": ([3, 80], bf), "D2": ([80, 2], bf), "VW": ([3, 80], bf), "VD": ([80], bf), "VR": ([3, 1296], bf),
+    "NT": ([1280], i32), "AI": ([1280], i32), "NM": ([1288], f32), "AL": ([1296], bf),
+    "UX": ([1288], f32), "FI": ([2, 1288 if max(OPT["merge"][1] + OPT["merge"][2]) else 8], i32),
+    "F0": ([FW(max(L_[0], L_[2]))], f32), "F1": ([FW(L_[1])], f32), "LF": ([3, 512], f32), "PT": ([8 if ALLA else 16 * OPT["cd"]], f32), "UA": ([3, 128], f32), "NO": ([3, 2, 256], u16),
+    "WT": ([792], f32), "IOT": ([1296], f32), "XT": ([1296], bf), "RC": ([8], f32), "DU": ([32], f32), "CG": ([8], u16),
+    "GO": ([3, 8, 4], f32), "NG": ([3, 32], f32), "LW": ([3, 32], f32), "FL": ([32], f32), "TG": ([32], f32),
+    "UT": ([3, 32], u16), "LH": ([128], f32), "XR": ([128], bf), "EH": ([8], f32),
+    "RG": ([128], f32), "RI": ([128], f32), "DM": ([128], f32), "DS": ([16], f32), "BO": ([128], bf), "TB": ([128], bf), "SH": ([128], bf),
+    "IDB": ([128], bf), "IDF": ([128], f32), "IDJ": ([2, 128], f32), "NEG": ([128], bf), "AK": ([144], bf), "RB": ([16, 128], bf),
+    "CO": ([40], f32), "CB": ([2], bf), "CI": ([32], i32), "CR": ([8, 16], f32), "C8": ([6, 8], f32), "TH": ([24], f32),
     "T1": ([128], f32), "T2": ([128], f32), "T3": ([8, 16], f32), "TI": ([96], i32), "XH": ([96], f32), "XL": ([16], f32),
-    "HA": ([96], f32), "HC": ([896], bf), "US": ([128], f32), "LT": ([128], f32), "NF": ([2, 256], f32), "C80": ([3, 80], f32),
-    "SM": ([64], bf), "SP": ([64], bf), "ZR": ([64], f32), "LC": ([8, 64], bf), "RK": ([72], f32), "CM": ([128], bf), "IM": ([8, 16], f32),
-    "W": ([3, 12, 8], f32), "I": ([3, 12, 8], i32), "U": ([3, 20, 8], u16), "UF": ([3, 32], u16), "UM": ([3, 32], u16),
-    "NU": ([128], u16), "GV": ([2048], bf), "A15": ([128], f32), "MR": ([3, 128], f32), "EQ": ([3, 128], bf), "NC": ([128], f32),
-    "PR": ([128], f32), "VM": ([2, 512], bf), "NO": ([2, 2, 256], u16),
-    "XA": ([128], bf), "XB": ([2, 128], bf), "HB": ([896], bf), "EB": ([6, 8, 2, 2, 2, 16], bf),
+    "HA": ([96], f32), "HC": ([896], bf), "US": ([128], f32), "C80": ([3, 80], f32),
+    "SM": ([64], bf), "SP": ([64], bf), "ZR": ([64], f32), "LC": ([8, 64], bf), "RK": ([72], f32), "CM": ([128], bf), "IM": ([8, 19], f32), "VE": ([64], f32), "VF": ([128], bf),
+    "W": ([3, 12, 8], f32), "I": ([3, 12, 8], i32), "U": ([3, 8, 8], u16), "UF": ([3, 32], u16), "UM": ([3, 32], u16),
+    "NU": ([3, 4, 128], u16), "GV": ([2048], bf), "AG": ([128], bf), "AT": ([128], f32), "MR": ([3, 128], f32), "EQ": ([4, 128], bf), "NC": ([128], f32),
+    "VI": ([128], i32), "PR": ([128], f32), "KY": ([8, 16], f32), "VM": ([3, 512], bf), "ZS": ([128], bf),
+    "XB": ([128], bf), "HB": ([896], bf), "EB": ([9, 8, 2, 2, 2, 16], bf),
     "CN": ([3, 80], bf), "LN": ([3, 32], bf), "NP": ([80], bf), "HM": ([80], bf),
-    "N1": ([3, 80], f32), "UW": ([2, 80], u16), "UO": ([2, 80], u16), "WN": ([1280], f32),
-    "G": ([2, 512 * GR], f32), "ON": ([2048], f32), "OX": ([2048], f32), "LO": ([128], f32), "HI": ([128], f32),
+    "N1": ([3, 80], f32), "UW": ([3, 80], u16), "UO": ([3, 80], u16), "WN": ([1280], f32),
+    "G": ([NG_], f32), "ON": ([NO_], f32), "OX": ([NO_], f32), "PB": ([128], bf), "LO": ([128], f32), "HI": ([128], f32),
     "UV": ([512], f32), "U0": ([128], f32), "DD": ([128], f32), "D8": ([128], f32), "S1": ([128], f32),
     "MM": ([128], f32), "TE": ([128], f32), "ES": ([512], f32), "ZH": ([2, 72, 16], bf), "ZL": ([2, 72, 16], bf),
     "CC": ([3, 128], f32), "GA": ([128], f32),
 }
 SCRATCH = {k: ("sbuf", [128] + v[0], v[1]) for k, v in SB.items()}
 for _b in range(8):
-    SCRATCH["P%d" % _b] = ("psum", [128, 32, 16] if _b in (1, 2, 3, 4) else [128, 512], f32)
+    SCRATCH["P%d" % _b] = ("psum", [128, 512] if _b == 0 else [128, 32, 16], f32)
 NDMA = 14
 SEMAPHORES = ["eD", "eA", "eP", "eG", "sent"] + ["d%d" % k for k in range(NDMA)] + ["x%d" % k for k in range(10)]
-CY = 0.83 * 1.2e-3
-GA_, SC_ = 1.55, 3.8
+CY = 0.83e-3 * 1.05
+GA_, SC_, PE_ = 1.55, 3.8, OPT["pe"]
 BIG = float(2 ** 24)
+MAGIC = 1.5 * 2 ** 23
 
 
 def _shape(name):
@@ -72,6 +79,10 @@ def _two(*aps):
     return all(SCRATCH[a[0]][2] in (bf, u16) for a in aps)
 
 
+def _ps(a):
+    return a[0] != "ind" and SCRATCH[a[0]][0] == "psum"
+
+
 def build():
     ops = []
 
@@ -90,14 +101,13 @@ def build():
 
     def dcost(out, ins, per):
         if out[0] == "ind":
-            return 0.06 + _n(out) * SC_ * CY
+            return 0.05 + _n(out) * SC_ * CY
         if ins[0][0] == "ind":
-            return 0.06 + _n(ins[0]) * GA_ * CY
-        return 0.03 + max(64, _n(ins[0]) * per) * CY
+            return 0.05 + _n(ins[0]) * GA_ * CY
+        return OPT["ov"] + max(64, _n(ins[0]) * per) * CY
 
     def tt(o, a, b, op):
-        ps = a[0][0] == "P" and a[0] != "PR" or b[0][0] == "P" and b[0] != "PR"
-        add({"D": ([("tensor_tensor", o, a, b, op)], dcost(o, [a], 1 if ps else 2))}, [a, b], [o])
+        add({"D": ([("tensor_tensor", o, a, b, op)], dcost(o, [a], 1 if _ps(a) or _ps(b) else 2))}, [a, b], [o])
 
     def ts(o, a, s1, op0, s2=None, op1=None):
         c = ("tensor_scalar", o, a, s1, s2, op0) + (() if op1 is None else (op1,))
@@ -107,7 +117,7 @@ def build():
         add({"D": ([("tensor_copy", o, a)], dcost(o, [a], 0.5 if a[0] != "ind" and o[0] != "ind" and _two(o, a) else 1))}, [a], [o])
 
     def acost(a):
-        return 0.08 + _n(a) * GA_ * CY if a[0] == "ind" else 0.06 + max(64, _n(a)) * CY
+        return 0.065 + _n(a) * GA_ * CY if a[0] == "ind" else OPT["ova"] + max(64, _n(a)) * CY
 
     def aff(o, a, sc=1.0, bi=None, eng="AD"):
         if bi is None:
@@ -119,9 +129,15 @@ def build():
         var = {"D": ([d], dcost(o, [a], 0.5 if a[0] != "ind" and _two(o, a) else 1)), "A": ([s], acost(a))}
         add({e: var[e] for e in eng}, [a, sc, bi], [o])
 
-    def hot(o, a):
-        add({"D": ([("tensor_scalar", o, a, -0.5, None, A.is_ge)], dcost(o, [a], 1)), "A": ([("act", o, a, F.Relu, ("CO", S_[:, 31:32]), 1.0)], acost(a))},
-            [a, ("CO", S_[:, 31:32])], [o])
+    def hot(o, a, at, bi):
+        add({"D": ([("tensor_scalar", o, a, at - 0.5, None, A.is_ge)], dcost(o, [a], 1)), "A": ([("act", o, a, F.Relu, bi, 1.0)], acost(a))},
+            [a, bi], [o])
+
+    def scatter(o, a):
+        var = {"D": ([("tensor_copy", o, a)], dcost(o, [a], 1))}
+        if OPT["silu"]:
+            var["A"] = ([("act", o, a, F.Silu, None, None)], 0.065 + _n(o) * SC_ * CY)
+        add(var, [a], [o])
 
     def red(o, a, op):
         add({"D": ([("reduce", o, a, op)], dcost(o, [a], 1))}, [a], [o])
@@ -133,7 +149,7 @@ def build():
         add({"D": ([("transpose", o, a)], dcost(o, [a], 1))}, [a], [o])
 
     def ms(o, c, soon=False):
-        if not soon and float(c).is_integer():
+        if not soon and float(c).is_integer() and abs(c) < BIG:
             return iota(o, [[0, _n(o)]], int(c))
         add({"D": ([("memset", o, c)], dcost(o, [o], 0.5 if _two(o) else 1))}, [], [o])
 
@@ -142,24 +158,27 @@ def build():
         for k, (o, l, r) in enumerate(lst):
             gs = len(lst) if group is True else max(1, int(group))
             calls.append(("matmul", o, l, r, k % gs == 0, k % gs == gs - 1))
-            c += max(64, _n(r)) * 0.7 * CY * (4 if SCRATCH[r[0]][2] == f32 else 1)
+            c += max(min(64, _n(l)), _n(r)) * PE_ * CY * (4 if SCRATCH[r[0]][2] == f32 else 1)
             rd += [l, r]; wr.append(o)
-        add({"P": (calls, c + 0.05)}, rd, wr)
+        add({"P": (calls, c)}, rd, wr, lat=0.05)
 
     def iota(o, pat, base=0, cm=0):
-        add({"G": ([("iota", o, pat, base, cm)], 0.15 + 2 * _n(o) * CY)}, [], [o])
+        add({"G": ([("iota", o, pat, base, cm)], 0.14 + 2 * _n(o) * CY)}, [], [o])
 
-    nd = [0]
+    nd = [0, 0.0]
 
     def dma(q, o, a, nbytes):
-        op = add({q: ([("dma", o, a, "d%d" % nd[0])], 0.1)}, [a], [o], lat=nbytes)
+        load = a[0] not in SCRATCH
+        nd[1] = (nd[1] if load else 0.0) + nbytes / 250e3
+        op = add({q: ([("dma", o, a, "d%d" % nd[0])], 0.05)}, [a], [o], lat=2.0 + nd[1])
         op["dma"] = "d%d" % nd[0]
+        op["load"] = load
         nd[0] += 1
 
     nx = [0]
 
     def xchg(parts, nbytes):
-        op = add({"G": ([("remote", parts, "x%d" % nx[0])], 0.3)}, [p[1] for p in parts], [p[2] for p in parts], lat=2.2 + nbytes / 60e3)
+        op = add({"G": ([("remote", parts, "x%d" % nx[0])], 0.3 if nx[0] else 1.8)}, [p[1] for p in parts], [p[2] for p in parts], lat=1.6 + nbytes / 100e3)
         op["x"] = "x%d" % nx[0]
         nx[0] += 1
 
@@ -172,18 +191,23 @@ def build():
     def ind(w, o):
         return ("ind", w, o)
 
-    UO_, BS_ = 1416, 2696
+    def pb(bank, c0, c1):
+        return ("P%d" % bank, S_[:, c0 // 16:c1 // 16, :])
+
+    p0 = lambda c0, c1: b("P0", S_[:, c0:c1])
+
     dma("S", b("Lin", S_[:, 0, :]), b("vol"), 32e3)
     dma("A", b("Lin", S_[:, 1, :]), b("dv", S_[:, 0:1024]), 32e3)
-    dma("S", b("F0", S_[:, UO_:UO_ + 128]), b("u", S_[:, 0:128]), 64e3)
-    dma("A", b("F0", S_[:, UO_ + 896:UO_ + 1024]), b("u", S_[:, 896:1024]), 64e3)
+    plain = not (OPT["silu"] or max(map(max, OPT["merge"])))
+    u0 = lambda c0, c1: b("F0", S_[:, UO_ + c0:UO_ + c1]) if plain else b("UX", S_[:, 8 + c0:8 + c1])
+    dma("S", u0(0, 128), b("u", S_[:, 0:128]), 64e3)
+    dma("A", u0(896, 1024), b("u", S_[:, 896:1024]), 64e3)
     dma("S", b("NT"), b("nt"), 655e3)
+    dma("S", u0(128, 896), b("u", S_[:, 128:896]), 393e3)
     dma("S", b("Lin", S_[:, 2, :]), b("dv", S_[:, 1024:2048]), 32e3)
     dma("S", b("Lin", S_[:, 3, :]), b("dv", S_[:, 2048:3072]), 32e3)
     dma("S", b("WT", S_[:, 8:264]), b("wt"), 131e3)
-    dma("S", b("F0", S_[:, UO_ + 128:UO_ + 896]), b("u", S_[:, 128:896]), 393e3)
-    xchg([(1, b("F0", S_[:, UO_ + 896:UO_ + 1024]), b("F0", S_[:, UO_ + 1024:UO_ + 1152])),
-          (-1, b("F0", S_[:, UO_:UO_ + 128]), b("F0", S_[:, UO_ + 1152:UO_ + 1280]))], 131e3)
+    xchg([(1, u0(896, 1024), u0(1024, 1152)), (-1, u0(0, 128), u0(1152, 1280))], 131e3)
     iota(b("CI", S_[:, 0:1]), [[0, 1]], 0, 1)
     iota(b("IOT", S_[:, 0:144]), [[1, 144]])
     iota(b("RG"), [[1, 8], [0, 16]])
@@ -199,20 +223,20 @@ def build():
     ts(ci(2), ci(0), 15, A.bitwise_and)
     ts(ci(3), ci(0), 4, A.arith_shift_right)
     cp(col(0), ci(0)); cp(col(1), ci(2)); cp(col(2), ci(3))
-    ms(col(31), 1.0)
-    ms(col(30), 1288.0)
+    for k, v in ((31, -11.0), (30, 1288.0), (25, 9.0), (26, -29.0), (27, MAGIC), (28, -MAGIC)):
+        ms(col(k), v)
     ms(b("ZR"), 0.0, True)
     ms(b("RK", S_[:, 64:72]), 0.0)
 
-    def unblock(a0, a1, outs):
+    def unblock(a0, a1, outs, shift):
         for h in (0, 1):
-            ts(b("Ld", S_[:, 4 * a0:4 * a1, h, :]), b("Ls", S_[:, a0:a1, :]), col(4 - h), A.mult)
+            ts(b("Ld", S_[:, 4 * a0:4 * a1, h, :]), b("Ls", S_[:, a0:a1, :]), shift, A.add, col(4 - h), A.mult)
         vtr(b("Lt", S_[:, a0:a1]), b("Ld", S_[:, 4 * a0:4 * a1]))
         for a in range(a0, a1):
             for c4 in range(4):
                 tt(outs(a, c4), b("Lt", S_[:, a, c4, 0, :]), b("Lt", S_[:, a, c4, 1, :]), A.add)
     tt(b("Ls", S_[:, 0, :]), b("Lin", S_[:, 0, :]), b("Lin", S_[:, 1, :]), A.add)
-    unblock(0, 1, lambda a, c4: b("V1", S_[:, 0, c4:64:4]))
+    unblock(0, 1, lambda a, c4: b("V1", S_[:, 0, c4:64:4]), -9.0)
     xchg([(1, b("V1", S_[:, 0, 56:64]), b("V1", S_[:, 0, 64:72])), (-1, b("V1", S_[:, 0, 0:8]), b("V1", S_[:, 0, 72:80]))], 16e3)
     ts(b("BO"), b("RG"), col(2), A.is_equal)
     ts(b("DM", S_[:, 0:128]), b("RI", S_[:, 0:128]), col(1), A.is_equal)
@@ -225,83 +249,110 @@ def build():
         aff(b("DU", S_[:, 8 * j:8 * j + 8]), c8(0), 1.0, col(30))
     cp(b("RC"), b("BO", S_[:, 0::16]))
     cp(b("CG"), b("IOT", S_[:, 0:8]))
-    ms(b("GO", S_[:, :, :, 0]), 1.0)
-    for i in range(16):
-        aff(b("RB", S_[:, i, :]), b("BO"), b("DM", S_[:, i:i + 1]))
+    aff(b("EH"), b("IOT", S_[:, 0:8]), -0.5)
+    aff(b("DS"), b("DM", S_[:, 0:16]), 0.0625)
+    if OPT["rbg"]:
+        ms(b("GV", S_[:, 0:512]), 0.0625)
+        for q in range(4):
+            o, a = b("RB", S_[:, 4 * q:4 * q + 4, :]), b("GV", S_[:, 0:512])
+            add({"G": ([("affine_select", o, a, [[-1, 4], [-16, 8], [0, 16]], A.is_equal, 0.0, -4 * q, 1)], 0.17 + 1024 * CY)}, [a], [o])
+    else:
+        for i in range(16):
+            aff(b("RB", S_[:, i, :]), b("BO"), b("DS", S_[:, i:i + 1]))
     ts(col(5), col(0), 15.0, A.add)
     ts(b("AK"), b("IOT", S_[:, 0:144]), col(5), A.is_equal, b("DM", S_[:, 0:1]), A.mult)
     ts(b("IDB"), b("IOT", S_[:, 0:128]), col(0), A.is_equal)
     ts(b("IDF"), b("IOT", S_[:, 0:128]), col(0), A.is_equal)
     aff(b("NEG"), b("IDB"), -BIG)
+    if OPT["pe_est"]:
+        for j in (2, 3):
+            aff(b("IDJ", S_[:, j - 2, :]), b("IDF"), float(j))
     ts(col(7), col(1), -2048.0, A.mult, 31 * 2048.0, A.add)
-    ms(b("VR", S_[:, :, 0:8]), 0.0)
-    ms(b("NM", S_[:, 0:8]), 8.0)
-    ms(b("AL", S_[:, 0:8]), 0)
+    ms(b("VR", S_[:, :, 0:8]), -0.5625)
+    ms(b("NM", S_[:, 0:8]), 0.0)
+    ms(b("AL", S_[:, 0:8]), 0.0)
+    ms(b("FI", S_[:, :, 0:8]), 0.0)
     for h in (0, 1):
-        al, nt = b("AL", S_[:, 8 + 640 * h:648 + 640 * h]), b("NT", S_[:, 640 * h:640 * h + 640])
-        ts(al, nt, 4, A.arith_shift_right)
-        ts(b("NM", al[1]), al, 8.0, A.add)
-        ts(al, nt, 15, A.bitwise_and)
+        c = S_[:, 640 * h:640 * h + 640]
+        c8_ = S_[:, 8 + 640 * h:648 + 640 * h]
+        ts(b("AI", c), b("NT", c), 4, A.arith_shift_right)
+        ts(b("NM", c8_), b("AI", c), 8.0, A.add)
+        ts(b("NT", c), b("NT", c), 15, A.bitwise_and)
+        ts(b("AL", c8_), b("NT", c), 32768.0, A.mult)
+    for c0, c1 in ((128, 512), (512, 896), (0, 128), (896, 1280)):
+        ux = b("UX", S_[:, 8 + c0:8 + c1])
+        if max(OPT["merge"][0]):
+            aff(ux, ux, 2.0 ** 17, col(27))
+            aff(ux, ux, 1.0, col(28))
+        elif not plain:
+            aff(b("F0", S_[:, UO_ + c0:UO_ + c1]), ux, 2.0 ** 17)
     ts(ci(4), ci(0), 112, A.add)
     ts(ci(5), ci(4), 127, A.bitwise_and)
     cp(col(6), ci(5))
     ts(b("SH"), b("IOT", S_[:, 0:128]), col(6), A.is_equal)
     cp(b("Ls", S_[:, 1:3, :]), b("Lin", S_[:, 2:4, :]))
-    unblock(1, 3, lambda a, c4: b("D2", S_[:, c4:64:4, a - 1]))
+    unblock(1, 3, lambda a, c4: b("D2", S_[:, c4:64:4, a - 1]), 0.0)
     xchg([(1, b("D2", S_[:, 56:64, :]), b("D2", S_[:, 64:72, :])), (-1, b("D2", S_[:, 0:8, :]), b("D2", S_[:, 72:80, :]))], 16e3)
     xchg([(1, b("WT", S_[:, 8:264]), b("WT", S_[:, 272:528])), (-1, b("WT", S_[:, 8:264]), b("WT", S_[:, 536:792]))], 262e3)
     for k in (0, 264, 528):
         ms(b("WT", S_[:, k:k + 8]), 1.0)
-    ms(b("CR"), 0.0)
-    for k, sl, v in ((0, S_[0:1], 1.0), (1, S_[2:6:3], 1.0), (2, S_[3:7:3], 1.0), (3, S_[1:2], 1.0), (4, S_[4:8:3], 1.0),
-                     (5, S_[5:8], 1.0), (6, S_[0:2], 2.0), (6, S_[5:8], -1.0), (7, S_[2:4], -1.0)):
-        ms(b("CR", (S_[:], k, sl)), v)
-    tt(b("T3"), b("CR"), b("DM", S_[:, 0:128]), A.mult)
-    red(b("CO", S_[:, 8:16]), b("T3"), A.add)
-    ts(col(16), col(13), -1.0, A.mult, 1.0, A.add)
-    ts(col(17), b("DM", S_[:, 4:5]), -1.0, A.mult)
-    tt(col(18), col(17), col(15), A.add)
-    for h in (0, 1):
-        tt(col(19 + h), col(14), col(4 - h), A.mult)
-        tt(col(21 + h), col(18), col(4 - h), A.mult)
-    x81 = b("IOT", S_[:, 0:96])
-    tt(b("TI"), x81, x81, A.mult)
-    cp(b("T1", S_[:, 0:96]), b("TI"))
-    ts(b("TI"), b("TI"), 31, A.bitwise_and)
-    tt(b("T1", S_[:, 0:96]), b("T1", S_[:, 0:96]), b("TI"), A.subtract)
-    ts(b("T1", S_[:, 0:96]), b("T1", S_[:, 0:96]), col(9), A.mult)
-    ts(b("T2", S_[:, 0:96]), b("TI"), col(10), A.mult)
-    ts(b("XH"), x81, col(8), A.mult)
-    tt(b("XH"), b("XH"), b("T1", S_[:, 0:96]), A.add)
-    tt(b("XH"), b("XH"), b("T2", S_[:, 0:96]), A.add)
-    ts(b("XL"), b("IOT", S_[:, 0:16]), col(12), A.mult, col(11), A.add)
-    tt(b("XL"), b("XL"), b("IOT", S_[:, 0:16]), A.mult)
+    ms(b("T1"), 0.5)
+    ms(b("GA"), 0.0)
+    scan(b("T2"), b("T1"), b("GA"), float(2 ** 65), A.mult, A.add)
+    tt(b("T1"), b("T2"), b("IDF"), A.mult)
+    red(b("CB", S_[:, 0:1]), b("T1"), A.max)
+    tt(b("T3"), b("T2"), b("DM", S_[:, 0:128]), A.mult)
+    red(c8(2), b("T3"), A.max)
+    for j in range(3):
+        aff(b("TH", S_[:, 8 * j:8 * j + 8]), c8(2), 2.5)
+    ts(col(8), col(1), 4.0, A.is_ge)
+    ts(col(9), col(1), 11.0, A.is_lt, col(8), A.mult)
+    ts(col(10), col(1), 4.0, A.is_lt)
+    ts(col(11), col(8), 15.0 * 2.0 ** -65, A.mult, 2.0 ** -65, A.add)
+    tt(col(11), col(11), b("C8", S_[:, 2, 0:1]), A.mult)
+    aff(col(12), b("DM", S_[:, 11:12]), 5.0)
+    aff(col(13), b("DM", S_[:, 11:12]), 7.0)
+    ts(b("XH"), b("IOT", S_[:, 0:96]), 0.5, A.add, col(11), A.mult)
+    ts(b("TI"), b("XH"), -0.5, A.add)
+    tt(b("XH"), b("XH"), b("TI"), A.subtract)
+    ts(b("HA"), b("XH"), 0.5, A.is_ge, 0.5, A.subtract)
+    ts(b("XH"), b("HA"), 2.0, A.mult, col(9), A.mult)
+    ts(b("XL"), b("HA", S_[:, 0:16]), 2.0, A.mult, col(10), A.mult)
+    aff(b("XL"), b("XL"), 1.0, b("DM", S_[:, 11:12]))
     for lo in range(16):
-        aff(b("XT", S_[:, 8 + lo::16]), b("XH", S_[:, 0:80]), 1.0, b("XL", S_[:, lo:lo + 1]))
-    aff(b("XT", S_[:, 0:8]), b("ZR", S_[:, 0:8]), 1.0, b("XH", S_[:, 80:81]))
+        aff(b("XT", S_[:, 8 + lo:1288:16]), b("XH", S_[:, 0:80]), 1.0, b("XL", S_[:, lo:lo + 1]))
+    tt(col(14), b("XH", S_[:, 80:81]), b("XL", S_[:, 0:1]), A.add)
+    aff(b("XT", S_[:, 0:8]), b("ZR", S_[:, 0:8]), 1.0, col(14))
     PERM = ((0, 56, 8), (8, 72, 8), (16, 64, 8), (24, 0, 56))
-    for p0, h0, w in PERM:
-        aff(b("HA", S_[:, p0:p0 + w]), b("XH", S_[:, h0:h0 + w]), col(14), col(15))
-    aff(b("HA", S_[:, 80:96]), b("XL"), col(14), col(17))
-    ms(b("HC", S_[:, 640:896]), -1.0)
+    for q0, h0, w in PERM:
+        aff(b("HA", S_[:, q0:q0 + w]), b("XH", S_[:, h0:h0 + w]), 1.0, col(12))
+    aff(b("HA", S_[:, 80:96]), b("XL"), 1.0, col(13))
+    ms(b("HC", S_[:, 640:896]), 0.0)
     for g in range(8):
         gm = b("RC", S_[:, g:g + 1])
         aff(b("HC", S_[:, 80 * g:80 * g + 80]), b("HA", S_[:, 0:80]), gm)
         o = 640 + 32 * g + 16 * (g % 2)
         aff(b("HC", S_[:, o:o + 16]), b("HA", S_[:, 80:96]), gm)
-    ms(b("T1"), 0.5)
-    ms(b("GA"), 0.0)
-    scan(b("T2"), b("T1"), b("GA"), float(2 ** 65), A.mult, A.add)
-    tt(b("T1"), b("T2"), b("IDF"), A.mult)
-    red(col(23), b("T1"), A.max)
-    cp(b("CB", S_[:, 0:1]), col(23))
-    tt(b("T3"), b("T2"), b("DM", S_[:, 0:128]), A.mult)
-    red(c8(2), b("T3"), A.max)
-    for j in range(3):
-        aff(b("TH", S_[:, 8 * j:8 * j + 8]), c8(2), 2.5)
-    for v in range(LV):
-        ms(b("US", S_[:, v::LV]), 2.0 ** (8 * v), v == 3)
-        ms(b("LT", S_[:, v::LV]), float(1800 + 1288 * (v - 1) if v else 0))
+    if not ALLA:
+        ms(b("TE"), 256.0)
+        ms(b("TE", S_[:, 0::16]), 0.0)
+        ms(b("MM"), 0.0)
+        ms(b("MM", S_[:, 0::16]), 2.0 ** -56)
+        scan(b("US"), b("TE"), b("MM"), 0.0, A.mult, A.add)
+        if max(map(max, OPT["merge"])):
+            tt(b("DD"), b("US"), b("IDF"), A.mult)
+            red(col(29), b("DD"), A.max)
+            ts(col(24), col(29), 16.0, A.mult)
+        npt = 16 * OPT["cd"]
+        ms(b("ON", S_[:, 0:npt]), 1.0)
+        ms(b("ON", S_[:, 0:npt:16]), 2.0 ** -8)
+        ms(b("ON", S_[:, 0:npt:256]), 0.0)
+        ms(b("OX", S_[:, 0:npt]), 0.0)
+        ms(b("OX", S_[:, 0:npt:256]), 2.0 ** 56)
+        scan(b("PT"), b("ON", S_[:, 0:npt]), b("OX", S_[:, 0:npt]), 0.0, A.mult, A.add)
+    for t in range(3):
+        for v in range(OPT["L"][t]):
+            ms(b("UA", S_[:, t, v::OPT["L"][t]]), 2.0 ** (8 * v))
     ts(b("C80", S_[:, 0, :]), b("C80", S_[:, 0, :]), col(1), A.add)
     for sl, o in ((S_[8:56], 8), (S_[0:8], BS_), (S_[56:80], BS_ - 768)):
         ms(b("C80", (S_[:], 1, sl)), float(UO_ - o))
@@ -310,216 +361,319 @@ def build():
     ms(b("C80", S_[:, 2, 64:72]), 271.0)
     ms(b("C80", S_[:, 2, 72:80]), 535.0)
     ms(b("CN", S_[:, :, 8:24]), 0.0)
-    for t in range(3):
+    Fn = lambda t: "F%d" % (t % 2)
+
+    def clear(t):
         for h in range(4):
-            iota(b("F%d" % t, S_[:, 354 * h:354 * h + 354]), [[0, 354]])
-        iota(b("F%d" % t, S_[:, BS_:BS_ + 512]), [[0, 512]])
+            iota(b(Fn(t), S_[:, 354 * h:354 * h + 354]), [[0, 354]])
+            ops[-1]["drain"] = t == 2
+    for t in range(2):
+        ms(b(Fn(t), S_[:, UO_ - 8:UO_]), 1.0 if plain else 2.0 ** 17)
+        clear(t)
     for Z in ("ZH", "ZL"):
         for z in range(6):
             iota(b(Z, S_[:, z // 3, 24 * (z % 3):24 * (z % 3) + 24, :]), [[0, 384]])
 
-    def ints(t):
+    packed = lambda t: max(OPT["merge"][t]) > 0
+
+    def gather(t, st):
+        nA = OPT["nA"][t]
+        nD, cd = 128 - nA, OPT["cd"]
+        for l0 in range(0, nD, cd):
+            n = min(cd, nD - l0)
+            o = 16 * (nD * st + l0)
+            tt(b("G", S_[:, o:o + 16 * n]), ind(b(Fn(t), S_[:, UO_ - 8:UO_ + 1280]), b("NU", S_[:, t, st, nA + l0:nA + l0 + n])), b("PT", S_[:, 0:16 * n]), A.mult)
+
+    def scans(o, a0, a1, n):
+        back = lambda x: S_[:, x + n - 1:x - 1:-1] if x else S_[:, n - 1::-1]
+        scan(b("ON", S_[:, o:o + n]), b("G", S_[:, a0:a0 + n]), b("G", S_[:, a1:a1 + n]), 1e29, A.min, A.min)
+        scan(b("OX", back(o)), b("G", back(a0)), b("G", back(a1)), 0.0, A.max, A.max)
+
+    def bounds(t, h):
+        nA = OPT["nA"][t]
+        nD = 128 - nA
+        if OPT["pair"][t]:
+            nA, nD, L = 0, 128, OPT["L"][t]
+            if h == 0:
+                copies(t)
+            for l0 in range(0, 128, 32):
+                for s in (0, 1):
+                    o = 2048 * s + 16 * l0
+                    aff(b("G", S_[:, o:o + 512]), ind(b(Fn(t), S_[:, UO_ - 8:]), b("NO", S_[:, t, h, 128 * s + l0:128 * s + l0 + 32])))
+                for l in range(l0, l0 + 32, L):
+                    scans(16 * l, 16 * l, 2048 + 16 * l, 16 * L)
+        if not nD:
+            return
+        for l0 in range(0, 0 if OPT["pair"][t] else nD, 16):
+            scans(16 * l0, 16 * (2 * h * nD + l0), 16 * ((2 * h + 1) * nD + l0), 256)
+        for O, k, acc, out, op in (("ON", 15, pb(5, 256, 256 + nD), "LO", A.min), ("OX", 0, pb(5, 384, 384 + nD), "HI", A.max)):
+            if h == 0:
+                aff(acc, b(O, S_[:, k:16 * nD:16]))
+            else:
+                tt(acc, acc, b(O, S_[:, k:16 * nD:16]), op)
+                tt(b(out, S_[:, nA:128]), acc, b("UA", S_[:, t, :]) if OPT["pair"][t] else b("US", S_[:, nA:128]), A.mult)
+
+    def copies(t):
+        for c0, c1 in ((136, 904), (0, 136), (904, 1288)):
+            for v in range(1, OPT["L"][t]):
+                o = CP_ + 1288 * (v - 1)
+                aff(b(Fn(t), S_[:, o + c0:o + c1]), b(Fn(t), S_[:, UO_ - 8 + c0:UO_ - 8 + c1]), 2.0 ** (-8 * v))
+
+    def copied(t):
+        nA, L_ = OPT["nA"][t], OPT["L"][t]
+        if not nA or OPT["pair"][t]:
+            return
+        g0, o0, n = 64 * (128 - nA), 16 * (128 - nA), 32 * L_
+        copies(t)
+        for l0 in range(0, nA, 16):
+            r = l0 % RG_
+            for s in (0, 1):
+                o = g0 + 32 * (RG_ * s + r)
+                aff(b("G", S_[:, o:o + 512]), ind(b(Fn(t), S_[:, UO_ - 8:]), b("NO", S_[:, t, s, 2 * l0:2 * l0 + 32])))
+            for l in range(0, 16, L_):
+                scans(o0 + 32 * (l0 % RO_ + l), g0 + 32 * (r + l), g0 + 32 * (RG_ + r + l), n)
+            if (l0 + 16) % RO_ == 0 or l0 + 16 == nA:
+                c, ua = S_[:, l0 - l0 % RO_:l0 + 16], b("UA", S_[:, t, l0 - l0 % RO_:l0 + 16])
+                e = o0 + 32 * (l0 % RO_ + 16)
+                tt(b("LO", c), b("ON", S_[:, o0 + 31:e:32]), ua, A.mult)
+                tt(b("HI", c), b("OX", S_[:, o0:e:32]), ua, A.mult)
+
+    def names(t, st):
+        cp(b("NU", S_[:, t, st, :]), ind(b("NM"), b("UF", S_[:, t, 8 * st:8 * st + 8])))
+        nA, L_ = OPT["nA"][t], OPT["L"][t]
+        for v in range(L_ if nA else 0):
+            sl = S_[128 * (st % 2) + v:128 * (st % 2) + 128:L_] if OPT["pair"][t] else S_[2 * v + st % 2:2 * nA:2 * L_]
+            ts(b("NO", (S_[:], t, st // 2, sl)), b("NU", S_[:, t, st, v:nA:L_]), float(CP_ - UO_ + 8 + 1288 * (v - 1) if v else 0), A.add)
+
+    def rows(t, c0, c1, bank, o):
+        mm([(b("P%d" % bank, S_[:, o:o + c1 - c0, i]), b("RB", S_[:, i, :]), b("VW", S_[:, t, c0:c1])) for i in range(16)], False)
+
+    def lanes(t):
         w = lambda k: b("W", S_[:, t, k, :])
         iw = lambda k: b("I", S_[:, t, k, :])
         uw = lambda k: b("U", S_[:, t, k, :])
-        par = t % 2
-        vr = b("VR", S_[:, par, :])
+        par = t
         s16 = (832 * t) % 1024 // 16
         v1 = lambda sl: b("V1", (S_[:], t, sl))
         for o, c0, n in ((0, s16, 64 - s16), (64 - s16, 0, s16)):
-            if n:
-                ts(b("SM", S_[:, o:o + n]), v1(S_[c0:c0 + n]), 8.0, A.is_lt)
-        ts(b("VW", S_[:, t, :]), v1(S_[:]), 1.0, A.max, 16.0, A.min)
+            if n and t:
+                tt(b("SM", S_[:, o:o + n]), p0(256 + c0, 256 + c0 + n), b("VE", S_[:, c0:c0 + n]), A.is_gt)
+            elif n:
+                ts(b("SM", S_[:, o:o + n]), v1(S_[c0:c0 + n]), -1.0, A.is_lt)
+        ts(b("VW", S_[:, t, :]), v1(S_[:]), -8.0, A.max, 7.0, A.min)
         scan(b("SP"), b("SM"), b("ZR"), 0.0, A.add, A.add)
-        mm([(b("P0", S_[:, 0:64]), b("BO"), b("SP"))])
-        mm([(b("P1", S_[:, 0:4, :]), b("BO"), b("SP")), (b("P1", S_[:, 0:4, :]), b("TB"), b("SM"))])
-        for bank in range(3):
-            nc = 32 if bank < 2 else 16
-            pb = "P%d" % (2 + bank)
-            mm([(b(pb, S_[:, 0:nc, i]), b("RB", S_[:, i, :]), b("VW", S_[:, t, 32 * bank:32 * bank + nc])) for i in range(16)], False)
-            aff(b("VR", S_[:, par, 8 + 512 * bank:8 + 512 * bank + 16 * nc]), b(pb, S_[:, 0:nc, :]))
+        mm([(p0(0, 64), b("BO"), b("SP"))])
+        mm([(pb(1, 448, 512), b("BO"), b("SP")), (pb(1, 448, 512), b("TB"), b("SM"))])
+        if not OPT["merge"][t][0]:
+            for c0, c1, bank in ((0, 32, 2), (32, 64, 3), (64, 80, 2)):
+                rows(t, c0, c1, bank, 0)
+                aff(b("VR", S_[:, par, 8 + 16 * c0:8 + 16 * c1]), pb(bank, 0, 16 * (c1 - c0)))
         rk = b("RK", S_[:, 0:64])
         for c in range(8):
-            o, a, bi, ac = b("LC", S_[:, c, :]), b("P0", S_[:, 0:64]), b("C8", S_[:, 1, c:c + 1]), b("W", S_[:, t, 0, c:c + 1])
-            add({"A": ([("sign", o, a, bi, ac)], 0.15)}, [a, bi], [o, ac])
-        cp(rk, b("P1", S_[:, 0:4, :]))
+            o, a, bi, ac = b("LC", S_[:, c, :]), p0(0, 64), b("C8", S_[:, 1, c:c + 1]), b("W", S_[:, t, 0, c:c + 1])
+            add({"A": ([("sign", o, a, bi, ac)], 0.075 + OPT["ova"])}, [a, bi], [o, ac])
+        cp(rk, pb(1, 448, 512))
         ts(uw(0), w(0), 0.5, A.mult, 32.0, A.add)
         tt(b("CM"), ind(b("RK"), uw(0)), b("IOT", S_[:, 0:128]), A.is_le)
-        ts(w(1), w(0), 8.0, A.mult, float(512 + 16 * s16), A.add)
-        has = b("FI", S_[:, 0:8])
-        ts(has, w(0), 64.0, A.is_lt)
-        mm([(b("P0", S_[:, 128:256]), b("BO"), b("CM"))])
-        tt(b("IM"), b("P0", S_[:, 128:256]), b("DM", S_[:, 0:128]), A.mult)
-        red(w(3), b("IM"), A.add)
-        tt(iw(0), w(3), w(1), A.add)
-        ts(iw(1), iw(0), 1023, A.bitwise_and)
-        ts(uw(1), iw(1), 8.0, A.add)
+        ts(b("IM", S_[:, :, 16]), w(0), 8.0, A.mult, float(520 + 16 * s16), A.add)
+        ts(b("IM", S_[:, :, 17]), w(0), 64.0, A.is_ge, -4096.0, A.mult)
+        if s16:
+            ts(b("IM", S_[:, :, 18]), w(0), 64.0 - 2 * s16, A.is_ge, -1024.0, A.mult)
+        ts(b("FL", S_[:, 0:8]), w(0), 64.0, A.is_lt)
+        mm([(p0(128, 256), b("BO"), b("CM"))])
+        tt(b("IM", S_[:, :, 0:16]), p0(128, 256), b("DM", S_[:, 0:128]), A.mult)
+        red(w(3), b("IM", S_[:, :, 0:19 if s16 else 18]), A.add)
+        cp(b("UF", S_[:, t, 0:8]), w(3))
+        ts(b("NG", S_[:, t, 0:8]), w(3), 0.0, A.max)
         ts(rk, rk, 128.0, A.is_le)
-        for h0, h1, p0 in ((0, 56, 24), (56, 64, 0)):
+        for h0, h1, q0 in ((0, 56, 24), (56, 64, 0)):
             for a0, a1 in ((h0, min(h1, max(s16, h0))), (max(h0, min(s16, h1)), h1)):
                 if a1 > a0:
                     r0 = (a0 - s16) % 64
-                    tt(b("CN", S_[:, t, p0 + a0 - h0:p0 + a1 - h0]), b("RK", S_[:, r0:r0 + a1 - a0]), b("SM", S_[:, r0:r0 + a1 - a0]), A.mult)
+                    tt(b("CN", S_[:, t, q0 + a0 - h0:q0 + a1 - h0]), b("RK", S_[:, r0:r0 + a1 - a0]), b("SM", S_[:, r0:r0 + a1 - a0]), A.mult)
         if t < 2:
             tt(b("VD"), b("VW", S_[:, t, :]), b("D2", S_[:, :, t]), A.add)
+            ts(b("VE"), b("VD", S_[:, 0:64]), 2.0, A.is_ge, 1000.0, A.mult)
+            tt(b("VE"), b("VE"), b("VD", S_[:, 0:64]), A.add)
+            ts(b("VE"), b("VE"), 1.0, A.add)
+
+    def pack(t):
+        for c0, c1, bank, o in ((8, 32, 5, 0), (32, 56, 7, 0), (0, 8, 4, 0), (56, 80, 4, 8)):
+            rows(t, c0, c1, bank, o)
+            src = b("FI", S_[:, t - 1, 8 + 16 * c0:8 + 16 * c1]) if t else b("UX", S_[:, 8 + 16 * c0:8 + 16 * c1])
+            v = pb(bank, 16 * o, 16 * (o + c1 - c0))
+            tt(b(Fn(t), S_[:, UO_ + 16 * c0:UO_ + 16 * c1]), src, v, A.add)
+            if OPT["merge"][t][0]:
+                aff(b("VR", S_[:, t, 8 + 16 * c0:8 + 16 * c1]), v)
+
+    def step(t, j):
+        w = lambda k: b("W", S_[:, t, k, :])
+        iw = lambda k: b("I", S_[:, t, k, :])
+        par = t
+        vr = b("VR", S_[:, par, :])
+        merged = OPT["merge"][t][j - 1]
         um = lambda j0, j1: b("UM", S_[:, t, 8 * j0:8 * j1])
         uf = lambda j0, j1: b("UF", S_[:, t, 8 * j0:8 * j1])
-        ng = lambda j: b("NG", S_[:, t, j::4])
-        ts(ng(0), iw(1), 8.0, A.add)
-        tt(w(4), ng(0), has, A.mult)
-        cp(um(0, 1), w(4))
-        go = has
-        for j in (1, 2, 3):
-            last = uw(j)
-            cp(b("NU"), ind(b("NM"), last))
+        ng = lambda j: b("NG", S_[:, t, 8 * j:8 * j + 8])
+        vm = lambda j0, j1: b("VM", S_[:, par, 128 * j0:128 * j1])
+        last = uf(j - 1, j)
+        names(t, j - 1)
+        vt, at, rest = pb(1, 0, 128), pb(6, 128, 256), pb(6, 256, 384)
+        if merged:
+            gather(t, j - 1)
+        else:
             for q in range(4):
-                aff(b("GV", S_[:, 512 * q:512 * q + 512]), ind(vr, b("NU", S_[:, 32 * q:32 * q + 32])))
-            aff(b("MR", S_[:, j - 1, :]), ind(b("IOT"), last))
-            aff(b("NC"), ind(b("NM"), last), 1.0, col(7))
-            for k in range(j):
-                tt(b("EQ", S_[:, k, :]), ind(b("NM"), last), b("MR", S_[:, k, :]), A.is_equal)
-            ts(b("A15"), ind(b("AL"), last), 32768.0, A.mult)
+                aff(b("GV", S_[:, 512 * q:512 * q + 512]), ind(vr, b("NU", S_[:, t, j - 1, 32 * q:32 * q + 32])), 16.0, col(25))
+        aff(b("MR", S_[:, j - 1, :]), ind(b("IOT"), last))
+        aff(b("NC"), ind(b("NM"), last), 1.0, col(7))
+        aff(b("AG"), ind(b("AL"), last))
+        for k in range(j):
+            tt(b("EQ", S_[:, k, :]), ind(b("NM"), last), b("MR", S_[:, k, :]), A.is_equal)
+        if j == 1:
+            aff(vm(0, 1), ind(vr, uf(0, 1)), 16.0, col(25))
+            prev = b("P6", S_[:, 24, 0:8])
+            mm([(prev, b("MR", S_[:, 0, :]), b("IDF", S_[:, 0::16]))])
+        else:
+            prev = iw(2 + j)
+        if j == 3:
+            aff(vm(1, 2), ind(vr, um(1, 2)), 16.0, col(25))
+            aff(b("VF"), ind(vr, last), 16.0, col(25))
+            mm([(p0(128, 256), b("IDB"), x) for x in (vm(0, 1), vm(1, 2), b("VF"))])
+            hot(b("EQ", S_[:, 3, :]), p0(128, 256), 30.0, col(26))
+        keys = [(rest, b("EQ", S_[:, k, :]), b("NEG")) for k in range(j + j // 3)] + [(rest, b("AG"), b("IDB"))] * merged + [(rest, b("NC"), b("IDF"))]
+        if OPT["sel"] and not merged:
             for h in (0, 1):
-                mm([(b("P0", S_[:, 64 * h:64 * h + 64]), b("AK", S_[:, 15 - k:143 - k]), b("GV", S_[:, 1024 * h + k:1024 * h + 1024:16])) for k in range(16)])
-            tt(b("PR"), b("P0", S_[:, 0:128]), b("A15"), A.mult)
-            keys = b("P1", S_[:, 8:16, :])
-            mm([(keys, b("EQ", S_[:, k, :]), b("NEG")) for k in range(j)] + [(keys, b("NC"), b("IDF")), (keys, b("PR"), b("IDF"))])
-            red(w(5), keys, A.max)
-            ts(iw(2), w(5), 0.0, A.max)
-            ts(iw(4), iw(2), 2047, A.bitwise_and)
-            tt(b("LH"), ind(iw(4), b("CG")), b("DM", S_[:, 0:128]), A.mult)
-            nw = b("P1", S_[:, 16, 0:8])
-            mm([(nw, b("LH"), b("RC"))])
-            if j < 3:
-                cp(uw(j + 1), nw)
-            tt(ng(j), nw, go, A.mult)
-            cp(um(j, j + 1), ng(j))
-            go = b("GO", S_[:, t, :, j])
-            ts(go, ng(j), 1.0, A.is_ge)
-
-            def volumes(j0, j1):
-                aff(b("VM", S_[:, par, 128 * j0:128 * j1]), ind(vr, um(j0, j1)))
-                mm([(b("P5", S_[:, 344 + 8 * j0:344 + 8 * j1]), b("AK", S_[:, 15 - k:143 - k]), b("VM", S_[:, par, 128 * j0 + k:128 * j1:16])) for k in range(16)])
-            if j == 2:
-                volumes(0, 3)
-                cp(w(8), b("P5", S_[:, 344:352]))
-                tt(w(8), b("P5", S_[:, 352:360]), w(8), A.add)
-                tt(w(8), b("P5", S_[:, 360:368]), w(8), A.add)
-                ts(w(6), w(8), 30.0, A.is_lt)
-                tt(w(6), w(6), go, A.mult)
-                go = w(6)
-            aff(b("XR"), ind(b("XT"), um(j, j + 1)))
-            aff(b("XA"), b("XR"), col(16), col(13))
-            mm([(b("P3"), b("XA"), b("HC", S_[:, 0:512])), (b("P4", S_[:, 0:24, :]), b("XA"), b("HC", S_[:, 512:896]))], False)
-            hot(b("HB", S_[:, 512:896]), b("P4", S_[:, 0:24, :]))
-            hot(b("HB", S_[:, 0:512]), b("P3"))
-            mm([(b("P5", S_[32 * (g // 2):32 * (g // 2) + 32, 80 * j:80 * j + 80]), b("HB", S_[:, 640 + 32 * g:672 + 32 * g]), b("HB", S_[:, 80 * g:80 * g + 80]))
-                for g in range(8)], 2)
-            ops[-1]["tile"] = 9
-            cn = b("CN", S_[:, t, :])
-            tt(cn, b("P5", S_[:, 80 * j:80 * j + 80]), cn, A.add)
-            if j == 3:
-                xchg([(1, b("CN", S_[:, t, 0:16]), b("LN", S_[:, t, 16:32])), (-1, b("CN", S_[:, t, 16:32]), b("LN", S_[:, t, 0:16]))], 30e3)
-            for h in (0, 1):
-                aff(b("XB", S_[:, h, :]), b("XR"), col(19 + h), col(21 + h))
-            e = 3 * par + j - 1
-            for x in (0, 1):
-                for y in (0, 1):
-                    rows = S_[64 * x + 32 * y:64 * x + 32 * y + 32]
-                    mm([(b("P%d" % (2 + y), S_[:, 2 * x + z::4, :]), b("XA", (rows, S_[:])), b("XB", (rows, z, S_[:]))) for z in (0, 1)], False)
-                    ops[-1]["tile"] = 1 + 2 * x + y
+                mm([(pb(1, 64 * h, 64 * h + 64), b("AK", S_[:, 15 - k:143 - k]), b("GV", S_[:, 1024 * h + k:1024 * h + 1024:16])) for k in range(16)])
+            tt(b("PB"), vt, b("AG"), A.mult)
+            mm(keys + [(rest, b("PB"), b("IDB"))])
+            red(w(5), rest, A.max)
+        else:
+            mm([(at, b("AG"), b("IDB"))])
+            mm(keys)
+            if merged:
+                mm([(b("P1", S_[:, 0:8, k]), b("G", S_[:, 2048 * (j - 1) + k:2048 * j:16]), b("IDF", S_[:, 0::16])) for k in range(16)], False)
+                ts(b("VI"), vt, col(24), A.mult, 8.0, A.add)
+                ts(b("VI"), b("VI"), 15, A.bitwise_and)
+                tt(b("PR"), b("VI"), at, A.mult)
+            else:
+                aff(b("AT"), at)
+                mm([(b("P1", S_[:, 0:8, k]), b("GV", S_[:, k::16]), b("IDB", S_[:, 0::16])) for k in range(16)], False)
+                tt(b("PR"), vt, b("AT"), A.mult)
+            tt(b("KY"), b("PR"), rest, A.add)
+            red(w(5), b("KY"), A.max)
+        tt(iw(2), w(5), prev, A.max)
+        ts(iw(3 + j), iw(2), 2047, A.bitwise_and)
+        tt(b("LH"), ind(iw(3 + j), b("CG")), b("DM", S_[:, 0:128]), A.mult)
+        nw = b("P1", S_[:, 25, 0:8])
+        mm([(nw, b("LH"), b("RC"))])
+        cp(uf(j, j + 1), nw)
+        go = b("GO", S_[:, t, :, j])
+        tt(go, nw, ng(0) if j == 1 else b("LW", S_[:, t, 8 * j - 8:8 * j]), A.not_equal)
+        tt(ng(j), nw, go, A.mult)
+        if j < 3:
+            aff(b("LW", S_[:, t, 8 * j:8 * j + 8]), nw)
+        cp(um(j, j + 1), ng(j))
+        aff(b("XR"), ind(b("XT"), um(j, j + 1)))
+        mm([(b("P2"), b("XR"), b("HC", S_[:, 0:512])), (pb(3, 0, 384), b("XR"), b("HC", S_[:, 512:896]))], False)
+        hot(b("HB", S_[:, 512:896]), pb(3, 0, 384), 12.0, col(31))
+        hot(b("HB", S_[:, 0:512]), b("P2"), 12.0, col(31))
+        mm([(b("P0", S_[32 * (g // 2):32 * (g // 2) + 32, 0:80]), b("HB", S_[:, 640 + 32 * g:672 + 32 * g]), b("HB", S_[:, 80 * g:80 * g + 80]))
+            for g in range(8)], 2)
+        ops[-1]["tile"] = 9
+        cn = b("CN", S_[:, t, :])
+        tt(cn, p0(0, 80), cn, A.add)
+        if j == 3:
+            xchg([(1, b("CN", S_[:, t, 0:16]), b("LN", S_[:, t, 16:32])), (-1, b("CN", S_[:, t, 16:32]), b("LN", S_[:, t, 0:16]))], 30e3)
+        aff(b("XB"), b("XR"), col(3))
+        e = 3 * par + j - 1
+        for x in (0, 1):
             for y in (0, 1):
-                hot(b("EB", S_[:, e, :, :, y, :, :]), b("P%d" % (2 + y)))
-            mm([(b("P5", S_[:, 312 + 8 * j + c:313 + 8 * j + c]), b("EB", S_[:, e, c]), b("CB", S_[:, 0:1])) for c in range(8)], False)
-        tt(b("FI", S_[:, 8:32]), b("P5", S_[:, 320:344]), b("TH"), A.is_lt)
-        cp(b("TG"), um(0, 4))
-        tt(b("TG"), b("TG"), b("DU"), A.subtract)
-        tt(b("TG"), b("TG"), b("FI"), A.mult)
+                r0 = 64 * x + 32 * y
+                mm([(b("P%d" % (2 + y), S_[:, 2 * x + z::4, :]), b("XR", S_[r0:r0 + 16 + 16 * z, :]), b("XB" if z else "XR", S_[r0:r0 + 16 + 16 * z, :])) for z in (0, 1)], False)
+                ops[-1]["tile"] = 1 + 2 * x + y
+        for y in (0, 1):
+            hot(b("EB", S_[:, e, :, :, y, :, :]), b("P%d" % (2 + y)), 12.0, col(31))
+        mm([(p0(328 + 8 * j + c, 329 + 8 * j + c), b("EB", S_[:, e, c]), b("CB", S_[:, 0:1])) for c in range(8)], False)
+
+    def counts(t):
+        w = lambda k: b("W", S_[:, t, k, :])
+        uw = lambda k: b("U", S_[:, t, k, :])
+        par = t
+        names(t, 3)
+        tt(b("FL", S_[:, 8:32]), p0(336, 360), b("TH"), A.is_lt)
+        tt(b("TG"), b("NG", S_[:, t, :]), b("DU"), A.subtract)
+        tt(b("TG"), b("TG"), b("FL"), A.mult)
         tt(b("TG"), b("TG"), b("DU"), A.add)
         cp(b("UT", S_[:, t, :]), b("TG"))
-        ts(b("OM"), b("GO", S_[:, t]), -1.0, A.mult, 1.0, A.add)
-        scan(b("FX"), b("OM"), b("NG", S_[:, t, :]), 0.0, A.mult, A.add)
-        for j in range(4):
-            cp(uf(j, j + 1), b("FX", S_[:, j::4]))
-            tt(b("NF", S_[:, j // 2, j % 2::2]), ind(b("NM"), uf(j, j + 1)), b("LT"), A.add)
-        for s in (0, 1):
-            cp(b("NO", S_[:, par, s, :]), b("NF", S_[:, s, :]))
-        volumes(3, 4)
-        tt(w(9), b("P5", S_[:, 368:376]), w(8), A.add)
-        ts(uw(12), w(9), 7.0, A.add)
+        vm = lambda j0, j1: b("VM", S_[:, par, 128 * j0:128 * j1])
+        aff(vm(2, 4), ind(b("VR", S_[:, par, :]), b("UM", S_[:, t, 16:32])), 16.0, col(25))
+        mm([(p0(128, 256), b("IDB"), vm(k, k + 1)) for k in range(4)])
+        aff(b("ZS"), p0(128, 256))
+        mm([(p0(360, 368), b("AK", S_[:, 15 - k:143 - k]), b("ZS", S_[:, k::16])) for k in range(16)])
+        ts(uw(2), p0(360, 368), 7.0, A.add)
         red(w(7), b("GO", S_[:, t, :, 1:4]), A.add)
-        cp(uw(13), w(7))
-        tt(b("NP", S_[:, 0:32]), b("CN", S_[:, t, 0:32]), b("LN", S_[:, t, :]), A.add)
+        cp(uw(3), w(7))
+        def whole(o, M):
+            mm([(p0(o + 8, o + 56), b(M), b("CN", S_[:, t, 32:80]))])
+            mm([(p0(o + h0, o + h0 + 8), b(M), b(X, S_[:, t, q0:q0 + 8])) for q0, h0, n in PERM for X in ("CN", "LN")], 2)
         if t < 2:
-            ts(b("HM", S_[:, 32:80]), b("CN", S_[:, t, 32:80]), 3.0, A.min)
-            ts(b("HM", S_[:, 0:32]), b("NP", S_[:, 0:32]), 3.0, A.min)
-            mm([(b("P0", S_[:, 256 + h0:256 + h0 + n]), b("SH"), b("HM", S_[:, p0:p0 + n])) for p0, h0, n in PERM], False)
-            tt(b("V1", S_[:, t + 1, :]), b("VD"), b("P0", S_[:, 256:336]), A.subtract)
-        cp(b("NP", S_[:, 32:80]), b("CN", S_[:, t, 32:80]))
-        mm([(b("P5", S_[:, 416 + h0:416 + h0 + n]), b("IDB"), b("NP", S_[:, p0:p0 + n])) for p0, h0, n in PERM], False)
+            whole(256, "SH")
+            ts(b("HM"), p0(256, 336), 3.0, A.min)
+            tt(b("V1", S_[:, t + 1, :]), b("VD"), b("HM"), A.subtract)
+        whole(368, "IDB")
         n1 = lambda k: b("N1", S_[:, k, :])
-        tt(n1(0), b("P5", S_[:, 416:496]), b("C80", S_[:, 2, :]), A.add)
-        ts(n1(1), b("P5", S_[:, 416:496]), 0.0, A.is_equal)
+        tt(n1(0), p0(368, 448), b("C80", S_[:, 2, :]), A.add)
+        ts(n1(1), p0(368, 448), 0.0, A.is_equal)
         cp(b("UW", S_[:, par, :]), n1(0))
         tt(n1(1), n1(1), b("C80", S_[:, 1, :]), A.mult)
         tt(n1(1), n1(1), b("C80", S_[:, 0, :]), A.add)
         cp(b("UO", S_[:, par, :]), n1(1))
 
     def floats(t):
-        par = t % 2
-        for c0, c1 in ((8, 32), (32, 56), (0, 8), (56, 80 if t < 2 else 64)):
-            aff(b("WN", S_[:, 16 * c0:16 * c1]), ind(b("WT"), b("UW", S_[:, par, c0:c1])))
-        Ft = "F%d" % t
+        par = t
+        Ft = Fn(t)
         uw = lambda k: b("U", S_[:, t, k, :])
-        u = b(Ft, S_[:, UO_ - 8:UO_ + 1280])
+        pk = b(Ft, S_[:, UO_ - 8:UO_ + 1280])
         ut = lambda j: b("UT", S_[:, t, 8 * j:8 * j + 8])
-        S = b(Ft, S_[:, 0:UO_])
-        for c0, c1 in ((136, 904), (0, 136), (904, 1288)) if t else ((0, 1288),):
-            for v in range(1, LV):
-                o = 3208 + 1288 * (v - 1)
-                aff(b(Ft, S_[:, o + c0:o + c1]), b(Ft, S_[:, UO_ - 8 + c0:UO_ - 8 + c1]), 2.0 ** (-8 * v))
-        n = 32 * LV
-        for q in range(8):
-            for s in (0, 1):
-                aff(b("G", S_[:, s, 512 * (q % GR):512 * (q % GR) + 512]), ind(b(Ft, S_[:, UO_ - 8:]), b("NO", S_[:, par, s, 32 * q:32 * q + 32])))
-            for o in range(512 * q, 512 * q + 512, n):
-                back = lambda x: S_[x + n - 1:x - 1:-1] if x else S_[n - 1::-1]
-                r, o = o % 2048, o % (512 * GR)
-                scan(b("ON", S_[:, r:r + n]), b("G", S_[:, 0, o:o + n]), b("G", S_[:, 1, o:o + n]), 1e29, A.min, A.min)
-                scan(b("OX", (S_[:], back(r))), b("G", (S_[:], 0, back(o))), b("G", (S_[:], 1, back(o))), 0.0, A.max, A.max)
-            if q % 4 == 3:
-                half = S_[:, 16 * q - 48:16 * q + 16]
-                tt(b("LO", half), b("ON", S_[:, 31::32]), b("US", half), A.mult)
-                tt(b("HI", half), b("OX", S_[:, 0::32]), b("US", half), A.mult)
-        tt(b("UV"), ind(u, b("UF", S_[:, t, :])), b("VM", S_[:, par, :]), A.mult)
-        aff(b("U0"), ind(u, b("UF", S_[:, t, 0:8])))
-        tt(b("DD"), ind(u, b("UF", S_[:, t, 24:32])), b("U0"), A.subtract)
-        mm([(b("P7", S_[:, 256:384]), b("IDF"), b("UV", S_[:, 128 * j:128 * j + 128])) for j in range(4)])
-        aff(b("S1"), b("P7", S_[:, 256:384]))
-        tt(b("MM"), ind(b("WT", S_[:, 0:264]), uw(12)), b("S1"), A.mult)
+        S = b(Ft, S_[:, 0:UO_ - 8])
+        gather(t, 3)
+        bounds(t, 1)
+        copied(t)
+        for c0, c1 in ((8, 32), (32, 56), (0, 8), (56, 80 if t < 2 else 64)):
+            aff(b("WN", S_[:, 16 * c0:16 * c1]), ind(b("WT"), b("UW", S_[:, par, c0:c1])), 1.0 if plain else (1.0, 0.5, 2.0 ** -16)[t])
+        tt(b("UV"), ind(b("FI", S_[:, t - 1, :]) if t and packed(t) else pk, b("UF", S_[:, t, :])), b("VM", S_[:, t, :]), A.mult)
+        aff(b("U0"), ind(pk, b("UF", S_[:, t, 0:8])))
+        tt(b("DD"), ind(pk, b("UF", S_[:, t, 24:32])), b("U0"), A.subtract)
+        mm([(pb(7, 256, 384), b("IDF"), b("UV", S_[:, 128 * j:128 * j + 128])) for j in range(4)])
+        aff(b("S1"), pb(7, 256, 384))
+        tt(b("MM"), ind(b("WT", S_[:, 0:264]), uw(2)), b("S1"), A.mult)
         aff(b("D8"), b("DD"), 0.125)
-        aff(b("U0"), b("DD"), 0.0625)
-        tt(b("TE"), ind(b("IOT"), uw(13)), b("U0"), A.mult)
-        p6 = lambda j: b("P6", S_[:, 128 * j:128 * j + 128])
-        tt(p6(0), b("MM"), b("TE"), A.subtract)
-        for j in (1, 2, 3):
-            tt(p6(j), p6(j - 1), b("D8"), A.add)
+        tt(b("TE"), ind(b("EH"), uw(3)), b("D8"), A.mult)
+        EP = 4
+        p6 = lambda j: pb(EP, 128 * j, 128 * j + 128)
+        if OPT["pe_est"]:
+            for j in (1, 2, 3, 0):
+                mm([(p6(j), b("IDF"), b("MM")), (p6(j), b("IDF"), b("TE"))] + [(p6(j), b("IDF") if j == 1 else b("IDJ", S_[:, j - 2, :]), b("D8"))] * min(j, 1))
+        else:
+            tt(p6(0), b("MM"), b("TE"), A.add)
+            for j in (1, 2, 3):
+                tt(p6(j), p6(j - 1), b("D8"), A.add)
         for j in (1, 2, 3, 0):
             tt(p6(j), p6(j), b("LO"), A.max)
             tt(b("ES", S_[:, 128 * j:128 * j + 128]), p6(j), b("HI"), A.min)
-        cp(ind(S, ut(0)), b("ES", S_[:, 0:128]))
+        scatter(ind(S, ut(0)), b("ES", S_[:, 0:128]))
         for j in (1, 2, 3):
-            pb = "P7" if j % 2 else "P6"
+            bk = 7 if j % 2 else 5
             z = j % 2
-            add({"P": ([("ptr", b(pb, S_[:, 0:128]), b("ES", S_[:, 128 * j:128 * j + 128]), b("IDF"))], 0.05 + 512 * 0.7 * CY)},
-                [b("ES", S_[:, 128 * j:128 * j + 128]), b("IDF")], [b(pb, S_[:, 0:128])])
-            aff(b("ZH", S_[:, z, 0::9, :]), b(pb, S_[:, 0:128]))
-            tt(b("ZL", S_[:, z, 0::9, :]), b(pb, S_[:, 0:128]), b("ZH", S_[:, z, 0::9, :]), A.subtract)
+            add({"P": ([("ptr", pb(bk, 0, 128), b("ES", S_[:, 128 * j:128 * j + 128]), b("IDF"))], 512 * PE_ * CY)},
+                [b("ES", S_[:, 128 * j:128 * j + 128]), b("IDF")], [pb(bk, 0, 128)], lat=0.05)
+            aff(b("ZH", S_[:, z, 0::9, :]), pb(bk, 0, 128))
+            tt(b("ZL", S_[:, z, 0::9, :]), pb(bk, 0, 128), b("ZH", S_[:, z, 0::9, :]), A.subtract)
             e = 3 * par + j - 1
-            mm([(b(pb, S_[:, 128:256]), b(Z, S_[:, z, 8 * g:8 * g + 8, :]), b("EB", S_[:, e, :, g // 4, g // 2 % 2, g % 2, :])) for Z in ("ZH", "ZL") for g in range(8)])
-            aff(b("CC", S_[:, j - 1, :]), b(pb, S_[:, 128:256]))
+            mm([(pb(bk, 128, 256), b(Z, S_[:, z, 8 * g:8 * g + 8, :]), b("EB", S_[:, e, :, g // 4, g // 2 % 2, g % 2, :])) for Z in ("ZH", "ZL") for g in range(8)])
+            aff(b("CC", S_[:, j - 1, :]), pb(bk, 128, 256))
             tt(b("GA"), ind(S, b("UM", S_[:, t, 8 * j:8 * j + 8])), b("CC", S_[:, j - 1, :]), A.add)
-            cp(ind(S, ut(j)), b("GA"))
+            scatter(ind(S, ut(j)), b("GA"))
         lf = lambda k: b("LF", S_[:, t, 128 * k:128 * k + 128])
         parts = [(1, b(Ft, S_[:, 1160:1288]), lf(0)), (-1, b(Ft, S_[:, 1032:1160]), lf(1))]
         if t < 2:
@@ -528,7 +682,12 @@ def build():
         top = 80 if t < 2 else 64
 
         def new(c0, c1, end):
-            o = b("F%d" % (t + 1), S_[:, UO_ + 16 * c0:UO_ + 16 * c1]) if t < 2 else b("F0", S_[:, UO_ + 16 * c0:UO_ + 16 * c1])
+            if t == 2:
+                o = b("UX", S_[:, 16 * c0:16 * c1])
+            elif packed(t + 1):
+                o = b("FI", S_[:, t, 8 + 16 * c0:8 + 16 * c1])
+            else:
+                o = b(Fn(t + 1), S_[:, UO_ + 16 * c0:UO_ + 16 * c1])
             tt(o, ind(b(Ft, S_[:, 0:end]), b("UO", S_[:, par, c0:c1])), b("WN", S_[:, 16 * c0:16 * c1]), A.mult)
             if t == 2:
                 dma("S" if c0 else "A", b("y", S_[:, 16 * c0:16 * c1]), o, 8192 * (c1 - c0))
@@ -538,8 +697,29 @@ def build():
         tt(b(Ft, S_[:, BS_ + 128:BS_ + 16 * top - 768]), b(Ft, S_[:, 904:8 + 16 * top]), b("LF", S_[:, t, 128:16 * top - 768]), A.add)
         new(56, top, BS_ + 16 * top - 768)
         new(0, 8, BS_ + 128)
+        if t == 0:
+            clear(2)
 
-    ints(0); ints(1); floats(0); ints(2); floats(1); floats(2)
+    def early(t):
+        for j in (1, 2, 3):
+            if not OPT["merge"][t][j - 1]:
+                gather(t, j - 1)
+            if j == 2:
+                bounds(t, 0)
+    todo = []
+    for t in range(3):
+        lanes(t)
+        if packed(t):
+            while todo:
+                u = todo.pop(0)
+                early(u); floats(u)
+            pack(t)
+        for j in (1, 2, 3):
+            step(t, j)
+        counts(t)
+        todo.append(t)
+    for u in todo:
+        early(u); floats(u)
     return ops
 
 
@@ -568,81 +748,117 @@ def schedule(ops):
     for k, o in enumerate(ops):
         for j in o["dep"]:
             succ[j].append(k)
-    SY = 0.08
-    pr = [0.0] * n
-    for k in range(n - 1, -1, -1):
-        o = ops[k]
-        c = min(v[1] for v in o["var"].values()) + (2.0 + o["lat"] / 200e3 if "dma" in o else o["lat"])
-        pr[k] = c + max([pr[s] + SY for s in succ[k]], default=0.0)
-    bias = [0.0] * n
-    for kind, lo, hi, amt in PAR["moves"]:
-        for k in range(lo, min(hi, n)):
-            if kind:
-                bias[k] += amt
+    SY = PAR["sy"]
+    pred = [sorted(o["dep"]) for o in ops]
+
+    def rank(xs, t):
+        lo, hi = 0, len(xs)
+        while lo < hi:
+            mid = (lo + hi) // 2
+            if xs[mid] <= t:
+                lo = mid + 1
             else:
-                pr[k] += amt
-    for k, o in enumerate(ops):
-        if "dma" in o and not o["dep"]:
-            pr[k] = 1e4 - k
-    free = {q: 0.0 for q in "DAPGS"}
-    bank = {}
-    dmafree = [0.0]
-    done = [None] * n
-    order = {q: [] for q in "DAPGS"}
-    left = [len(o["dep"]) for o in ops]
-    ready = [k for k in range(n) if left[k] == 0]
-    seq = []
-    firstx = [1.5]
-    while ready:
-        cand = []
-        for k in ready:
+                hi = mid
+        return lo
+
+    def gap(lists, t, c, me):
+        moved = True
+        while moved:
+            moved = False
+            for st, en, who in lists:
+                i = rank(en, t - SY + 1e-9)
+                while i < len(st) and st[i] < t + c + SY:
+                    pad = 0.0 if who is None or who[i] == me else SY
+                    if st[i] < t + c + pad and en[i] + pad > t + 1e-9:
+                        t = en[i] + pad
+                        moved = True
+                    i += 1
+        return t
+
+    def place(key, before, after, back, fixed):
+        busy = {x: ([], [], []) for x in list("DAPGS") + ["P%d" % k for k in range(8)]}
+        left = [len(x) for x in before]
+        rt = [0.0] * n
+        start, queue = [0.0] * n, [None] * n
+        ready = sorted((key[k], k) for k in range(n) if left[k] == 0)
+        while ready:
+            k = min(ready)[1]
+            ready.remove((key[k], k))
             o = ops[k]
-            rt = max([done[j] + SY for j in o["dep"]], default=0.0)
-            v = {}
+            best = None
             for q, (calls, c) in o["var"].items():
-                v[q] = (max(rt, free[q], max([bank[x][0] + (SY if bank[x][1] != q else 0) for x in o["banks"] if x in bank], default=0.0)), k, q, c)
-            if len(v) == 2 and v["A"][0] <= v["D"][0] + PAR["m0"] + bias[k]:
-                del v["D"]
-            cand += v.values()
-        t0 = min(c[0] for c in cand)
-        q0 = min(cand)[2]
-        pick = min(cand)
-        same = [c for c in cand if c[2] == q0]
-        same.sort(key=lambda c: -pr[c[1]] + (PAR["m1"] if q0 == "D" and len(ops[c[1]]["var"]) == 2 else 0.0))
-        for c in same:
-            if c[0] <= t0 + PAR["e0"]:
-                pick = c
-                break
-        for c in same:
-            if pr[c[1]] > pr[pick[1]] + PAR["p1"] and c[0] < pick[0] + PAR["f1"] * pick[3] and c[0] - pick[0] < PAR["e1"]:
-                pick = c
-                break
-        st, k, q, c = pick
+                if fixed and q != fixed[k]:
+                    continue
+                me = (q, o.get("tile"))
+                t = gap([busy[q][:2] + (None,)] + [busy[x] for x in o["banks"]], rt[k] + (o["lat"] if back else 0.0), c, me)
+                v = t + c + (PAR["m0"] + PAR["m1"] * c if q == "D" else 0.0)
+                if q == "A" and t + c < due[k]:
+                    v = -1.0
+                if best is None or v < best[0]:
+                    best = (v, t, q, c)
+            v, t, q, c = best
+            start[k], queue[k] = t, q
+            for x in [q] + list(o["banks"]):
+                i = rank(busy[x][0], t)
+                busy[x][0].insert(i, t); busy[x][1].insert(i, t + c); busy[x][2].insert(i, (q, o.get("tile")))
+            for s in after[k]:
+                left[s] -= 1
+                rt[s] = max(rt[s], t + c + SY + (0.0 if back else o["lat"]))
+                if left[s] == 0:
+                    ready.append((key[s], s))
+        end = [start[k] + ops[k]["var"][queue[k]][1] + (0.0 if back else ops[k]["lat"]) for k in range(n)]
+        return start, queue, end
+
+    key, due = [0.0] * n, [0.0] * n
+    rng = np.random.default_rng(1)
+    for k in range(n - 1, -1, -1):
+        key[k] = min([key[s] - SY for s in succ[k]], default=0.0) - min(v[1] for v in ops[k]["var"].values()) - ops[k]["lat"]
+    best = None
+    for it in range(PAR["passes"]):
+        key = [k - 1e4 if ops[k].get("load") else key[k] for k in range(n)]
+        start, queue, end = place(key, pred, succ, False, None)
+        if best is None or max(end) < best[0]:
+            best = (max(end), start, queue, end)
+        elif max(end) > best[0] + PAR["back"]:
+            start, queue, end = best[1:]
+        s2, q2, e2 = place([-e for e in end], succ, pred, True, queue)
+        key = [-e + PAR["jit"] * x for e, x in zip(e2, rng.standard_normal(n).tolist())]
+        for k in range(n):
+            due[k] = max(e2) - s2[k] - PAR["due"]
+    both = [k for k in range(n) if len(ops[k]["var"]) == 2]
+    cur = best
+    for it in range(PAR["polish"]):
+        t0 = rng.random() * cur[0]
+        w = PAR["win"] * (0.3 + rng.random())
+        x = rng.standard_normal(n).tolist()
+        back = it % 2
+        base = [-e for e in cur[3]] if back else cur[1]
+        key = [base[k] + (PAR["jit2"] * x[k] if t0 <= cur[1][k] < t0 + w else 0.0) for k in range(n)]
+        fixed = list(cur[2])
+        for k in both:
+            if t0 <= cur[1][k] < t0 + w and rng.random() < PAR["flip"] * (PAR["toA"] if fixed[k] == "D" else 1.0):
+                fixed[k] = "A" if fixed[k] == "D" else "D"
+        if back:
+            s2, q2, e2 = place(key, succ, pred, True, fixed)
+            key = [-e for e in e2]
+        key = [k - 1e4 if ops[k].get("load") else key[k] for k in range(n)]
+        start, queue, end = place(key, pred, succ, False, fixed)
+        if max(end) <= cur[0] + PAR["tol"]:
+            cur = (max(end), start, queue, end)
+            if cur[0] < best[0]:
+                best = cur
+    done, start, queue, end = best
+    seq = sorted(range(n), key=lambda k: (start[k], k))
+    bank = {}
+    for k in seq:
         o = ops[k]
-        o["q"], o["st"] = q, st
-        free[q] = st + c
-        end = st + c
-        if "dma" in o:
-            dmafree[0] = max(dmafree[0], st + 1.6) + o["lat"] / 250e3
-            end = dmafree[0] + 0.4
-        elif "x" in o:
-            end += o["lat"] + firstx[0]
-            free[q] += firstx[0]
-            firstx[0] = 0.0
-        done[k] = end
+        o["q"], o["st"] = queue[k], start[k]
         prev = set()
         for x in o["banks"]:
-            if x in bank and (bank[x][1] != q or ops[bank[x][2]].get("tile") != o.get("tile")):
-                prev.add(bank[x][2])
-            bank[x] = (end, q, k)
+            if x in bank and (ops[bank[x]]["q"] != o["q"] or ops[bank[x]].get("tile") != o.get("tile")):
+                prev.add(bank[x])
+            bank[x] = k
         o["dep2"] = o["dep"] | prev
-        order[q].append(k)
-        seq.append(k)
-        ready.remove(k)
-        for s in succ[k]:
-            left[s] -= 1
-            if left[s] == 0:
-                ready.append(s)
     cnt = {q: 0 for q in "DAPG"}
     know = {q: {} for q in "DAPGS"}
     for k in seq:
@@ -657,7 +873,7 @@ def schedule(ops):
                     know[q][s2] = max(know[q].get(s2, 0), v2)
                 know[q][sem] = val
         o["waits"] = waits
-        o["know"] = dict(know[q])
+        o["know"] = {} if "x" in o else dict(know[q])
         if "dma" in o:
             o["sig"] = (o["dma"], 16)
         elif "x" in o:
@@ -665,12 +881,11 @@ def schedule(ops):
         else:
             cnt[q] += 1
             o["sig"] = ("e" + q, cnt[q])
-    return seq, cnt, max(done)
+    return seq, cnt, done
 
 
 PLAN = {}
-PAR = dict(m0=0.7, m1=10.0, e0=0.02, p1=1.0, f1=0.3, e1=0.6,
-           moves=[(1, 798, 878, -0.5), (1, 421, 621, 3.0), (1, 1110, 1120, 1.0), (0, 1239, 1242, -1.5), (1, 382, 385, -0.5), (0, 171, 201, -1.5)])
+PAR = dict(m0=0.4, m1=0.5, sy=0.21, passes=30, jit=0.25, due=0.0, back=1.5, polish=1100, win=5.0, jit2=1.0, flip=0.1, toA=4.0, tol=0.05)
 
 
 def plan():
@@ -696,12 +911,15 @@ def rank_program(g, core, T, topo):
             return ap(a[1]).indirect(ap(a[2]))
         return T[a[0]][a[1]]
 
-    sent = 0
+    sent = drained = 0
     for k in P["seq"]:
         o = P["ops"][k]
         q = Q[o["q"]]
         for sem, val in o["waits"].items():
             q.wait_ge(T.sem[sem], val)
+        if o.get("drain") and sent > drained:
+            g.wait_ge(T.sem.sent, sent)
+            drained = sent
         last = None
         for c in o["var"][o["q"]][0]:
             kind, a = c[0], [ap(x) for x in c[1:]]
@@ -722,7 +940,12 @@ def rank_program(g, core, T, topo):
             elif kind == "matmul":
                 last = q.matmul(*a)
             elif kind == "act":
-                last = q.activation(a[0], a[1], a[2], scale=a[4]) if a[3] is None else q.activation(a[0], a[1], a[2], bias=a[3], scale=a[4])
+                if a[4] is None:
+                    last = q.activation(a[0], a[1], a[2])
+                elif a[3] is None:
+                    last = q.activation(a[0], a[1], a[2], scale=a[4])
+                else:
+                    last = q.activation(a[0], a[1], a[2], bias=a[3], scale=a[4])
             elif kind == "sign":
                 last = q.activation(a[0], a[1], F.Sign, bias=a[2], scale=-1.0, accum_out=a[3])
             elif kind == "iota":
@@ -730,6 +953,8 @@ def rank_program(g, core, T, topo):
                     last = q.iota(*a)
                 else:
                     last = q.iota(*a, allow_small_or_imprecise_dtypes=True)
+            elif kind == "affine_select":
+                last = q.affine_select(*a)
             elif kind == "dma":
                 q.dma_start(a[0], a[1]).then_inc(T.sem[c[3]], 16)
             elif kind == "remote":

import numpy as np
from concourse.bass import DstId, RemoteDMATransfer
from concourse.mybir import AluOpType as A, AxisListType as AX, ActivationFunctionType as F

S_ = np.s_
f32, bf, i32, u16 = "float32", "bfloat16", "int32", "uint16"
OPT = dict(rbg=1, L=(4, 2, 2), pair=(1, 0, 0), nA=(128, 128, 128), merge=((0, 0, 0), (0, 0, 0), (0, 0, 0)), pe_est=1, silu=0, sel=0, cd=32, rg=64, ro=64, ov=0.0, ova=0.04, pe=0.55)
L_ = OPT["L"]
UO_, BS_, CP_ = 1424, 2704, 3216
FW = lambda L: CP_ + 1288 * (L - 1)
RG_, RO_ = OPT["rg"], OPT["ro"]
NG_ = max(64 * (128 - n + min(n, RG_)) for n in OPT["nA"])
NO_ = max(16 * (128 - n) + 32 * min(n, RO_) for n in OPT["nA"])
ALLA = min(OPT["nA"]) == 128
SB = {
    "Lin": ([4, 64], i32), "Ls": ([3, 64], f32), "Ld": ([12, 2, 16], f32), "Lt": ([3, 4, 2, 16], f32),
    "V1": ([3, 80], bf), "D2": ([80, 2], bf), "VW": ([3, 80], bf), "VD": ([80], bf), "VR": ([3, 1296], bf),
    "NT": ([1280], i32), "AI": ([1280], i32), "NM": ([1288], f32), "AL": ([1296], bf),
    "UX": ([1288], f32), "FI": ([2, 1288 if max(OPT["merge"][1] + OPT["merge"][2]) else 8], i32),
    "F0": ([FW(max(L_[0], L_[2]))], f32), "F1": ([FW(L_[1])], f32), "LF": ([3, 512], f32), "PT": ([8 if ALLA else 16 * OPT["cd"]], f32), "UA": ([3, 128], f32), "NO": ([3, 2, 256], u16),
    "WT": ([792], f32), "IOT": ([1296], f32), "XT": ([1296], bf), "RC": ([8], f32), "DU": ([32], f32), "CG": ([8], u16),
    "GO": ([3, 8, 4], f32), "NG": ([3, 32], f32), "LW": ([3, 32], f32), "FL": ([32], f32), "TG": ([32], f32),
    "UT": ([3, 32], u16), "LH": ([128], f32), "XR": ([128], bf), "EH": ([8], f32),
    "RG": ([128], f32), "RI": ([128], f32), "DM": ([128], f32), "DS": ([16], f32), "BO": ([128], bf), "TB": ([128], bf), "SH": ([128], bf),
    "IDB": ([128], bf), "IDF": ([128], f32), "IDJ": ([2, 128], f32), "NEG": ([128], bf), "AK": ([144], bf), "RB": ([16, 128], bf),
    "CO": ([40], f32), "CB": ([2], bf), "CI": ([32], i32), "CR": ([8, 16], f32), "C8": ([6, 8], f32), "TH": ([24], f32),
    "T1": ([128], f32), "T2": ([128], f32), "T3": ([8, 16], f32), "TI": ([96], i32), "XH": ([96], f32), "XL": ([16], f32),
    "HA": ([96], f32), "HC": ([896], bf), "US": ([128], f32), "C80": ([3, 80], f32),
    "SM": ([64], bf), "SP": ([64], bf), "ZR": ([64], f32), "LC": ([8, 64], bf), "RK": ([72], f32), "CM": ([128], bf), "IM": ([8, 19], f32), "VE": ([64], f32), "VF": ([128], bf),
    "W": ([3, 12, 8], f32), "I": ([3, 12, 8], i32), "U": ([3, 8, 8], u16), "UF": ([3, 32], u16), "UM": ([3, 32], u16),
    "NU": ([3, 4, 128], u16), "GV": ([2048], bf), "AG": ([128], bf), "AT": ([128], f32), "MR": ([3, 128], f32), "EQ": ([4, 128], bf), "NC": ([128], f32),
    "VI": ([128], i32), "PR": ([128], f32), "KY": ([8, 16], f32), "VM": ([3, 512], bf), "ZS": ([128], bf),
    "XB": ([128], bf), "HB": ([896], bf), "EB": ([9, 8, 2, 2, 2, 16], bf),
    "CN": ([3, 80], bf), "LN": ([3, 32], bf), "NP": ([80], bf), "HM": ([80], bf),
    "N1": ([3, 80], f32), "UW": ([3, 80], u16), "UO": ([3, 80], u16), "WN": ([1280], f32),
    "G": ([NG_], f32), "ON": ([NO_], f32), "OX": ([NO_], f32), "PB": ([128], bf), "LO": ([128], f32), "HI": ([128], f32),
    "UV": ([512], f32), "U0": ([128], f32), "DD": ([128], f32), "D8": ([128], f32), "S1": ([128], f32),
    "MM": ([128], f32), "TE": ([128], f32), "ES": ([512], f32), "ZH": ([2, 72, 16], bf), "ZL": ([2, 72, 16], bf),
    "CC": ([3, 128], f32), "GA": ([128], f32),
}
SCRATCH = {k: ("sbuf", [128] + v[0], v[1]) for k, v in SB.items()}
for _b in range(8):
    SCRATCH["P%d" % _b] = ("psum", [128, 512] if _b == 0 else [128, 32, 16], f32)
NDMA = 14
SEMAPHORES = ["eD", "eA", "eP", "eG", "sent"] + ["d%d" % k for k in range(NDMA)] + ["x%d" % k for k in range(10)]
CY = 0.83e-3 * 1.05
GA_, SC_, PE_ = 1.55, 3.8, OPT["pe"]
BIG = float(2 ** 24)
MAGIC = 1.5 * 2 ** 23


def _shape(name):
    return SCRATCH[name][1]


def _cells(ap):
    name, idx = ap
    if name not in SCRATCH:
        return None
    sh = _shape(name)
    n = int(np.prod(sh[1:]))
    m = np.zeros(n, bool)
    ix = idx if isinstance(idx, tuple) else (idx,)
    m[np.arange(n).reshape(sh[1:])[ix[1:]].ravel()] = True
    return name, m


def _n(ap):
    if ap[0] == "ind":
        return 16 * _n(ap[2])
    return int(_cells(ap)[1].sum())


def _isap(x):
    return isinstance(x, tuple)


def _two(*aps):
    return all(SCRATCH[a[0]][2] in (bf, u16) for a in aps)


def _ps(a):
    return a[0] != "ind" and SCRATCH[a[0]][0] == "psum"


def build():
    ops = []

    def add(var, rd, wr, lat=0.0):
        r, w = [], []
        for a in rd:
            if _isap(a):
                r += [a[1], a[2]] if a[0] == "ind" else [a]
        for a in wr:
            if a[0] == "ind":
                w.append(a[1]); r.append(a[2])
            else:
                w.append(a)
        ops.append(dict(var=var, r=[c for c in map(_cells, r) if c], w=[c for c in map(_cells, w) if c], lat=lat))
        return ops[-1]

    def dcost(out, ins, per):
        if out[0] == "ind":
            return 0.05 + _n(out) * SC_ * CY
        if ins[0][0] == "ind":
            return 0.05 + _n(ins[0]) * GA_ * CY
        return OPT["ov"] + max(64, _n(ins[0]) * per) * CY

    def tt(o, a, b, op):
        add({"D": ([("tensor_tensor", o, a, b, op)], dcost(o, [a], 1 if _ps(a) or _ps(b) else 2))}, [a, b], [o])

    def ts(o, a, s1, op0, s2=None, op1=None):
        c = ("tensor_scalar", o, a, s1, s2, op0) + (() if op1 is None else (op1,))
        add({"D": ([c], dcost(o, [a], 0.5 if a[0] != "ind" and o[0] != "ind" and _two(o, a) else 1))}, [a, s1, s2], [o])

    def cp(o, a):
        add({"D": ([("tensor_copy", o, a)], dcost(o, [a], 0.5 if a[0] != "ind" and o[0] != "ind" and _two(o, a) else 1))}, [a], [o])

    def acost(a):
        return 0.065 + _n(a) * GA_ * CY if a[0] == "ind" else OPT["ova"] + max(64, _n(a)) * CY

    def aff(o, a, sc=1.0, bi=None, eng="AD"):
        if bi is None:
            d = ("tensor_copy", o, a) if sc == 1.0 else ("tensor_scalar", o, a, sc, None, A.mult)
            s = ("act", o, a, F.Copy, None, sc)
        else:
            d = ("tensor_scalar", o, a, bi, None, A.add) if sc == 1.0 else ("tensor_scalar", o, a, sc, bi, A.mult, A.add)
            s = ("act", o, a, F.Identity, bi, sc)
        var = {"D": ([d], dcost(o, [a], 0.5 if a[0] != "ind" and _two(o, a) else 1)), "A": ([s], acost(a))}
        add({e: var[e] for e in eng}, [a, sc, bi], [o])

    def hot(o, a, at, bi):
        add({"D": ([("tensor_scalar", o, a, at - 0.5, None, A.is_ge)], dcost(o, [a], 1)), "A": ([("act", o, a, F.Relu, bi, 1.0)], acost(a))},
            [a, bi], [o])

    def scatter(o, a):
        var = {"D": ([("tensor_copy", o, a)], dcost(o, [a], 1))}
        if OPT["silu"]:
            var["A"] = ([("act", o, a, F.Silu, None, None)], 0.065 + _n(o) * SC_ * CY)
        add(var, [a], [o])

    def red(o, a, op):
        add({"D": ([("reduce", o, a, op)], dcost(o, [a], 1))}, [a], [o])

    def scan(o, a, b, init, op0, op1):
        add({"D": ([("tensor_tensor_scan", o, a, b, init, op0, op1)], dcost(o, [a], 1))}, [a, b], [o])

    def vtr(o, a):
        add({"D": ([("transpose", o, a)], dcost(o, [a], 1))}, [a], [o])

    def ms(o, c, soon=False):
        if not soon and float(c).is_integer() and abs(c) < BIG:
            return iota(o, [[0, _n(o)]], int(c))
        add({"D": ([("memset", o, c)], dcost(o, [o], 0.5 if _two(o) else 1))}, [], [o])

    def mm(lst, group=True):
        calls, c, rd, wr = [], 0.0, [], []
        for k, (o, l, r) in enumerate(lst):
            gs = len(lst) if group is True else max(1, int(group))
            calls.append(("matmul", o, l, r, k % gs == 0, k % gs == gs - 1))
            c += max(min(64, _n(l)), _n(r)) * PE_ * CY * (4 if SCRATCH[r[0]][2] == f32 else 1)
            rd += [l, r]; wr.append(o)
        add({"P": (calls, c)}, rd, wr, lat=0.05)

    def iota(o, pat, base=0, cm=0):
        add({"G": ([("iota", o, pat, base, cm)], 0.14 + 2 * _n(o) * CY)}, [], [o])

    nd = [0, 0.0]

    def dma(q, o, a, nbytes):
        load = a[0] not in SCRATCH
        nd[1] = (nd[1] if load else 0.0) + nbytes / 250e3
        op = add({q: ([("dma", o, a, "d%d" % nd[0])], 0.05)}, [a], [o], lat=2.0 + nd[1])
        op["dma"] = "d%d" % nd[0]
        op["load"] = load
        nd[0] += 1

    nx = [0]

    def xchg(parts, nbytes):
        op = add({"G": ([("remote", parts, "x%d" % nx[0])], 0.3 if nx[0] else 1.8)}, [p[1] for p in parts], [p[2] for p in parts], lat=1.6 + nbytes / 100e3)
        op["x"] = "x%d" % nx[0]
        nx[0] += 1

    def col(k):
        return ("CO", S_[:, k:k + 1])

    def b(name, idx=S_[:]):
        return (name, idx)

    def ind(w, o):
        return ("ind", w, o)

    def pb(bank, c0, c1):
        return ("P%d" % bank, S_[:, c0 // 16:c1 // 16, :])

    p0 = lambda c0, c1: b("P0", S_[:, c0:c1])

    dma("S", b("Lin", S_[:, 0, :]), b("vol"), 32e3)
    dma("A", b("Lin", S_[:, 1, :]), b("dv", S_[:, 0:1024]), 32e3)
    plain = not (OPT["silu"] or max(map(max, OPT["merge"])))
    u0 = lambda c0, c1: b("F0", S_[:, UO_ + c0:UO_ + c1]) if plain else b("UX", S_[:, 8 + c0:8 + c1])
    dma("S", u0(0, 128), b("u", S_[:, 0:128]), 64e3)
    dma("A", u0(896, 1024), b("u", S_[:, 896:1024]), 64e3)
    dma("S", b("NT"), b("nt"), 655e3)
    dma("S", u0(128, 896), b("u", S_[:, 128:896]), 393e3)
    dma("S", b("Lin", S_[:, 2, :]), b("dv", S_[:, 1024:2048]), 32e3)
    dma("S", b("Lin", S_[:, 3, :]), b("dv", S_[:, 2048:3072]), 32e3)
    dma("S", b("WT", S_[:, 8:264]), b("wt"), 131e3)
    xchg([(1, u0(896, 1024), u0(1024, 1152)), (-1, u0(0, 128), u0(1152, 1280))], 131e3)
    iota(b("CI", S_[:, 0:1]), [[0, 1]], 0, 1)
    iota(b("IOT", S_[:, 0:144]), [[1, 144]])
    iota(b("RG"), [[1, 8], [0, 16]])
    iota(b("RI", S_[:, 0:128]), [[0, 8], [1, 16]])
    iota(b("C8", S_[:, 0, :]), [[16, 8]])
    iota(b("C80", S_[:, 0, :]), [[16, 80]])
    iota(b("IOT", S_[:, 144:720]), [[1, 576]], 144)
    iota(b("IOT", S_[:, 720:1296]), [[1, 576]], 720)
    ci = lambda k: b("CI", S_[:, k:k + 1])
    ts(ci(1), ci(0), 4, A.arith_shift_right, 1, A.bitwise_and)
    cp(col(3), ci(1))
    ts(col(4), ci(1), -1.0, A.mult, 1.0, A.add)
    ts(ci(2), ci(0), 15, A.bitwise_and)
    ts(ci(3), ci(0), 4, A.arith_shift_right)
    cp(col(0), ci(0)); cp(col(1), ci(2)); cp(col(2), ci(3))
    for k, v in ((31, -11.0), (30, 1288.0), (25, 9.0), (26, -29.0), (27, MAGIC), (28, -MAGIC)):
        ms(col(k), v)
    ms(b("ZR"), 0.0, True)
    ms(b("RK", S_[:, 64:72]), 0.0)

    def unblock(a0, a1, outs, shift):
        for h in (0, 1):
            ts(b("Ld", S_[:, 4 * a0:4 * a1, h, :]), b("Ls", S_[:, a0:a1, :]), shift, A.add, col(4 - h), A.mult)
        vtr(b("Lt", S_[:, a0:a1]), b("Ld", S_[:, 4 * a0:4 * a1]))
        for a in range(a0, a1):
            for c4 in range(4):
                tt(outs(a, c4), b("Lt", S_[:, a, c4, 0, :]), b("Lt", S_[:, a, c4, 1, :]), A.add)
    tt(b("Ls", S_[:, 0, :]), b("Lin", S_[:, 0, :]), b("Lin", S_[:, 1, :]), A.add)
    unblock(0, 1, lambda a, c4: b("V1", S_[:, 0, c4:64:4]), -9.0)
    xchg([(1, b("V1", S_[:, 0, 56:64]), b("V1", S_[:, 0, 64:72])), (-1, b("V1", S_[:, 0, 0:8]), b("V1", S_[:, 0, 72:80]))], 16e3)
    ts(b("BO"), b("RG"), col(2), A.is_equal)
    ts(b("DM", S_[:, 0:128]), b("RI", S_[:, 0:128]), col(1), A.is_equal)
    ts(b("T1"), b("RI", S_[:, 0:128]), col(1), A.is_lt, -1.0, A.mult)
    tt(b("TB"), b("T1"), b("BO"), A.mult)
    c8 = lambda k: b("C8", S_[:, k, :])
    ts(c8(0), c8(0), col(1), A.add)
    ts(c8(1), c8(0), 0.5, A.add)
    for j in range(4):
        aff(b("DU", S_[:, 8 * j:8 * j + 8]), c8(0), 1.0, col(30))
    cp(b("RC"), b("BO", S_[:, 0::16]))
    cp(b("CG"), b("IOT", S_[:, 0:8]))
    aff(b("EH"), b("IOT", S_[:, 0:8]), -0.5)
    aff(b("DS"), b("DM", S_[:, 0:16]), 0.0625)
    if OPT["rbg"]:
        ms(b("GV", S_[:, 0:512]), 0.0625)
        for q in range(4):
            o, a = b("RB", S_[:, 4 * q:4 * q + 4, :]), b("GV", S_[:, 0:512])
            add({"G": ([("affine_select", o, a, [[-1, 4], [-16, 8], [0, 16]], A.is_equal, 0.0, -4 * q, 1)], 0.17 + 1024 * CY)}, [a], [o])
    else:
        for i in range(16):
            aff(b("RB", S_[:, i, :]), b("BO"), b("DS", S_[:, i:i + 1]))
    ts(col(5), col(0), 15.0, A.add)
    ts(b("AK"), b("IOT", S_[:, 0:144]), col(5), A.is_equal, b("DM", S_[:, 0:1]), A.mult)
    ts(b("IDB"), b("IOT", S_[:, 0:128]), col(0), A.is_equal)
    ts(b("IDF"), b("IOT", S_[:, 0:128]), col(0), A.is_equal)
    aff(b("NEG"), b("IDB"), -BIG)
    if OPT["pe_est"]:
        for j in (2, 3):
            aff(b("IDJ", S_[:, j - 2, :]), b("IDF"), float(j))
    ts(col(7), col(1), -2048.0, A.mult, 31 * 2048.0, A.add)
    ms(b("VR", S_[:, :, 0:8]), -0.5625)
    ms(b("NM", S_[:, 0:8]), 0.0)
    ms(b("AL", S_[:, 0:8]), 0.0)
    ms(b("FI", S_[:, :, 0:8]), 0.0)
    for h in (0, 1):
        c = S_[:, 640 * h:640 * h + 640]
        c8_ = S_[:, 8 + 640 * h:648 + 640 * h]
        ts(b("AI", c), b("NT", c), 4, A.arith_shift_right)
        ts(b("NM", c8_), b("AI", c), 8.0, A.add)
        ts(b("NT", c), b("NT", c), 15, A.bitwise_and)
        ts(b("AL", c8_), b("NT", c), 32768.0, A.mult)
    for c0, c1 in ((128, 512), (512, 896), (0, 128), (896, 1280)):
        ux = b("UX", S_[:, 8 + c0:8 + c1])
        if max(OPT["merge"][0]):
            aff(ux, ux, 2.0 ** 17, col(27))
            aff(ux, ux, 1.0, col(28))
        elif not plain:
            aff(b("F0", S_[:, UO_ + c0:UO_ + c1]), ux, 2.0 ** 17)
    ts(ci(4), ci(0), 112, A.add)
    ts(ci(5), ci(4), 127, A.bitwise_and)
    cp(col(6), ci(5))
    ts(b("SH"), b("IOT", S_[:, 0:128]), col(6), A.is_equal)
    cp(b("Ls", S_[:, 1:3, :]), b("Lin", S_[:, 2:4, :]))
    unblock(1, 3, lambda a, c4: b("D2", S_[:, c4:64:4, a - 1]), 0.0)
    xchg([(1, b("D2", S_[:, 56:64, :]), b("D2", S_[:, 64:72, :])), (-1, b("D2", S_[:, 0:8, :]), b("D2", S_[:, 72:80, :]))], 16e3)
    xchg([(1, b("WT", S_[:, 8:264]), b("WT", S_[:, 272:528])), (-1, b("WT", S_[:, 8:264]), b("WT", S_[:, 536:792]))], 262e3)
    for k in (0, 264, 528):
        ms(b("WT", S_[:, k:k + 8]), 1.0)
    ms(b("T1"), 0.5)
    ms(b("GA"), 0.0)
    scan(b("T2"), b("T1"), b("GA"), float(2 ** 65), A.mult, A.add)
    tt(b("T1"), b("T2"), b("IDF"), A.mult)
    red(b("CB", S_[:, 0:1]), b("T1"), A.max)
    tt(b("T3"), b("T2"), b("DM", S_[:, 0:128]), A.mult)
    red(c8(2), b("T3"), A.max)
    for j in range(3):
        aff(b("TH", S_[:, 8 * j:8 * j + 8]), c8(2), 2.5)
    ts(col(8), col(1), 4.0, A.is_ge)
    ts(col(9), col(1), 11.0, A.is_lt, col(8), A.mult)
    ts(col(10), col(1), 4.0, A.is_lt)
    ts(col(11), col(8), 15.0 * 2.0 ** -65, A.mult, 2.0 ** -65, A.add)
    tt(col(11), col(11), b("C8", S_[:, 2, 0:1]), A.mult)
    aff(col(12), b("DM", S_[:, 11:12]), 5.0)
    aff(col(13), b("DM", S_[:, 11:12]), 7.0)
    ts(b("XH"), b("IOT", S_[:, 0:96]), 0.5, A.add, col(11), A.mult)
    ts(b("TI"), b("XH"), -0.5, A.add)
    tt(b("XH"), b("XH"), b("TI"), A.subtract)
    ts(b("HA"), b("XH"), 0.5, A.is_ge, 0.5, A.subtract)
    ts(b("XH"), b("HA"), 2.0, A.mult, col(9), A.mult)
    ts(b("XL"), b("HA", S_[:, 0:16]), 2.0, A.mult, col(10), A.mult)
    aff(b("XL"), b("XL"), 1.0, b("DM", S_[:, 11:12]))
    for lo in range(16):
        aff(b("XT", S_[:, 8 + lo:1288:16]), b("XH", S_[:, 0:80]), 1.0, b("XL", S_[:, lo:lo + 1]))
    tt(col(14), b("XH", S_[:, 80:81]), b("XL", S_[:, 0:1]), A.add)
    aff(b("XT", S_[:, 0:8]), b("ZR", S_[:, 0:8]), 1.0, col(14))
    PERM = ((0, 56, 8), (8, 72, 8), (16, 64, 8), (24, 0, 56))
    for q0, h0, w in PERM:
        aff(b("HA", S_[:, q0:q0 + w]), b("XH", S_[:, h0:h0 + w]), 1.0, col(12))
    aff(b("HA", S_[:, 80:96]), b("XL"), 1.0, col(13))
    ms(b("HC", S_[:, 640:896]), 0.0)
    for g in range(8):
        gm = b("RC", S_[:, g:g + 1])
        aff(b("HC", S_[:, 80 * g:80 * g + 80]), b("HA", S_[:, 0:80]), gm)
        o = 640 + 32 * g + 16 * (g % 2)
        aff(b("HC", S_[:, o:o + 16]), b("HA", S_[:, 80:96]), gm)
    if not ALLA:
        ms(b("TE"), 256.0)
        ms(b("TE", S_[:, 0::16]), 0.0)
        ms(b("MM"), 0.0)
        ms(b("MM", S_[:, 0::16]), 2.0 ** -56)
        scan(b("US"), b("TE"), b("MM"), 0.0, A.mult, A.add)
        if max(map(max, OPT["merge"])):
            tt(b("DD"), b("US"), b("IDF"), A.mult)
            red(col(29), b("DD"), A.max)
            ts(col(24), col(29), 16.0, A.mult)
        npt = 16 * OPT["cd"]
        ms(b("ON", S_[:, 0:npt]), 1.0)
        ms(b("ON", S_[:, 0:npt:16]), 2.0 ** -8)
        ms(b("ON", S_[:, 0:npt:256]), 0.0)
        ms(b("OX", S_[:, 0:npt]), 0.0)
        ms(b("OX", S_[:, 0:npt:256]), 2.0 ** 56)
        scan(b("PT"), b("ON", S_[:, 0:npt]), b("OX", S_[:, 0:npt]), 0.0, A.mult, A.add)
    for t in range(3):
        for v in range(OPT["L"][t]):
            ms(b("UA", S_[:, t, v::OPT["L"][t]]), 2.0 ** (8 * v))
    ts(b("C80", S_[:, 0, :]), b("C80", S_[:, 0, :]), col(1), A.add)
    for sl, o in ((S_[8:56], 8), (S_[0:8], BS_), (S_[56:80], BS_ - 768)):
        ms(b("C80", (S_[:], 1, sl)), float(UO_ - o))
        ts(b("C80", (S_[:], 0, sl)), b("C80", (S_[:], 0, sl)), float(o), A.add)
    ms(b("C80", S_[:, 2, 0:64]), 7.0)
    ms(b("C80", S_[:, 2, 64:72]), 271.0)
    ms(b("C80", S_[:, 2, 72:80]), 535.0)
    ms(b("CN", S_[:, :, 8:24]), 0.0)
    Fn = lambda t: "F%d" % (t % 2)

    def clear(t):
        for h in range(4):
            iota(b(Fn(t), S_[:, 354 * h:354 * h + 354]), [[0, 354]])
            ops[-1]["drain"] = t == 2
    for t in range(2):
        ms(b(Fn(t), S_[:, UO_ - 8:UO_]), 1.0 if plain else 2.0 ** 17)
        clear(t)
    for Z in ("ZH", "ZL"):
        for z in range(6):
            iota(b(Z, S_[:, z // 3, 24 * (z % 3):24 * (z % 3) + 24, :]), [[0, 384]])

    packed = lambda t: max(OPT["merge"][t]) > 0

    def gather(t, st):
        nA = OPT["nA"][t]
        nD, cd = 128 - nA, OPT["cd"]
        for l0 in range(0, nD, cd):
            n = min(cd, nD - l0)
            o = 16 * (nD * st + l0)
            tt(b("G", S_[:, o:o + 16 * n]), ind(b(Fn(t), S_[:, UO_ - 8:UO_ + 1280]), b("NU", S_[:, t, st, nA + l0:nA + l0 + n])), b("PT", S_[:, 0:16 * n]), A.mult)

    def scans(o, a0, a1, n):
        back = lambda x: S_[:, x + n - 1:x - 1:-1] if x else S_[:, n - 1::-1]
        scan(b("ON", S_[:, o:o + n]), b("G", S_[:, a0:a0 + n]), b("G", S_[:, a1:a1 + n]), 1e29, A.min, A.min)
        scan(b("OX", back(o)), b("G", back(a0)), b("G", back(a1)), 0.0, A.max, A.max)

    def bounds(t, h):
        nA = OPT["nA"][t]
        nD = 128 - nA
        if OPT["pair"][t]:
            nA, nD, L = 0, 128, OPT["L"][t]
            if h == 0:
                copies(t)
            for l0 in range(0, 128, 32):
                for s in (0, 1):
                    o = 2048 * s + 16 * l0
                    aff(b("G", S_[:, o:o + 512]), ind(b(Fn(t), S_[:, UO_ - 8:]), b("NO", S_[:, t, h, 128 * s + l0:128 * s + l0 + 32])))
                for l in range(l0, l0 + 32, L):
                    scans(16 * l, 16 * l, 2048 + 16 * l, 16 * L)
        if not nD:
            return
        for l0 in range(0, 0 if OPT["pair"][t] else nD, 16):
            scans(16 * l0, 16 * (2 * h * nD + l0), 16 * ((2 * h + 1) * nD + l0), 256)
        for O, k, acc, out, op in (("ON", 15, pb(5, 256, 256 + nD), "LO", A.min), ("OX", 0, pb(5, 384, 384 + nD), "HI", A.max)):
            if h == 0:
                aff(acc, b(O, S_[:, k:16 * nD:16]))
            else:
                tt(acc, acc, b(O, S_[:, k:16 * nD:16]), op)
                tt(b(out, S_[:, nA:128]), acc, b("UA", S_[:, t, :]) if OPT["pair"][t] else b("US", S_[:, nA:128]), A.mult)

    def copies(t):
        for c0, c1 in ((136, 904), (0, 136), (904, 1288)):
            for v in range(1, OPT["L"][t]):
                o = CP_ + 1288 * (v - 1)
                aff(b(Fn(t), S_[:, o + c0:o + c1]), b(Fn(t), S_[:, UO_ - 8 + c0:UO_ - 8 + c1]), 2.0 ** (-8 * v))

    def copied(t):
        nA, L_ = OPT["nA"][t], OPT["L"][t]
        if not nA or OPT["pair"][t]:
            return
        g0, o0, n = 64 * (128 - nA), 16 * (128 - nA), 32 * L_
        copies(t)
        for l0 in range(0, nA, 16):
            r = l0 % RG_
            for s in (0, 1):
                o = g0 + 32 * (RG_ * s + r)
                aff(b("G", S_[:, o:o + 512]), ind(b(Fn(t), S_[:, UO_ - 8:]), b("NO", S_[:, t, s, 2 * l0:2 * l0 + 32])))
            for l in range(0, 16, L_):
                scans(o0 + 32 * (l0 % RO_ + l), g0 + 32 * (r + l), g0 + 32 * (RG_ + r + l), n)
            if (l0 + 16) % RO_ == 0 or l0 + 16 == nA:
                c, ua = S_[:, l0 - l0 % RO_:l0 + 16], b("UA", S_[:, t, l0 - l0 % RO_:l0 + 16])
                e = o0 + 32 * (l0 % RO_ + 16)
                tt(b("LO", c), b("ON", S_[:, o0 + 31:e:32]), ua, A.mult)
                tt(b("HI", c), b("OX", S_[:, o0:e:32]), ua, A.mult)

    def names(t, st):
        cp(b("NU", S_[:, t, st, :]), ind(b("NM"), b("UF", S_[:, t, 8 * st:8 * st + 8])))
        nA, L_ = OPT["nA"][t], OPT["L"][t]
        for v in range(L_ if nA else 0):
            sl = S_[128 * (st % 2) + v:128 * (st % 2) + 128:L_] if OPT["pair"][t] else S_[2 * v + st % 2:2 * nA:2 * L_]
            ts(b("NO", (S_[:], t, st // 2, sl)), b("NU", S_[:, t, st, v:nA:L_]), float(CP_ - UO_ + 8 + 1288 * (v - 1) if v else 0), A.add)

    def rows(t, c0, c1, bank, o):
        mm([(b("P%d" % bank, S_[:, o:o + c1 - c0, i]), b("RB", S_[:, i, :]), b("VW", S_[:, t, c0:c1])) for i in range(16)], False)

    def lanes(t):
        w = lambda k: b("W", S_[:, t, k, :])
        iw = lambda k: b("I", S_[:, t, k, :])
        uw = lambda k: b("U", S_[:, t, k, :])
        par = t
        s16 = (832 * t) % 1024 // 16
        v1 = lambda sl: b("V1", (S_[:], t, sl))
        for o, c0, n in ((0, s16, 64 - s16), (64 - s16, 0, s16)):
            if n and t:
                tt(b("SM", S_[:, o:o + n]), p0(256 + c0, 256 + c0 + n), b("VE", S_[:, c0:c0 + n]), A.is_gt)
            elif n:
                ts(b("SM", S_[:, o:o + n]), v1(S_[c0:c0 + n]), -1.0, A.is_lt)
        ts(b("VW", S_[:, t, :]), v1(S_[:]), -8.0, A.max, 7.0, A.min)
        scan(b("SP"), b("SM"), b("ZR"), 0.0, A.add, A.add)
        mm([(p0(0, 64), b("BO"), b("SP"))])
        mm([(pb(1, 448, 512), b("BO"), b("SP")), (pb(1, 448, 512), b("TB"), b("SM"))])
        if not OPT["merge"][t][0]:
            for c0, c1, bank in ((0, 32, 2), (32, 64, 3), (64, 80, 2)):
                rows(t, c0, c1, bank, 0)
                aff(b("VR", S_[:, par, 8 + 16 * c0:8 + 16 * c1]), pb(bank, 0, 16 * (c1 - c0)))
        rk = b("RK", S_[:, 0:64])
        for c in range(8):
            o, a, bi, ac = b("LC", S_[:, c, :]), p0(0, 64), b("C8", S_[:, 1, c:c + 1]), b("W", S_[:, t, 0, c:c + 1])
            add({"A": ([("sign", o, a, bi, ac)], 0.075 + OPT["ova"])}, [a, bi], [o, ac])
        cp(rk, pb(1, 448, 512))
        ts(uw(0), w(0), 0.5, A.mult, 32.0, A.add)
        tt(b("CM"), ind(b("RK"), uw(0)), b("IOT", S_[:, 0:128]), A.is_le)
        ts(b("IM", S_[:, :, 16]), w(0), 8.0, A.mult, float(520 + 16 * s16), A.add)
        ts(b("IM", S_[:, :, 17]), w(0), 64.0, A.is_ge, -4096.0, A.mult)
        if s16:
            ts(b("IM", S_[:, :, 18]), w(0), 64.0 - 2 * s16, A.is_ge, -1024.0, A.mult)
        ts(b("FL", S_[:, 0:8]), w(0), 64.0, A.is_lt)
        mm([(p0(128, 256), b("BO"), b("CM"))])
        tt(b("IM", S_[:, :, 0:16]), p0(128, 256), b("DM", S_[:, 0:128]), A.mult)
        red(w(3), b("IM", S_[:, :, 0:19 if s16 else 18]), A.add)
        cp(b("UF", S_[:, t, 0:8]), w(3))
        ts(b("NG", S_[:, t, 0:8]), w(3), 0.0, A.max)
        ts(rk, rk, 128.0, A.is_le)
        for h0, h1, q0 in ((0, 56, 24), (56, 64, 0)):
            for a0, a1 in ((h0, min(h1, max(s16, h0))), (max(h0, min(s16, h1)), h1)):
                if a1 > a0:
                    r0 = (a0 - s16) % 64
                    tt(b("CN", S_[:, t, q0 + a0 - h0:q0 + a1 - h0]), b("RK", S_[:, r0:r0 + a1 - a0]), b("SM", S_[:, r0:r0 + a1 - a0]), A.mult)
        if t < 2:
            tt(b("VD"), b("VW", S_[:, t, :]), b("D2", S_[:, :, t]), A.add)
            ts(b("VE"), b("VD", S_[:, 0:64]), 2.0, A.is_ge, 1000.0, A.mult)
            tt(b("VE"), b("VE"), b("VD", S_[:, 0:64]), A.add)
            ts(b("VE"), b("VE"), 1.0, A.add)

    def pack(t):
        for c0, c1, bank, o in ((8, 32, 5, 0), (32, 56, 7, 0), (0, 8, 4, 0), (56, 80, 4, 8)):
            rows(t, c0, c1, bank, o)
            src = b("FI", S_[:, t - 1, 8 + 16 * c0:8 + 16 * c1]) if t else b("UX", S_[:, 8 + 16 * c0:8 + 16 * c1])
            v = pb(bank, 16 * o, 16 * (o + c1 - c0))
            tt(b(Fn(t), S_[:, UO_ + 16 * c0:UO_ + 16 * c1]), src, v, A.add)
            if OPT["merge"][t][0]:
                aff(b("VR", S_[:, t, 8 + 16 * c0:8 + 16 * c1]), v)

    def step(t, j):
        w = lambda k: b("W", S_[:, t, k, :])
        iw = lambda k: b("I", S_[:, t, k, :])
        par = t
        vr = b("VR", S_[:, par, :])
        merged = OPT["merge"][t][j - 1]
        um = lambda j0, j1: b("UM", S_[:, t, 8 * j0:8 * j1])
        uf = lambda j0, j1: b("UF", S_[:, t, 8 * j0:8 * j1])
        ng = lambda j: b("NG", S_[:, t, 8 * j:8 * j + 8])
        vm = lambda j0, j1: b("VM", S_[:, par, 128 * j0:128 * j1])
        last = uf(j - 1, j)
        names(t, j - 1)
        vt, at, rest = pb(1, 0, 128), pb(6, 128, 256), pb(6, 256, 384)
        if merged:
            gather(t, j - 1)
        else:
            for q in range(4):
                aff(b("GV", S_[:, 512 * q:512 * q + 512]), ind(vr, b("NU", S_[:, t, j - 1, 32 * q:32 * q + 32])), 16.0, col(25))
        aff(b("MR", S_[:, j - 1, :]), ind(b("IOT"), last))
        aff(b("NC"), ind(b("NM"), last), 1.0, col(7))
        aff(b("AG"), ind(b("AL"), last))
        for k in range(j):
            tt(b("EQ", S_[:, k, :]), ind(b("NM"), last), b("MR", S_[:, k, :]), A.is_equal)
        if j == 1:
            aff(vm(0, 1), ind(vr, uf(0, 1)), 16.0, col(25))
            prev = b("P6", S_[:, 24, 0:8])
            mm([(prev, b("MR", S_[:, 0, :]), b("IDF", S_[:, 0::16]))])
        else:
            prev = iw(2 + j)
        if j == 3:
            aff(vm(1, 2), ind(vr, um(1, 2)), 16.0, col(25))
            aff(b("VF"), ind(vr, last), 16.0, col(25))
            mm([(p0(128, 256), b("IDB"), x) for x in (vm(0, 1), vm(1, 2), b("VF"))])
            hot(b("EQ", S_[:, 3, :]), p0(128, 256), 30.0, col(26))
        keys = [(rest, b("EQ", S_[:, k, :]), b("NEG")) for k in range(j + j // 3)] + [(rest, b("AG"), b("IDB"))] * merged + [(rest, b("NC"), b("IDF"))]
        if OPT["sel"] and not merged:
            for h in (0, 1):
                mm([(pb(1, 64 * h, 64 * h + 64), b("AK", S_[:, 15 - k:143 - k]), b("GV", S_[:, 1024 * h + k:1024 * h + 1024:16])) for k in range(16)])
            tt(b("PB"), vt, b("AG"), A.mult)
            mm(keys + [(rest, b("PB"), b("IDB"))])
            red(w(5), rest, A.max)
        else:
            mm([(at, b("AG"), b("IDB"))])
            mm(keys)
            if merged:
                mm([(b("P1", S_[:, 0:8, k]), b("G", S_[:, 2048 * (j - 1) + k:2048 * j:16]), b("IDF", S_[:, 0::16])) for k in range(16)], False)
                ts(b("VI"), vt, col(24), A.mult, 8.0, A.add)
                ts(b("VI"), b("VI"), 15, A.bitwise_and)
                tt(b("PR"), b("VI"), at, A.mult)
            else:
                aff(b("AT"), at)
                mm([(b("P1", S_[:, 0:8, k]), b("GV", S_[:, k::16]), b("IDB", S_[:, 0::16])) for k in range(16)], False)
                tt(b("PR"), vt, b("AT"), A.mult)
            tt(b("KY"), b("PR"), rest, A.add)
            red(w(5), b("KY"), A.max)
        tt(iw(2), w(5), prev, A.max)
        ts(iw(3 + j), iw(2), 2047, A.bitwise_and)
        tt(b("LH"), ind(iw(3 + j), b("CG")), b("DM", S_[:, 0:128]), A.mult)
        nw = b("P1", S_[:, 25, 0:8])
        mm([(nw, b("LH"), b("RC"))])
        cp(uf(j, j + 1), nw)
        go = b("GO", S_[:, t, :, j])
        tt(go, nw, ng(0) if j == 1 else b("LW", S_[:, t, 8 * j - 8:8 * j]), A.not_equal)
        tt(ng(j), nw, go, A.mult)
        if j < 3:
            aff(b("LW", S_[:, t, 8 * j:8 * j + 8]), nw)
        cp(um(j, j + 1), ng(j))
        aff(b("XR"), ind(b("XT"), um(j, j + 1)))
        mm([(b("P2"), b("XR"), b("HC", S_[:, 0:512])), (pb(3, 0, 384), b("XR"), b("HC", S_[:, 512:896]))], False)
        hot(b("HB", S_[:, 512:896]), pb(3, 0, 384), 12.0, col(31))
        hot(b("HB", S_[:, 0:512]), b("P2"), 12.0, col(31))
        mm([(b("P0", S_[32 * (g // 2):32 * (g // 2) + 32, 0:80]), b("HB", S_[:, 640 + 32 * g:672 + 32 * g]), b("HB", S_[:, 80 * g:80 * g + 80]))
            for g in range(8)], 2)
        ops[-1]["tile"] = 9
        cn = b("CN", S_[:, t, :])
        tt(cn, p0(0, 80), cn, A.add)
        if j == 3:
            xchg([(1, b("CN", S_[:, t, 0:16]), b("LN", S_[:, t, 16:32])), (-1, b("CN", S_[:, t, 16:32]), b("LN", S_[:, t, 0:16]))], 30e3)
        aff(b("XB"), b("XR"), col(3))
        e = 3 * par + j - 1
        for x in (0, 1):
            for y in (0, 1):
                r0 = 64 * x + 32 * y
                mm([(b("P%d" % (2 + y), S_[:, 2 * x + z::4, :]), b("XR", S_[r0:r0 + 16 + 16 * z, :]), b("XB" if z else "XR", S_[r0:r0 + 16 + 16 * z, :])) for z in (0, 1)], False)
                ops[-1]["tile"] = 1 + 2 * x + y
        for y in (0, 1):
            hot(b("EB", S_[:, e, :, :, y, :, :]), b("P%d" % (2 + y)), 12.0, col(31))
        mm([(p0(328 + 8 * j + c, 329 + 8 * j + c), b("EB", S_[:, e, c]), b("CB", S_[:, 0:1])) for c in range(8)], False)

    def counts(t):
        w = lambda k: b("W", S_[:, t, k, :])
        uw = lambda k: b("U", S_[:, t, k, :])
        par = t
        names(t, 3)
        tt(b("FL", S_[:, 8:32]), p0(336, 360), b("TH"), A.is_lt)
        tt(b("TG"), b("NG", S_[:, t, :]), b("DU"), A.subtract)
        tt(b("TG"), b("TG"), b("FL"), A.mult)
        tt(b("TG"), b("TG"), b("DU"), A.add)
        cp(b("UT", S_[:, t, :]), b("TG"))
        vm = lambda j0, j1: b("VM", S_[:, par, 128 * j0:128 * j1])
        aff(vm(2, 4), ind(b("VR", S_[:, par, :]), b("UM", S_[:, t, 16:32])), 16.0, col(25))
        mm([(p0(128, 256), b("IDB"), vm(k, k + 1)) for k in range(4)])
        aff(b("ZS"), p0(128, 256))
        mm([(p0(360, 368), b("AK", S_[:, 15 - k:143 - k]), b("ZS", S_[:, k::16])) for k in range(16)])
        ts(uw(2), p0(360, 368), 7.0, A.add)
        red(w(7), b("GO", S_[:, t, :, 1:4]), A.add)
        cp(uw(3), w(7))
        def whole(o, M):
            mm([(p0(o + 8, o + 56), b(M), b("CN", S_[:, t, 32:80]))])
            mm([(p0(o + h0, o + h0 + 8), b(M), b(X, S_[:, t, q0:q0 + 8])) for q0, h0, n in PERM for X in ("CN", "LN")], 2)
        if t < 2:
            whole(256, "SH")
            ts(b("HM"), p0(256, 336), 3.0, A.min)
            tt(b("V1", S_[:, t + 1, :]), b("VD"), b("HM"), A.subtract)
        whole(368, "IDB")
        n1 = lambda k: b("N1", S_[:, k, :])
        tt(n1(0), p0(368, 448), b("C80", S_[:, 2, :]), A.add)
        ts(n1(1), p0(368, 448), 0.0, A.is_equal)
        cp(b("UW", S_[:, par, :]), n1(0))
        tt(n1(1), n1(1), b("C80", S_[:, 1, :]), A.mult)
        tt(n1(1), n1(1), b("C80", S_[:, 0, :]), A.add)
        cp(b("UO", S_[:, par, :]), n1(1))

    def floats(t):
        par = t
        Ft = Fn(t)
        uw = lambda k: b("U", S_[:, t, k, :])
        pk = b(Ft, S_[:, UO_ - 8:UO_ + 1280])
        ut = lambda j: b("UT", S_[:, t, 8 * j:8 * j + 8])
        S = b(Ft, S_[:, 0:UO_ - 8])
        gather(t, 3)
        bounds(t, 1)
        copied(t)
        for c0, c1 in ((8, 32), (32, 56), (0, 8), (56, 80 if t < 2 else 64)):
            aff(b("WN", S_[:, 16 * c0:16 * c1]), ind(b("WT"), b("UW", S_[:, par, c0:c1])), 1.0 if plain else (1.0, 0.5, 2.0 ** -16)[t])
        tt(b("UV"), ind(b("FI", S_[:, t - 1, :]) if t and packed(t) else pk, b("UF", S_[:, t, :])), b("VM", S_[:, t, :]), A.mult)
        aff(b("U0"), ind(pk, b("UF", S_[:, t, 0:8])))
        tt(b("DD"), ind(pk, b("UF", S_[:, t, 24:32])), b("U0"), A.subtract)
        mm([(pb(7, 256, 384), b("IDF"), b("UV", S_[:, 128 * j:128 * j + 128])) for j in range(4)])
        aff(b("S1"), pb(7, 256, 384))
        tt(b("MM"), ind(b("WT", S_[:, 0:264]), uw(2)), b("S1"), A.mult)
        aff(b("D8"), b("DD"), 0.125)
        tt(b("TE"), ind(b("EH"), uw(3)), b("D8"), A.mult)
        EP = 4
        p6 = lambda j: pb(EP, 128 * j, 128 * j + 128)
        if OPT["pe_est"]:
            for j in (1, 2, 3, 0):
                mm([(p6(j), b("IDF"), b("MM")), (p6(j), b("IDF"), b("TE"))] + [(p6(j), b("IDF") if j == 1 else b("IDJ", S_[:, j - 2, :]), b("D8"))] * min(j, 1))
        else:
            tt(p6(0), b("MM"), b("TE"), A.add)
            for j in (1, 2, 3):
                tt(p6(j), p6(j - 1), b("D8"), A.add)
        for j in (1, 2, 3, 0):
            tt(p6(j), p6(j), b("LO"), A.max)
            tt(b("ES", S_[:, 128 * j:128 * j + 128]), p6(j), b("HI"), A.min)
        scatter(ind(S, ut(0)), b("ES", S_[:, 0:128]))
        for j in (1, 2, 3):
            bk = 7 if j % 2 else 5
            z = j % 2
            add({"P": ([("ptr", pb(bk, 0, 128), b("ES", S_[:, 128 * j:128 * j + 128]), b("IDF"))], 512 * PE_ * CY)},
                [b("ES", S_[:, 128 * j:128 * j + 128]), b("IDF")], [pb(bk, 0, 128)], lat=0.05)
            aff(b("ZH", S_[:, z, 0::9, :]), pb(bk, 0, 128))
            tt(b("ZL", S_[:, z, 0::9, :]), pb(bk, 0, 128), b("ZH", S_[:, z, 0::9, :]), A.subtract)
            e = 3 * par + j - 1
            mm([(pb(bk, 128, 256), b(Z, S_[:, z, 8 * g:8 * g + 8, :]), b("EB", S_[:, e, :, g // 4, g // 2 % 2, g % 2, :])) for Z in ("ZH", "ZL") for g in range(8)])
            aff(b("CC", S_[:, j - 1, :]), pb(bk, 128, 256))
            tt(b("GA"), ind(S, b("UM", S_[:, t, 8 * j:8 * j + 8])), b("CC", S_[:, j - 1, :]), A.add)
            scatter(ind(S, ut(j)), b("GA"))
        lf = lambda k: b("LF", S_[:, t, 128 * k:128 * k + 128])
        parts = [(1, b(Ft, S_[:, 1160:1288]), lf(0)), (-1, b(Ft, S_[:, 1032:1160]), lf(1))]
        if t < 2:
            parts += [(1, b(Ft, S_[:, 904:1032]), lf(2)), (-1, b(Ft, S_[:, 8:136]), lf(3))]
        xchg(parts, 131e3 * (2 if t < 2 else 1))
        top = 80 if t < 2 else 64

        def new(c0, c1, end):
            if t == 2:
                o = b("UX", S_[:, 16 * c0:16 * c1])
            elif packed(t + 1):
                o = b("FI", S_[:, t, 8 + 16 * c0:8 + 16 * c1])
            else:
                o = b(Fn(t + 1), S_[:, UO_ + 16 * c0:UO_ + 16 * c1])
            tt(o, ind(b(Ft, S_[:, 0:end]), b("UO", S_[:, par, c0:c1])), b("WN", S_[:, 16 * c0:16 * c1]), A.mult)
            if t == 2:
                dma("S" if c0 else "A", b("y", S_[:, 16 * c0:16 * c1]), o, 8192 * (c1 - c0))
        new(8, 32, BS_)
        new(32, 56, BS_)
        tt(b(Ft, S_[:, BS_:BS_ + 128]), b(Ft, S_[:, 8:136]), lf(0), A.add)
        tt(b(Ft, S_[:, BS_ + 128:BS_ + 16 * top - 768]), b(Ft, S_[:, 904:8 + 16 * top]), b("LF", S_[:, t, 128:16 * top - 768]), A.add)
        new(56, top, BS_ + 16 * top - 768)
        new(0, 8, BS_ + 128)
        if t == 0:
            clear(2)

    def early(t):
        for j in (1, 2, 3):
            if not OPT["merge"][t][j - 1]:
                gather(t, j - 1)
            if j == 2:
                bounds(t, 0)
    todo = []
    for t in range(3):
        lanes(t)
        if packed(t):
            while todo:
                u = todo.pop(0)
                early(u); floats(u)
            pack(t)
        for j in (1, 2, 3):
            step(t, j)
        counts(t)
        todo.append(t)
    for u in todo:
        early(u); floats(u)
    return ops


def schedule(ops):
    n = len(ops)
    hist = {}
    for k, o in enumerate(ops if "dep" not in ops[0] else []):
        dep = set()
        for name, m in o["r"]:
            for j, wm, wr in hist.get(name, []):
                if wr and (wm & m).any():
                    dep.add(j)
        for name, m in o["w"]:
            for j, wm, wr in hist.get(name, []):
                if (wm & m).any():
                    dep.add(j)
        o["dep"] = dep
        for name, m in o["w"]:
            hist[name] = [h for h in hist.get(name, []) if (h[1] & ~m).any()]
        for name, m in o["r"]:
            hist.setdefault(name, []).append((k, m, False))
        for name, m in o["w"]:
            hist.setdefault(name, []).append((k, m, True))
        o["banks"] = {name for name, m in o["r"] + o["w"] if SCRATCH[name][0] == "psum"}
    succ = [[] for _ in ops]
    for k, o in enumerate(ops):
        for j in o["dep"]:
            succ[j].append(k)
    SY = PAR["sy"]
    pred = [sorted(o["dep"]) for o in ops]

    def rank(xs, t):
        lo, hi = 0, len(xs)
        while lo < hi:
            mid = (lo + hi) // 2
            if xs[mid] <= t:
                lo = mid + 1
            else:
                hi = mid
        return lo

    def gap(lists, t, c, me):
        moved = True
        while moved:
            moved = False
            for st, en, who in lists:
                i = rank(en, t - SY + 1e-9)
                while i < len(st) and st[i] < t + c + SY:
                    pad = 0.0 if who is None or who[i] == me else SY
                    if st[i] < t + c + pad and en[i] + pad > t + 1e-9:
                        t = en[i] + pad
                        moved = True
                    i += 1
        return t

    def place(key, before, after, back, fixed):
        busy = {x: ([], [], []) for x in list("DAPGS") + ["P%d" % k for k in range(8)]}
        left = [len(x) for x in before]
        rt = [0.0] * n
        start, queue = [0.0] * n, [None] * n
        ready = sorted((key[k], k) for k in range(n) if left[k] == 0)
        while ready:
            k = min(ready)[1]
            ready.remove((key[k], k))
            o = ops[k]
            best = None
            for q, (calls, c) in o["var"].items():
                if fixed and q != fixed[k]:
                    continue
                me = (q, o.get("tile"))
                t = gap([busy[q][:2] + (None,)] + [busy[x] for x in o["banks"]], rt[k] + (o["lat"] if back else 0.0), c, me)
                v = t + c + (PAR["m0"] + PAR["m1"] * c if q == "D" else 0.0)
                if q == "A" and t + c < due[k]:
                    v = -1.0
                if best is None or v < best[0]:
                    best = (v, t, q, c)
            v, t, q, c = best
            start[k], queue[k] = t, q
            for x in [q] + list(o["banks"]):
                i = rank(busy[x][0], t)
                busy[x][0].insert(i, t); busy[x][1].insert(i, t + c); busy[x][2].insert(i, (q, o.get("tile")))
            for s in after[k]:
                left[s] -= 1
                rt[s] = max(rt[s], t + c + SY + (0.0 if back else o["lat"]))
                if left[s] == 0:
                    ready.append((key[s], s))
        end = [start[k] + ops[k]["var"][queue[k]][1] + (0.0 if back else ops[k]["lat"]) for k in range(n)]
        return start, queue, end

    key, due = [0.0] * n, [0.0] * n
    rng = np.random.default_rng(1)
    for k in range(n - 1, -1, -1):
        key[k] = min([key[s] - SY for s in succ[k]], default=0.0) - min(v[1] for v in ops[k]["var"].values()) - ops[k]["lat"]
    best = None
    for it in range(PAR["passes"]):
        key = [k - 1e4 if ops[k].get("load") else key[k] for k in range(n)]
        start, queue, end = place(key, pred, succ, False, None)
        if best is None or max(end) < best[0]:
            best = (max(end), start, queue, end)
        elif max(end) > best[0] + PAR["back"]:
            start, queue, end = best[1:]
        s2, q2, e2 = place([-e for e in end], succ, pred, True, queue)
        key = [-e + PAR["jit"] * x for e, x in zip(e2, rng.standard_normal(n).tolist())]
        for k in range(n):
            due[k] = max(e2) - s2[k] - PAR["due"]
    both = [k for k in range(n) if len(ops[k]["var"]) == 2]
    cur = best
    for it in range(PAR["polish"]):
        t0 = rng.random() * cur[0]
        w = PAR["win"] * (0.3 + rng.random())
        x = rng.standard_normal(n).tolist()
        back = it % 2
        base = [-e for e in cur[3]] if back else cur[1]
        key = [base[k] + (PAR["jit2"] * x[k] if t0 <= cur[1][k] < t0 + w else 0.0) for k in range(n)]
        fixed = list(cur[2])
        for k in both:
            if t0 <= cur[1][k] < t0 + w and rng.random() < PAR["flip"] * (PAR["toA"] if fixed[k] == "D" else 1.0):
                fixed[k] = "A" if fixed[k] == "D" else "D"
        if back:
            s2, q2, e2 = place(key, succ, pred, True, fixed)
            key = [-e for e in e2]
        key = [k - 1e4 if ops[k].get("load") else key[k] for k in range(n)]
        start, queue, end = place(key, pred, succ, False, fixed)
        if max(end) <= cur[0] + PAR["tol"]:
            cur = (max(end), start, queue, end)
            if cur[0] < best[0]:
                best = cur
    done, start, queue, end = best
    seq = sorted(range(n), key=lambda k: (start[k], k))
    bank = {}
    for k in seq:
        o = ops[k]
        o["q"], o["st"] = queue[k], start[k]
        prev = set()
        for x in o["banks"]:
            if x in bank and (ops[bank[x]]["q"] != o["q"] or ops[bank[x]].get("tile") != o.get("tile")):
                prev.add(bank[x])
            bank[x] = k
        o["dep2"] = o["dep"] | prev
    cnt = {q: 0 for q in "DAPG"}
    know = {q: {} for q in "DAPGS"}
    for k in seq:
        o = ops[k]
        q = o["q"]
        waits = {}
        for j in sorted(o["dep2"], key=lambda j: -ops[j]["st"]):
            sem, val = ops[j]["sig"]
            if know[q].get(sem, 0) < val:
                waits[sem] = max(waits.get(sem, 0), val)
                for s2, v2 in ops[j]["know"].items():
                    know[q][s2] = max(know[q].get(s2, 0), v2)
                know[q][sem] = val
        o["waits"] = waits
        o["know"] = {} if "x" in o else dict(know[q])
        if "dma" in o:
            o["sig"] = (o["dma"], 16)
        elif "x" in o:
            o["sig"] = (o["x"], 8)
        else:
            cnt[q] += 1
            o["sig"] = ("e" + q, cnt[q])
    return seq, cnt, done


PLAN = {}
PAR = dict(m0=0.4, m1=0.5, sy=0.21, passes=30, jit=0.25, due=0.0, back=1.5, polish=1100, win=5.0, jit2=1.0, flip=0.1, toA=4.0, tol=0.05)


def plan():
    if not PLAN:
        ops = build()
        seq, cnt, end = schedule(ops)
        PLAN.update(ops=ops, seq=seq, cnt=cnt, end=end)
    return PLAN


def rank_program(g, core, T, topo):
    rank = T.rank_of(core)
    if rank is None:
        return
    P = plan()
    n = len(T.cores)
    Q = {"D": g.vector, "A": g.scalar, "P": g.tensor, "G": g, "S": g.sync}

    def ap(a):
        if not _isap(a):
            return a
        if a[0] == "ind":
            return ap(a[1]).indirect(ap(a[2]))
        return T[a[0]][a[1]]

    sent = drained = 0
    for k in P["seq"]:
        o = P["ops"][k]
        q = Q[o["q"]]
        for sem, val in o["waits"].items():
            q.wait_ge(T.sem[sem], val)
        if o.get("drain") and sent > drained:
            g.wait_ge(T.sem.sent, sent)
            drained = sent
        last = None
        for c in o["var"][o["q"]][0]:
            kind, a = c[0], [ap(x) for x in c[1:]]
            if kind == "tensor_tensor":
                last = q.tensor_tensor(*a)
            elif kind == "tensor_scalar":
                last = q.tensor_scalar(*a)
            elif kind == "tensor_copy":
                last = q.tensor_copy(*a)
            elif kind == "tensor_tensor_scan":
                last = q.tensor_tensor_scan(*a)
            elif kind == "transpose" or kind == "ptr":
                last = q.transpose(*a)
            elif kind == "memset":
                last = q.memset(*a)
            elif kind == "reduce":
                last = q.tensor_reduce(a[0], a[1], AX.X, a[2])
            elif kind == "matmul":
                last = q.matmul(*a)
            elif kind == "act":
                if a[4] is None:
                    last = q.activation(a[0], a[1], a[2])
                elif a[3] is None:
                    last = q.activation(a[0], a[1], a[2], scale=a[4])
                else:
                    last = q.activation(a[0], a[1], a[2], bias=a[3], scale=a[4])
            elif kind == "sign":
                last = q.activation(a[0], a[1], F.Sign, bias=a[2], scale=-1.0, accum_out=a[3])
            elif kind == "iota":
                if SCRATCH[c[1][0]][2] == i32:
                    last = q.iota(*a)
                else:
                    last = q.iota(*a, allow_small_or_imprecise_dtypes=True)
            elif kind == "affine_select":
                last = q.affine_select(*a)
            elif kind == "dma":
                q.dma_start(a[0], a[1]).then_inc(T.sem[c[3]], 16)
            elif kind == "remote":
                parts = c[1]
                eng = [e for e in topo.engines(core, T.cores[(rank + 1) % n]) if e in topo.engines(core, T.cores[(rank - 1) % n])]
                per = len(eng) // len(parts)
                tr = []
                for m, (side, src, dst) in enumerate(parts):
                    rid, pid = topo.addr(T.cores[(rank + side) % n], core)
                    tr.append(RemoteDMATransfer(dst_ids=[DstId(rid=rid, pnc=pid)], dma_engine_mask=sum(1 << e for e in eng[per * m:per * m + per]),
                                                remote_sem=T.sem[c[2]], src=ap(src), dst=ap(dst)))
                g.remote_dma_fused(tr, local_sem=T.sem.sent)
                sent += per * len(parts)
        if last is not None:
            last.then_inc(T.sem[o["sig"][0]], 1)
    for e, v in P["cnt"].items():
        g.wait_ge(T.sem["e" + e], v)
    for o in P["ops"]:
        if "dma" in o or "x" in o:
            g.wait_ge(T.sem[o["sig"][0]], o["sig"][1])
    g.wait_ge(T.sem.sent, sent)
